import numpy as np
import ml_dtypes


def mxq(x, axis, fmt="e4m3"):
    dtype, down = {"e4m3": (ml_dtypes.float8_e4m3fn, 7), "e5m2": (ml_dtypes.float8_e5m2, 14)}[fmt]
    v = np.moveaxis(np.asarray(x, np.float32).astype(ml_dtypes.bfloat16).astype(np.float64), axis, -1)
    blocks = v.reshape(v.shape[:-1] + (-1, 32))
    amax = np.abs(blocks).max(-1, keepdims=True)
    byte = np.maximum(np.where(amax > 0, np.frexp(amax)[1] - 1 + 127, 0) - down, 1)
    scale = np.exp2(byte - 127.0)
    codes = (blocks / scale).astype(np.float32).astype(dtype).astype(np.float64)
    return np.moveaxis((codes * scale).reshape(v.shape), -1, axis)


WIDE = False


def mx_kscale(k):
    if not WIDE:
        return np.ones(k)
    levels = np.array([10, -10, 5, -5, 0])
    if k % 512:
        return np.exp2(np.random.permutation(np.resize(levels, k // 32))).repeat(32)
    a = np.empty((k // 512, 16))
    for p in range(k // 512):
        a[p, :8] = np.random.permutation(np.resize(levels, 8))
        for g in range(8):
            far = levels[np.abs(levels - a[p, g]) >= 10]
            a[p, g + 8] = far[np.random.randint(len(far))]
    return np.exp2(a.ravel()).repeat(32)


def f64(x):
    return np.asarray(x).astype(np.float64)


def striped(idx):
    return np.tile(idx.reshape(-1, 16).T, (8, 1)).astype(np.uint16)


def unstriped(offs):
    return offs[:16].T.reshape(-1).astype(np.int64)


def relu(v):
    return np.maximum(v, 0.0)


K, T, S, D, V, H, N, U = 512, 2048, 512, 4, 512, 512, 256, 1024
P = 2 ** 7


def setup_inputs():
    n = np.random.standard_normal
    s = mx_kscale(K)[:, None]
    u = mx_kscale(H)
    return {
        "xT": (n((K, T)) * s).astype(np.float32),
        "w1": (n((K, H)) / np.sqrt(K) / s * u).astype(np.float32),
        "w2": (n((H, N)) / np.sqrt(H) / u[:, None]).astype(np.float32),
        "gate": np.tile(np.random.uniform(0.2, 0.6, (D, 1, V)), (1, P, 1)).astype(np.float32),
        "emb": (0.5 * n((H, U)) * u[:, None]).astype(np.float32),
        "offs": striped(np.random.permutation(T)[:S]),
        "cell": striped(np.random.permutation(U)[:S]),
        "pos1": striped(np.random.permutation(U)[:V]),
        "pos2": striped(np.random.permutation(U)[:V]),
        "pos3": striped(np.random.permutation(U)[:V]),
        "pos4": striped(np.random.permutation(U)[:V]),
    }


def reference(xT, w1, w2, gate, emb, offs, cell, pos1, pos2, pos3, pos4):
    xq = mxq(f64(xT)[:, unstriped(offs)], 0, "e4m3")
    up = np.zeros((H, U))
    up[:, unstriped(cell)] = relu(mxq(f64(w1), 0, "e4m3").T @ xq)
    z = up + f64(emb)
    y = mxq(f64(w2), 0, "e4m3").T @ mxq(z, 0, "e4m3")
    return y[:, unstriped(pos1)] * f64(gate)[0, :1] + y[:, unstriped(pos2)] * f64(gate)[1, :1] + y[:, unstriped(pos3)] * f64(gate)[2, :1] + y[:, unstriped(pos4)] * f64(gate)[3, :1]

@@ -1,0 +1,249 @@
+from contextlib import ExitStack
+
+import concourse.mybir as mybir
+from concourse.masks import make_identity
+
+K, T, S, D, V, H, N, U = 512, 2048, 512, 4, 512, 512, 256, 1024
+P = 128
+FLOPS = 2 * K * H * S + 2 * H * N * U
+
+F32 = mybir.dt.float32
+BF16 = mybir.dt.bfloat16
+U32 = mybir.dt.uint32
+U16 = mybir.dt.uint16
+U8 = mybir.dt.uint8
+FP8X4 = mybir.dt.float8_e4m3fn_x4
+COPY = mybir.ActivationFunctionType.Copy
+RELU = mybir.ActivationFunctionType.Relu
+MULT = mybir.AluOpType.mult
+ADD = mybir.AluOpType.add
+
+
+def tile_picked_devox_none_e_kernel(
+    tc, xT, w1, w2, gate, emb, offs, cell, pos1, pos2, pos3, pos4, out
+):
+    nc = tc.nc
+    with ExitStack() as ctx:
+        lists = ctx.enter_context(tc.tile_pool(name="lists", bufs=1))
+        keep = ctx.enter_context(tc.tile_pool(name="keep", bufs=1))
+        ring = ctx.enter_context(tc.tile_pool(name="ring", bufs=3))
+        psum = ctx.enter_context(tc.psum_pool(name="psum", bufs=1))
+
+        def bank(b, name):
+            return psum.tile([P, 512], F32, name=name, tag="bank%d" % b)
+
+        def load_list(src, name):
+            t = lists.tile([P, S // 16], U16, name=name)
+            nc.sync.dma_start(t[:], src)
+            return t
+
+        def quantize(codes, scales, values):
+            nc.vector.quantize_mx(out=codes.bitcast(FP8X4), scales=scales, in_=values)
+
+        def product(dst, w_codes, w_scales, x_codes, x_scales):
+            nc.tensor.matmul_mx(
+                out=dst, lhsT=w_codes.bitcast(FP8X4), lhsT_scale=w_scales,
+                rhs=x_codes.bitcast(FP8X4), rhs_scale=x_scales, start=True, stop=True,
+            )
+
+        def turn(dst, src, start, stop):
+            nc.tensor.matmul(dst, src, ident[:], start=start, stop=stop, is_transpose=True)
+
+        ident = keep.tile([P, P], F32, name="ident")
+        make_identity(nc, ident[:])
+        gate_rows = keep.tile([P, V], F32, name="gate_rows")
+        nc.vector.memset(gate_rows[:], 0.0)
+        up = []
+        for k in range(4):
+            up.append(keep.tile([P, U], F32, name="up%d" % k))
+            nc.vector.memset(up[k][:], 0.0)
+
+        x_rows = xT.rearrange("(p j) t -> j p t", j=4)
+        w1_rows = w1.rearrange("(p j) c -> p j c", j=4)
+        emb_rows = emb.rearrange("(f r a) c -> f a r c", f=2, a=2)
+        offs_t = load_list(offs, "offs_t")
+        w1_raw = [keep.tile([P, 4, 256], F32, name="w1_raw%d" % f) for f in range(2)]
+        x_plane = [keep.tile([P, T], F32, name="x_plane%d" % j) for j in range(4)]
+        emb_t = [keep.tile([P, U], F32, name="emb_t%d" % k) for k in range(4)]
+        w2_raw = keep.tile([P, 4, N], F32, name="w2_raw")
+        gate_last = keep.tile([P, V], F32, name="gate_last")
+        nc.sync.dma_start(w1_raw[0][:], w1_rows[:, :, 0:256])
+        for j in range(4):
+            nc.sync.dma_start(x_plane[j][:], x_rows[j])
+        cell_t = load_list(cell, "cell_t")
+        nc.sync.dma_start(w1_raw[1][:], w1_rows[:, :, 256:512])
+        nc.sync.dma_start(emb_t[0][:], emb_rows[0, 0])
+        nc.sync.dma_start(w2_raw[:], w2.rearrange("(p j) c -> p j c", j=4))
+        for k in range(1, 4):
+            nc.sync.dma_start(emb_t[k][:], emb_rows[k // 2, k % 2])
+        nc.sync.dma_start(gate_rows[0:D, :], gate[:, 0, :])
+        pos_t = [load_list(src, "pos_t%d" % d) for d, src in enumerate((pos1, pos2, pos3, pos4))]
+        nc.sync.dma_start(gate_last[:], gate[D - 1])
+
+        w1_bf = [keep.tile([P, 256, 4], BF16, name="w1_bf%d" % f, align_bytes=64) for f in range(2)]
+        w1_codes = [keep.tile([P, 256], U32, name="w1_codes%d" % f, align_bytes=64) for f in range(2)]
+        w1_scales = [keep.tile([P, 256], U8, name="w1_scales%d" % f, align_bytes=64) for f in range(2)]
+
+        def prepare_w1(f):
+            nc.scalar.copy(
+                w1_bf[f][:].rearrange("p (a r) j -> p a r j", a=2),
+                w1_raw[f][:].rearrange("p j (r a) -> p a r j", a=2),
+            )
+            quantize(w1_codes[f][:], w1_scales[f][:], w1_bf[f][:].rearrange("p c j -> p (c j)"))
+
+        prepare_w1(0)
+
+        x_bf = [keep.tile([P, 256, 4], BF16, name="x_bf%d" % s, align_bytes=64) for s in range(2)]
+        x_codes = keep.tile([P, S], U32, name="x_codes", align_bytes=64)
+        x_scales = keep.tile([P, S], U8, name="x_scales", align_bytes=64)
+        halves = [slice(0, 256), slice(256, 512)]
+        list_halves = [slice(0, 16), slice(16, 32)]
+        h_first = [keep.tile([P, 256], F32, name="h_first%d" % s) for s in range(2)]
+        for j in range(4):
+            for s in range(2):
+                nc.vector.tensor_copy(x_bf[s][:, :, j], x_plane[j][:].indirect(offs_t[:, list_halves[s]]))
+                if j == 3:
+                    quantize(x_codes[:, halves[s]], x_scales[:, halves[s]], x_bf[s][:].rearrange("p c j -> p (c j)"))
+                    acc = bank(4 + s, "h_first_ps%d" % s)
+                    product(acc[:, 0:256], w1_codes[0][:, 0:P], w1_scales[0][:, 0:P],
+                            x_codes[:, halves[s]], x_scales[:, halves[s]])
+                    nc.scalar.activation(h_first[s][:], acc[:, 0:256], RELU)
+
+        h = [None]
+
+        def first_product(k):
+            f, a = divmod(k, 2)
+            acc = bank(4 + (k + 1) % 4, "h_ps%d" % k)
+            product(acc[:], w1_codes[f][:, a * P:(a + 1) * P], w1_scales[f][:, a * P:(a + 1) * P],
+                    x_codes[:], x_scales[:])
+            h.append(keep.tile([P, S], F32, name="h%d" % k, tag="h%d" % k, align_bytes=64))
+            nc.scalar.activation(h[k][:], acc[:], RELU)
+
+        for s in range(2):
+            nc.vector.tensor_copy(up[0][:].indirect(cell_t[:, list_halves[s]]), h_first[s][:])
+        first_product(1)
+        prepare_w1(1)
+        nc.vector.tensor_copy(up[1][:].indirect(cell_t[:]), h[1][:])
+        first_product(2)
+        first_product(3)
+        nc.vector.tensor_copy(up[2][:].indirect(cell_t[:]), h[2][:])
+        nc.vector.tensor_copy(up[3][:].indirect(cell_t[:]), h[3][:])
+
+        w2_bf = keep.tile([P, N, 4], BF16, name="w2_bf", align_bytes=64)
+        nc.scalar.copy(
+            w2_bf[:].rearrange("p m (u e) -> p m u e", u=2),
+            w2_raw[:].rearrange("p (e u) m -> p m u e", u=2),
+        )
+        w2_codes = keep.tile([P, N], U32, name="w2_codes", tag="h3", align_bytes=64)
+        w2_scales = keep.tile([P, N], U8, name="w2_scales", align_bytes=64)
+        quantize(w2_codes[:], w2_scales[:], w2_bf[:].rearrange("p m j -> p (m j)"))
+
+        zT = [[keep.tile([P, 4, 256], BF16, name="zT%d_%d" % (u, c)) for c in range(2)] for u in range(2)]
+        sums = {}
+
+        def emb_turn(k):
+            for c in range(2):
+                sums[k, c] = bank(2 * (k % 2) + c, "sum%d_%d" % (k, c))
+                for b in range(4):
+                    cells = slice((4 * c + b) * P, (4 * c + b + 1) * P)
+                    turn(sums[k, c][:, b * P:(b + 1) * P], emb_t[k][:, cells], b == 0, False)
+
+        def up_turn(k):
+            f, a = divmod(k, 2)
+            for c in range(2):
+                for b in range(4):
+                    cells = slice((4 * c + b) * P, (4 * c + b + 1) * P)
+                    turn(sums[k, c][:, b * P:(b + 1) * P], up[k][:, cells], False, b == 3)
+                dst = zT[a][c][:, :, f * P:(f + 1) * P]
+                src = sums[k, c][:].rearrange("p (b r) -> p b r", b=4)
+                if k == 3 and c == 1:
+                    nc.vector.tensor_copy(dst, src)
+                else:
+                    nc.scalar.copy(dst, src)
+
+        def back_turn(u, q):
+            c, b0 = divmod(2 * q, 4)
+            words = zT[u][c][:].rearrange("p b r -> p (b r)").bitcast(F32)
+            for b in range(2):
+                dst = back[q][:, u * 256 + b * P:u * 256 + (b + 1) * P]
+                turn(dst, words[:, (b0 + b) * P:(b0 + b + 1) * P], True, True)
+
+        emb_turn(0)
+        emb_turn(1)
+        up_turn(0)
+        emb_turn(2)
+        gate_ps = bank(5, "gate_ps")
+        for b in range(4):
+            turn(gate_ps[:, b * P:(b + 1) * P], gate_rows[:, b * P:(b + 1) * P], True, True)
+        gate_cols = keep.tile([P, 4, D], F32, name="gate_cols")
+        nc.scalar.copy(gate_cols[:], gate_ps[:].rearrange("p (b r) -> p b r", b=4)[:, :, 0:D])
+        up_turn(1)
+        emb_turn(3)
+        up_turn(2)
+        back = [bank(4 + q, "back%d" % q) for q in range(4)]
+        for q in range(4):
+            back_turn(0, q)
+        up_turn(3)
+
+        y = [keep.tile([P, U], F32, name="y%d" % n) for n in range(2)]
+        z_bf = [keep.tile([P, 256, 4], BF16, name="z_bf%d" % q, align_bytes=64) for q in range(4)]
+        z_codes = [keep.tile([P, 256], U32, name="z_codes%d" % q, align_bytes=64) for q in range(4)]
+        z_scales = [keep.tile([P, 256], U8, name="z_scales%d" % q, align_bytes=64) for q in range(4)]
+        for q in range(4):
+            back_turn(1, q)
+            dst = z_bf[q][:].rearrange("p c j -> p (c j)").bitcast(F32).rearrange("p (c u) -> p c u", u=2)
+            src = back[q][:].rearrange("p (u c) -> p c u", u=2)
+            if q == 1:
+                nc.vector.tensor_copy(dst, src)
+            else:
+                nc.scalar.copy(dst, src)
+        for q in range(4):
+            quantize(z_codes[q][:], z_scales[q][:], z_bf[q][:].rearrange("p c j -> p (c j)"))
+            acc = bank(q, "y0_ps%d" % q)
+            product(acc[:, 0:256], w2_codes[:, 0:P], w2_scales[:, 0:P], z_codes[q][:], z_scales[q][:])
+            nc.scalar.copy(y[0][:, q * 256:(q + 1) * 256], acc[:, 0:256])
+        for c in range(2):
+            acc = bank(4 + c, "y1_ps%d" % c)
+            for b in range(2):
+                q = 2 * c + b
+                product(acc[:, b * 256:(b + 1) * 256], w2_codes[:, P:N], w2_scales[:, P:N],
+                        z_codes[q][:], z_scales[q][:])
+            nc.scalar.copy(y[1][:, c * 512:(c + 1) * 512], acc[:])
+
+        total = [bank(6 + n, "total%d" % n) for n in range(2)]
+        steps = [(n, d) for n in range(2) for d in range(D)][:-1]
+        scaled = {}
+
+        def fetch(i):
+            n, d = steps[i]
+            got = ring.tile([P, V], F32, name="got")
+            nc.vector.tensor_copy(got[:], y[n][:].indirect(pos_t[d][:]))
+            turned = bank(i % 4, "turned%d" % i)
+            for b in range(4):
+                turn(turned[:, b * P:(b + 1) * P], got[:, b * P:(b + 1) * P], True, True)
+            scaled[i] = ring.tile([P, V], F32, name="scaled")
+            for b in range(4):
+                nc.scalar.activation(scaled[i][:, b * P:(b + 1) * P], turned[:, b * P:(b + 1) * P], COPY,
+                                     scale=gate_cols[:, b, d:d + 1])
+
+        def add_up(i):
+            n, d = steps[i]
+            last = i + 1 == len(steps) or steps[i + 1][0] != n
+            for b in range(4):
+                turn(total[n][:, b * P:(b + 1) * P], scaled[i][:, b * P:(b + 1) * P],
+                     d == 0 and b == 0, last and b == 3)
+            if last and n == 0:
+                res = keep.tile([P, V], F32, name="res0")
+                nc.scalar.copy(res[:], total[0][:])
+                nc.sync.dma_start(out[0:P, :], res[:])
+
+        fetch(0)
+        for i in range(1, len(steps)):
+            fetch(i)
+            add_up(i - 1)
+        add_up(len(steps) - 1)
+        last_term = keep.tile([P, V], F32, name="last_term")
+        nc.vector.tensor_tensor(last_term[:], y[1][:].indirect(pos_t[D - 1][:]), gate_last[:], MULT)
+        res = keep.tile([P, V], F32, name="res1")
+        nc.vector.tensor_tensor(res[:], total[1][:], last_term[:], ADD)
+        nc.sync.dma_start(out[P:N, :], res[:])

@@ -68,6 +68,7 @@ def tile_picked_devox_none_e_kernel(
         w2_raw = keep.tile([P, 4, N], F32, name="w2_raw")
         gate_last = keep.tile([P, V], F32, name="gate_last")
         nc.sync.dma_start(w1_raw[0][:], w1_rows[:, :, 0:256])
+        nc.sync.dma_start(gate_rows[0:D, :], gate[:, 0, :])
         for j in range(4):
             nc.sync.dma_start(x_plane[j][:], x_rows[j])
         cell_t = load_list(cell, "cell_t")
@@ -75,8 +76,7 @@ def tile_picked_devox_none_e_kernel(
         nc.sync.dma_start(emb_t[0][:], emb_rows[0, 0])
         nc.sync.dma_start(w2_raw[:], w2.rearrange("(p j) c -> p j c", j=4))
         for k in range(1, 4):
-            nc.sync.dma_start(emb_t[k][:], emb_rows[k // 2, k % 2])
-        nc.sync.dma_start(gate_rows[0:D, :], gate[:, 0, :])
+            nc.sync.dma_start(emb_t[k][:], emb_rows[k % 2, k // 2])
         pos_t = [load_list(src, "pos_t%d" % d) for d, src in enumerate((pos1, pos2, pos3, pos4))]
         nc.sync.dma_start(gate_last[:], gate[D - 1])
 
@@ -92,13 +92,18 @@ def tile_picked_devox_none_e_kernel(
             quantize(w1_codes[f][:], w1_scales[f][:], w1_bf[f][:].rearrange("p c j -> p (c j)"))
 
         prepare_w1(0)
+        gate_ps = bank(7, "gate_ps")
+        for b in range(4):
+            turn(gate_ps[:, b * P:(b + 1) * P], gate_rows[:, b * P:(b + 1) * P], True, True)
+        gate_cols = keep.tile([P, 4, D], F32, name="gate_cols")
+        nc.scalar.copy(gate_cols[:], gate_ps[:].rearrange("p (b r) -> p b r", b=4)[:, :, 0:D])
 
         x_bf = [keep.tile([P, 256, 4], BF16, name="x_bf%d" % s, align_bytes=64) for s in range(2)]
         x_codes = keep.tile([P, S], U32, name="x_codes", align_bytes=64)
         x_scales = keep.tile([P, S], U8, name="x_scales", align_bytes=64)
         halves = [slice(0, 256), slice(256, 512)]
         list_halves = [slice(0, 16), slice(16, 32)]
-        h_first = [keep.tile([P, 256], F32, name="h_first%d" % s) for s in range(2)]
+        h_first = []
         for j in range(4):
             for s in range(2):
                 nc.vector.tensor_copy(x_bf[s][:, :, j], x_plane[j][:].indirect(offs_t[:, list_halves[s]]))
@@ -107,13 +112,16 @@ def tile_picked_devox_none_e_kernel(
                     acc = bank(4 + s, "h_first_ps%d" % s)
                     product(acc[:, 0:256], w1_codes[0][:, 0:P], w1_scales[0][:, 0:P],
                             x_codes[:, halves[s]], x_scales[:, halves[s]])
+                    if s == 1:
+                        prepare_w1(1)
+                    h_first.append(keep.tile([P, 256], F32, name="h_first%d" % s, tag=("h_first0", "w1_raw1")[s]))
                     nc.scalar.activation(h_first[s][:], acc[:, 0:256], RELU)
 
         h = [None]
 
         def first_product(k):
-            f, a = divmod(k, 2)
-            acc = bank(4 + (k + 1) % 4, "h_ps%d" % k)
+            a, f = divmod(k, 2)
+            acc = bank(6, "h_ps%d" % k)
             product(acc[:], w1_codes[f][:, a * P:(a + 1) * P], w1_scales[f][:, a * P:(a + 1) * P],
                     x_codes[:], x_scales[:])
             h.append(keep.tile([P, S], F32, name="h%d" % k, tag="h%d" % k, align_bytes=64))
@@ -122,7 +130,6 @@ def tile_picked_devox_none_e_kernel(
         for s in range(2):
             nc.vector.tensor_copy(up[0][:].indirect(cell_t[:, list_halves[s]]), h_first[s][:])
         first_product(1)
-        prepare_w1(1)
         nc.vector.tensor_copy(up[1][:].indirect(cell_t[:]), h[1][:])
         first_product(2)
         first_product(3)
@@ -138,59 +145,61 @@ def tile_picked_devox_none_e_kernel(
         w2_scales = keep.tile([P, N], U8, name="w2_scales", align_bytes=64)
         quantize(w2_codes[:], w2_scales[:], w2_bf[:].rearrange("p m j -> p (m j)"))
 
-        zT = [[keep.tile([P, 4, 256], BF16, name="zT%d_%d" % (u, c)) for c in range(2)] for u in range(2)]
+        zT = [[keep.tile([P, 2, 256], BF16, name="zT%d_%d" % (u, q)) for q in range(4)] for u in range(2)]
         sums = {}
 
-        def emb_turn(k):
-            for c in range(2):
-                sums[k, c] = bank(2 * (k % 2) + c, "sum%d_%d" % (k, c))
-                for b in range(4):
-                    cells = slice((4 * c + b) * P, (4 * c + b + 1) * P)
-                    turn(sums[k, c][:, b * P:(b + 1) * P], emb_t[k][:, cells], b == 0, False)
+        def emb_turn(k, blocks):
+            per_bank = 2 if k == 3 else 4
+            for b in blocks:
+                if b % per_bank == 0:
+                    which = (2 * (k % 2) + b // per_bank) % 4
+                    acc = bank(which, "sum%d_%d" % (k, b))
+                sums[k, b] = acc[:, (b % per_bank) * P:(b % per_bank + 1) * P]
+                if b % 2 == 0:
+                    sums[k, b // 2, "pair"] = acc[:, (b % per_bank) * P:(b % per_bank + 2) * P]
+                turn(sums[k, b], emb_t[k][:, b * P:(b + 1) * P], b % per_bank == 0, False)
 
-        def up_turn(k):
-            f, a = divmod(k, 2)
-            for c in range(2):
-                for b in range(4):
-                    cells = slice((4 * c + b) * P, (4 * c + b + 1) * P)
-                    turn(sums[k, c][:, b * P:(b + 1) * P], up[k][:, cells], False, b == 3)
-                dst = zT[a][c][:, :, f * P:(f + 1) * P]
-                src = sums[k, c][:].rearrange("p (b r) -> p b r", b=4)
-                if k == 3 and c == 1:
-                    nc.vector.tensor_copy(dst, src)
-                else:
-                    nc.scalar.copy(dst, src)
+        def up_turn(k, banks):
+            a, f = divmod(k, 2)
+            per_bank = 2 if k == 3 else 4
+            for c in banks:
+                for b in range(c * per_bank, (c + 1) * per_bank):
+                    turn(sums[k, b], up[k][:, b * P:(b + 1) * P], False, b % per_bank == per_bank - 1)
+                for q in range(c * per_bank // 2, (c + 1) * per_bank // 2):
+                    dst = zT[a][q][:, :, f * P:(f + 1) * P]
+                    src = sums[k, q, "pair"].rearrange("p (b r) -> p b r", b=2)
+                    if k == 3:
+                        nc.vector.tensor_copy(dst, src)
+                    else:
+                        nc.scalar.copy(dst, src)
 
         def back_turn(u, q):
-            c, b0 = divmod(2 * q, 4)
-            words = zT[u][c][:].rearrange("p b r -> p (b r)").bitcast(F32)
+            words = zT[u][q][:].rearrange("p b r -> p (b r)").bitcast(F32)
             for b in range(2):
                 dst = back[q][:, u * 256 + b * P:u * 256 + (b + 1) * P]
-                turn(dst, words[:, (b0 + b) * P:(b0 + b + 1) * P], True, True)
+                turn(dst, words[:, b * P:(b + 1) * P], True, True)
 
-        emb_turn(0)
-        emb_turn(1)
-        up_turn(0)
-        emb_turn(2)
-        gate_ps = bank(5, "gate_ps")
-        for b in range(4):
-            turn(gate_ps[:, b * P:(b + 1) * P], gate_rows[:, b * P:(b + 1) * P], True, True)
-        gate_cols = keep.tile([P, 4, D], F32, name="gate_cols")
-        nc.scalar.copy(gate_cols[:], gate_ps[:].rearrange("p (b r) -> p b r", b=4)[:, :, 0:D])
-        up_turn(1)
-        emb_turn(3)
-        up_turn(2)
+        emb_turn(0, range(8))
+        emb_turn(1, range(8))
+        up_turn(0, range(2))
+        emb_turn(2, range(8))
+        up_turn(1, range(2))
+        emb_turn(3, range(4))
         back = [bank(4 + q, "back%d" % q) for q in range(4)]
         for q in range(4):
             back_turn(0, q)
-        up_turn(3)
+        up_turn(2, range(2))
+        emb_turn(3, range(4, 8))
 
         y = [keep.tile([P, U], F32, name="y%d" % n) for n in range(2)]
         z_bf = [keep.tile([P, 256, 4], BF16, name="z_bf%d" % q, align_bytes=64) for q in range(4)]
         z_codes = [keep.tile([P, 256], U32, name="z_codes%d" % q, align_bytes=64) for q in range(4)]
         z_scales = [keep.tile([P, 256], U8, name="z_scales%d" % q, align_bytes=64) for q in range(4)]
+        up_turn(3, range(3))
         for q in range(4):
             back_turn(1, q)
+            if q == 0:
+                up_turn(3, [3])
             dst = z_bf[q][:].rearrange("p c j -> p (c j)").bitcast(F32).rearrange("p (c u) -> p c u", u=2)
             src = back[q][:].rearrange("p (u c) -> p c u", u=2)
             if q == 1:
@@ -199,7 +208,7 @@ def tile_picked_devox_none_e_kernel(
                 nc.scalar.copy(dst, src)
         for q in range(4):
             quantize(z_codes[q][:], z_scales[q][:], z_bf[q][:].rearrange("p c j -> p (c j)"))
-            acc = bank(q, "y0_ps%d" % q)
+            acc = bank((q + 2) % 4, "y0_ps%d" % q)
             product(acc[:, 0:256], w2_codes[:, 0:P], w2_scales[:, 0:P], z_codes[q][:], z_scales[q][:])
             nc.scalar.copy(y[0][:, q * 256:(q + 1) * 256], acc[:, 0:256])
         for c in range(2):
@@ -211,39 +220,53 @@ def tile_picked_devox_none_e_kernel(
             nc.scalar.copy(y[1][:, c * 512:(c + 1) * 512], acc[:])
 
         total = [bank(6 + n, "total%d" % n) for n in range(2)]
-        steps = [(n, d) for n in range(2) for d in range(D)][:-1]
+        steps = [(n, d) for n in range(2) for d in range(D - 1)]
         scaled = {}
 
         def fetch(i):
             n, d = steps[i]
-            got = ring.tile([P, V], F32, name="got")
+            got = keep.tile([P, V], F32, name="got%d" % i, tag="got%d" % i)
             nc.vector.tensor_copy(got[:], y[n][:].indirect(pos_t[d][:]))
-            turned = bank(i % 4, "turned%d" % i)
-            for b in range(4):
-                turn(turned[:, b * P:(b + 1) * P], got[:, b * P:(b + 1) * P], True, True)
             scaled[i] = ring.tile([P, V], F32, name="scaled")
-            for b in range(4):
-                nc.scalar.activation(scaled[i][:, b * P:(b + 1) * P], turned[:, b * P:(b + 1) * P], COPY,
-                                     scale=gate_cols[:, b, d:d + 1])
+            for c in range(2):
+                turned = bank((2 * i + c + 2) % 6, "turned%d_%d" % (i, c))
+                for b in range(2):
+                    v0 = (2 * c + b) * P
+                    turn(turned[:, b * P:(b + 1) * P], got[:, v0:v0 + P], True, True)
+                for b in range(2):
+                    v0 = (2 * c + b) * P
+                    nc.scalar.activation(scaled[i][:, v0:v0 + P], turned[:, b * P:(b + 1) * P], COPY,
+                                         scale=gate_cols[:, 2 * c + b, d:d + 1])
 
         def add_up(i):
             n, d = steps[i]
-            last = i + 1 == len(steps) or steps[i + 1][0] != n
             for b in range(4):
                 turn(total[n][:, b * P:(b + 1) * P], scaled[i][:, b * P:(b + 1) * P],
-                     d == 0 and b == 0, last and b == 3)
-            if last and n == 0:
-                res = keep.tile([P, V], F32, name="res0")
-                nc.scalar.copy(res[:], total[0][:])
-                nc.sync.dma_start(out[0:P, :], res[:])
+                     d == 0 and b == 0, d == D - 2 and b == 3)
 
         fetch(0)
         for i in range(1, len(steps)):
             fetch(i)
             add_up(i - 1)
         add_up(len(steps) - 1)
-        last_term = keep.tile([P, V], F32, name="last_term")
-        nc.vector.tensor_tensor(last_term[:], y[1][:].indirect(pos_t[D - 1][:]), gate_last[:], MULT)
-        res = keep.tile([P, V], F32, name="res1")
-        nc.vector.tensor_tensor(res[:], total[1][:], last_term[:], ADD)
-        nc.sync.dma_start(out[P:N, :], res[:])
+        pieces = [(0, 0, 512), (1, 0, 256), (1, 256, 512)]
+        last_term = []
+
+        def fetch_last(i):
+            n, v0, v1 = pieces[i]
+            last_term.append(keep.tile([P, v1 - v0], F32, name="last_term%d" % i, tag=("got4", "last1", "last2")[i]))
+            nc.vector.tensor_tensor(last_term[i][:], y[n][:].indirect(pos_t[D - 1][:, v0 // 16:v1 // 16]),
+                                    gate_last[:, v0:v1], MULT)
+
+        def finish(i):
+            n, v0, v1 = pieces[i]
+            res = keep.tile([P, v1 - v0], F32, name="res%d" % i)
+            nc.vector.tensor_tensor(res[:], total[n][:, v0:v1], last_term[i][:], ADD)
+            nc.sync.dma_start(out[n * P:(n + 1) * P, v0:v1], res[:])
+
+        fetch_last(0)
+        fetch_last(1)
+        finish(0)
+        fetch_last(2)
+        finish(1)
+        finish(2)

@@ -65,7 +65,7 @@ def tile_picked_devox_none_e_kernel(
         w1_raw = [keep.tile([P, 4, 256], F32, name="w1_raw%d" % f) for f in range(2)]
         x_plane = [keep.tile([P, T], F32, name="x_plane%d" % j) for j in range(4)]
         emb_t = [keep.tile([P, U], F32, name="emb_t%d" % k) for k in range(4)]
-        w2_raw = keep.tile([P, 4, N], F32, name="w2_raw")
+        w2_raw = keep.tile([P, 4, N], F32, name="w2_raw", tag="h3", align_bytes=64)
         gate_last = keep.tile([P, V], F32, name="gate_last")
         nc.sync.dma_start(w1_raw[0][:], w1_rows[:, :, 0:256])
         nc.sync.dma_start(gate_rows[0:D, :], gate[:, 0, :])
@@ -73,10 +73,9 @@ def tile_picked_devox_none_e_kernel(
             nc.sync.dma_start(x_plane[j][:], x_rows[j])
         cell_t = load_list(cell, "cell_t")
         nc.sync.dma_start(w1_raw[1][:], w1_rows[:, :, 256:512])
-        nc.sync.dma_start(emb_t[0][:], emb_rows[0, 0])
-        nc.sync.dma_start(w2_raw[:], w2.rearrange("(p j) c -> p j c", j=4))
-        for k in range(1, 4):
+        for k in (0, 1, 3, 2):
             nc.sync.dma_start(emb_t[k][:], emb_rows[k % 2, k // 2])
+        nc.sync.dma_start(w2_raw[:], w2.rearrange("(p j) c -> p j c", j=4))
         pos_t = [load_list(src, "pos_t%d" % d) for d, src in enumerate((pos1, pos2, pos3, pos4))]
         nc.sync.dma_start(gate_last[:], gate[D - 1])
 
@@ -132,15 +131,15 @@ def tile_picked_devox_none_e_kernel(
         first_product(1)
         nc.vector.tensor_copy(up[1][:].indirect(cell_t[:]), h[1][:])
         first_product(2)
-        first_product(3)
-        nc.vector.tensor_copy(up[2][:].indirect(cell_t[:]), h[2][:])
-        nc.vector.tensor_copy(up[3][:].indirect(cell_t[:]), h[3][:])
-
         w2_bf = keep.tile([P, N, 4], BF16, name="w2_bf", align_bytes=64)
         nc.scalar.copy(
             w2_bf[:].rearrange("p m (u e) -> p m u e", u=2),
             w2_raw[:].rearrange("p (e u) m -> p m u e", u=2),
         )
+        first_product(3)
+        nc.vector.tensor_copy(up[2][:].indirect(cell_t[:]), h[2][:])
+        nc.vector.tensor_copy(up[3][:].indirect(cell_t[:]), h[3][:])
+
         w2_codes = keep.tile([P, N], U32, name="w2_codes", tag="h3", align_bytes=64)
         w2_scales = keep.tile([P, N], U8, name="w2_scales", align_bytes=64)
         quantize(w2_codes[:], w2_scales[:], w2_bf[:].rearrange("p m j -> p (m j)"))
@@ -148,30 +147,35 @@ def tile_picked_devox_none_e_kernel(
         zT = [[keep.tile([P, 2, 256], BF16, name="zT%d_%d" % (u, q)) for q in range(4)] for u in range(2)]
         sums = {}
 
-        def emb_turn(k, blocks):
-            per_bank = 2 if k == 3 else 4
-            for b in blocks:
-                if b % per_bank == 0:
-                    which = (2 * (k % 2) + b // per_bank) % 4
-                    acc = bank(which, "sum%d_%d" % (k, b))
-                sums[k, b] = acc[:, (b % per_bank) * P:(b % per_bank + 1) * P]
-                if b % 2 == 0:
-                    sums[k, b // 2, "pair"] = acc[:, (b % per_bank) * P:(b % per_bank + 2) * P]
-                turn(sums[k, b], emb_t[k][:, b * P:(b + 1) * P], b % per_bank == 0, False)
+        def open_sums(k, banks):
+            per = 4 // len(banks)
+            sums[k] = [(banks[q // per], (q % per) * 256, q % per == 0, q % per == per - 1) for q in range(4)]
 
-        def up_turn(k, banks):
+        def emb_turn(k, quarters):
+            for q in quarters:
+                acc, col, first, last = sums[k][q]
+                for b in range(2):
+                    cells = slice((2 * q + b) * P, (2 * q + b + 1) * P)
+                    turn(acc[:, col + b * P:col + (b + 1) * P], emb_t[k][:, cells], first and b == 0, False)
+
+        def up_turn(k):
             a, f = divmod(k, 2)
-            per_bank = 2 if k == 3 else 4
-            for c in banks:
-                for b in range(c * per_bank, (c + 1) * per_bank):
-                    turn(sums[k, b], up[k][:, b * P:(b + 1) * P], False, b % per_bank == per_bank - 1)
-                for q in range(c * per_bank // 2, (c + 1) * per_bank // 2):
-                    dst = zT[a][q][:, :, f * P:(f + 1) * P]
-                    src = sums[k, q, "pair"].rearrange("p (b r) -> p b r", b=2)
-                    if k == 3:
-                        nc.vector.tensor_copy(dst, src)
-                    else:
-                        nc.scalar.copy(dst, src)
+            ready = []
+            for q in range(4):
+                acc, col, first, last = sums[k][q]
+                for b in range(2):
+                    cells = slice((2 * q + b) * P, (2 * q + b + 1) * P)
+                    turn(acc[:, col + b * P:col + (b + 1) * P], up[k][:, cells], False, last and b == 1)
+                ready.append(q)
+                if last:
+                    for r in ready:
+                        dst = zT[a][r][:, :, f * P:(f + 1) * P]
+                        src = acc[:, sums[k][r][1]:sums[k][r][1] + 256].rearrange("p (b r) -> p b r", b=2)
+                        if k == 3 and r % 2 == 1:
+                            nc.vector.tensor_copy(dst, src)
+                        else:
+                            nc.scalar.copy(dst, src)
+                    ready = []
 
         def back_turn(u, q):
             words = zT[u][q][:].rearrange("p b r -> p (b r)").bitcast(F32)
@@ -179,27 +183,29 @@ def tile_picked_devox_none_e_kernel(
                 dst = back[q][:, u * 256 + b * P:u * 256 + (b + 1) * P]
                 turn(dst, words[:, b * P:(b + 1) * P], True, True)
 
-        emb_turn(0, range(8))
-        emb_turn(1, range(8))
-        up_turn(0, range(2))
-        emb_turn(2, range(8))
-        up_turn(1, range(2))
-        emb_turn(3, range(4))
+        open_sums(0, [bank(0, "sum0_0"), bank(1, "sum0_1")])
+        emb_turn(0, range(4))
+        open_sums(1, [bank(4, "sum1_0"), bank(5, "sum1_1")])
+        emb_turn(1, range(4))
+        late = [bank(2, "sum3_2"), bank(3, "sum3_3")]
+        up_turn(0)
+        open_sums(3, [bank(0, "sum3_0"), bank(1, "sum3_1")] + late)
+        emb_turn(3, (2, 3, 0, 1))
+        up_turn(1)
         back = [bank(4 + q, "back%d" % q) for q in range(4)]
         for q in range(4):
             back_turn(0, q)
-        up_turn(2, range(2))
-        emb_turn(3, range(4, 8))
+        sums[2] = [(back[q], 256, True, True) for q in range(4)]
+        emb_turn(2, range(4))
+        up_turn(2)
 
         y = [keep.tile([P, U], F32, name="y%d" % n) for n in range(2)]
         z_bf = [keep.tile([P, 256, 4], BF16, name="z_bf%d" % q, align_bytes=64) for q in range(4)]
         z_codes = [keep.tile([P, 256], U32, name="z_codes%d" % q, align_bytes=64) for q in range(4)]
         z_scales = [keep.tile([P, 256], U8, name="z_scales%d" % q, align_bytes=64) for q in range(4)]
-        up_turn(3, range(3))
+        up_turn(3)
         for q in range(4):
             back_turn(1, q)
-            if q == 0:
-                up_turn(3, [3])
             dst = z_bf[q][:].rearrange("p c j -> p (c j)").bitcast(F32).rearrange("p (c u) -> p c u", u=2)
             src = back[q][:].rearrange("p (u c) -> p c u", u=2)
             if q == 1:
@@ -208,19 +214,23 @@ def tile_picked_devox_none_e_kernel(
                 nc.scalar.copy(dst, src)
         for q in range(4):
             quantize(z_codes[q][:], z_scales[q][:], z_bf[q][:].rearrange("p c j -> p (c j)"))
-            acc = bank((q + 2) % 4, "y0_ps%d" % q)
+            acc = bank(q, "y0_ps%d" % q)
             product(acc[:, 0:256], w2_codes[:, 0:P], w2_scales[:, 0:P], z_codes[q][:], z_scales[q][:])
-            nc.scalar.copy(y[0][:, q * 256:(q + 1) * 256], acc[:, 0:256])
+            if q == 2:
+                nc.vector.tensor_copy(y[0][:, q * 256:(q + 1) * 256], acc[:, 0:256])
+            else:
+                nc.scalar.copy(y[0][:, q * 256:(q + 1) * 256], acc[:, 0:256])
         for c in range(2):
-            acc = bank(4 + c, "y1_ps%d" % c)
+            acc = bank(3 - c, "y1_ps%d" % c)
             for b in range(2):
                 q = 2 * c + b
                 product(acc[:, b * 256:(b + 1) * 256], w2_codes[:, P:N], w2_scales[:, P:N],
                         z_codes[q][:], z_scales[q][:])
             nc.scalar.copy(y[1][:, c * 512:(c + 1) * 512], acc[:])
 
-        total = [bank(6 + n, "total%d" % n) for n in range(2)]
-        steps = [(n, d) for n in range(2) for d in range(D - 1)]
+        total0 = bank(7, "total0")
+        total1 = [bank(5 + c, "total1_%d" % c) for c in range(2)]
+        steps = [(n, d) for n in range(2) for d in range(D)][:-1]
         scaled = {}
 
         def fetch(i):
@@ -229,7 +239,7 @@ def tile_picked_devox_none_e_kernel(
             nc.vector.tensor_copy(got[:], y[n][:].indirect(pos_t[d][:]))
             scaled[i] = ring.tile([P, V], F32, name="scaled")
             for c in range(2):
-                turned = bank((2 * i + c + 2) % 6, "turned%d_%d" % (i, c))
+                turned = bank((2 * i + c + 4) % 5, "turned%d_%d" % (i, c))
                 for b in range(2):
                     v0 = (2 * c + b) * P
                     turn(turned[:, b * P:(b + 1) * P], got[:, v0:v0 + P], True, True)
@@ -241,32 +251,28 @@ def tile_picked_devox_none_e_kernel(
         def add_up(i):
             n, d = steps[i]
             for b in range(4):
-                turn(total[n][:, b * P:(b + 1) * P], scaled[i][:, b * P:(b + 1) * P],
-                     d == 0 and b == 0, d == D - 2 and b == 3)
+                src = scaled[i][:, b * P:(b + 1) * P]
+                if n == 0:
+                    turn(total0[:, b * P:(b + 1) * P], src, d == 0 and b == 0, d == D - 1 and b == 3)
+                else:
+                    turn(total1[b // 2][:, (b % 2) * P:(b % 2 + 1) * P], src,
+                         d == 0 and b % 2 == 0, d == D - 2 and b % 2 == 1)
+            if n == 0 and d == D - 1:
+                res0 = keep.tile([P, V], F32, name="res0")
+                nc.scalar.copy(res0[:], total0[:])
+                nc.sync.dma_start(out[0:P, :], res0[:])
 
         fetch(0)
         for i in range(1, len(steps)):
             fetch(i)
             add_up(i - 1)
         add_up(len(steps) - 1)
-        pieces = [(0, 0, 512), (1, 0, 256), (1, 256, 512)]
         last_term = []
-
-        def fetch_last(i):
-            n, v0, v1 = pieces[i]
-            last_term.append(keep.tile([P, v1 - v0], F32, name="last_term%d" % i, tag=("got4", "last1", "last2")[i]))
-            nc.vector.tensor_tensor(last_term[i][:], y[n][:].indirect(pos_t[D - 1][:, v0 // 16:v1 // 16]),
-                                    gate_last[:, v0:v1], MULT)
-
-        def finish(i):
-            n, v0, v1 = pieces[i]
-            res = keep.tile([P, v1 - v0], F32, name="res%d" % i)
-            nc.vector.tensor_tensor(res[:], total[n][:, v0:v1], last_term[i][:], ADD)
-            nc.sync.dma_start(out[n * P:(n + 1) * P, v0:v1], res[:])
-
-        fetch_last(0)
-        fetch_last(1)
-        finish(0)
-        fetch_last(2)
-        finish(1)
-        finish(2)
+        for c in range(2):
+            last_term.append(keep.tile([P, 256], F32, name="last_term%d" % c))
+            nc.vector.tensor_tensor(last_term[c][:], y[1][:].indirect(pos_t[D - 1][:, list_halves[c]]),
+                                    gate_last[:, halves[c]], MULT)
+        for c in range(2):
+            res1 = keep.tile([P, 256], F32, name="res1_%d" % c)
+            nc.vector.tensor_tensor(res1[:], total1[c][:, 0:256], last_term[c][:], ADD)
+            nc.sync.dma_start(out[P:N, halves[c]], res1[:])

@@ -68,13 +68,14 @@ def tile_picked_devox_none_e_kernel(
         w2_raw = keep.tile([P, 4, N], F32, name="w2_raw", tag="h3", align_bytes=64)
         gate_last = keep.tile([P, V], F32, name="gate_last")
         nc.sync.dma_start(w1_raw[0][:], w1_rows[:, :, 0:256])
-        nc.sync.dma_start(gate_rows[0:D, :], gate[:, 0, :])
         for j in range(4):
             nc.sync.dma_start(x_plane[j][:], x_rows[j])
         cell_t = load_list(cell, "cell_t")
         nc.sync.dma_start(w1_raw[1][:], w1_rows[:, :, 256:512])
         for k in (0, 1, 3, 2):
             nc.sync.dma_start(emb_t[k][:], emb_rows[k % 2, k // 2])
+            if k == 1:
+                nc.sync.dma_start(gate_rows[0:D, :], gate[:, 0, :])
         nc.sync.dma_start(w2_raw[:], w2.rearrange("(p j) c -> p j c", j=4))
         pos_t = [load_list(src, "pos_t%d" % d) for d, src in enumerate((pos1, pos2, pos3, pos4))]
         nc.sync.dma_start(gate_last[:], gate[D - 1])
@@ -91,23 +92,22 @@ def tile_picked_devox_none_e_kernel(
             quantize(w1_codes[f][:], w1_scales[f][:], w1_bf[f][:].rearrange("p c j -> p (c j)"))
 
         prepare_w1(0)
-        gate_ps = bank(7, "gate_ps")
-        for b in range(4):
-            turn(gate_ps[:, b * P:(b + 1) * P], gate_rows[:, b * P:(b + 1) * P], True, True)
-        gate_cols = keep.tile([P, 4, D], F32, name="gate_cols")
-        nc.scalar.copy(gate_cols[:], gate_ps[:].rearrange("p (b r) -> p b r", b=4)[:, :, 0:D])
 
-        x_bf = [keep.tile([P, 256, 4], BF16, name="x_bf%d" % s, align_bytes=64) for s in range(2)]
+        x_bf = keep.tile([P, S, 4], BF16, name="x_bf", align_bytes=64)
         x_codes = keep.tile([P, S], U32, name="x_codes", align_bytes=64)
         x_scales = keep.tile([P, S], U8, name="x_scales", align_bytes=64)
         halves = [slice(0, 256), slice(256, 512)]
         list_halves = [slice(0, 16), slice(16, 32)]
         h_first = []
-        for j in range(4):
+        for j in range(3):
+            nc.vector.tensor_copy(x_bf[:, :, j], x_plane[j][:].indirect(offs_t[:]))
+        for j in range(3, 4):
             for s in range(2):
-                nc.vector.tensor_copy(x_bf[s][:, :, j], x_plane[j][:].indirect(offs_t[:, list_halves[s]]))
+                c0, c1 = ((0, 16), (14, 32))[s]
+                nc.vector.tensor_copy(x_bf[:, 16 * c0:16 * c1, j], x_plane[j][:].indirect(offs_t[:, c0:c1]))
                 if j == 3:
-                    quantize(x_codes[:, halves[s]], x_scales[:, halves[s]], x_bf[s][:].rearrange("p c j -> p (c j)"))
+                    quantize(x_codes[:, halves[s]], x_scales[:, halves[s]],
+                             x_bf[:, halves[s], :].rearrange("p c j -> p (c j)"))
                     acc = bank(4 + s, "h_first_ps%d" % s)
                     product(acc[:, 0:256], w1_codes[0][:, 0:P], w1_scales[0][:, 0:P],
                             x_codes[:, halves[s]], x_scales[:, halves[s]])
@@ -187,6 +187,11 @@ def tile_picked_devox_none_e_kernel(
         emb_turn(0, range(4))
         open_sums(1, [bank(4, "sum1_0"), bank(5, "sum1_1")])
         emb_turn(1, range(4))
+        gate_ps = bank(7, "gate_ps")
+        for b in range(4):
+            turn(gate_ps[:, b * P:(b + 1) * P], gate_rows[:, b * P:(b + 1) * P], True, True)
+        gate_cols = keep.tile([P, 4, D], F32, name="gate_cols")
+        nc.scalar.copy(gate_cols[:], gate_ps[:].rearrange("p (b r) -> p b r", b=4)[:, :, 0:D])
         late = [bank(2, "sum3_2"), bank(3, "sum3_3")]
         up_turn(0)
         open_sums(3, [bank(0, "sum3_0"), bank(1, "sum3_1")] + late)
@@ -236,9 +241,13 @@ def tile_picked_devox_none_e_kernel(
         def fetch(i):
             n, d = steps[i]
             got = keep.tile([P, V], F32, name="got%d" % i, tag="got%d" % i)
-            nc.vector.tensor_copy(got[:], y[n][:].indirect(pos_t[d][:]))
+            in_halves = i == len(steps) - 1
+            if not in_halves:
+                nc.vector.tensor_copy(got[:], y[n][:].indirect(pos_t[d][:]))
             scaled[i] = ring.tile([P, V], F32, name="scaled")
             for c in range(2):
+                if in_halves:
+                    nc.vector.tensor_copy(got[:, halves[c]], y[n][:].indirect(pos_t[d][:, list_halves[c]]))
                 turned = bank((2 * i + c + 4) % 5, "turned%d_%d" % (i, c))
                 for b in range(2):
                     v0 = (2 * c + b) * P

@@ -4,8 +4,14 @@ import concourse.mybir as mybir
 from concourse.masks import make_identity
 
 K, T, S, D, V, H, N, U = 512, 2048, 512, 4, 512, 512, 256, 1024
-P = 128
 FLOPS = 2 * K * H * S + 2 * H * N * U
+
+P = 128
+PACK = 4
+HALF = 256
+BANK = 512
+STRIPE = 16
+ROW_TILES = ((0, 0), (0, 1), (1, 1), (1, 0))
 
 F32 = mybir.dt.float32
 BF16 = mybir.dt.bfloat16
@@ -19,6 +25,10 @@ MULT = mybir.AluOpType.mult
 ADD = mybir.AluOpType.add
 
 
+def span(index, width):
+    return slice(index * width, (index + 1) * width)
+
+
 def tile_picked_devox_none_e_kernel(
     tc, xT, w1, w2, gate, emb, offs, cell, pos1, pos2, pos3, pos4, out
 ):
@@ -30,108 +40,111 @@ def tile_picked_devox_none_e_kernel(
         psum = ctx.enter_context(tc.psum_pool(name="psum", bufs=1))
 
         def bank(b, name):
-            return psum.tile([P, 512], F32, name=name, tag="bank%d" % b)
+            return psum.tile([P, BANK], F32, name=name, tag="bank%d" % b)
 
         def load_list(src, name):
-            t = lists.tile([P, S // 16], U16, name=name)
-            nc.sync.dma_start(t[:], src)
-            return t
+            offsets = lists.tile([P, S // STRIPE], U16, name=name)
+            nc.sync.dma_start(offsets[:], src)
+            return offsets
 
         def quantize(codes, scales, values):
-            nc.vector.quantize_mx(out=codes.bitcast(FP8X4), scales=scales, in_=values)
+            nc.vector.quantize_mx(out=codes.bitcast(FP8X4), scales=scales, in_=values.rearrange("p c j -> p (c j)"))
 
-        def product(dst, w_codes, w_scales, x_codes, x_scales):
+        def product(dst, w_codes, w_scales, moving_codes, moving_scales):
             nc.tensor.matmul_mx(
                 out=dst, lhsT=w_codes.bitcast(FP8X4), lhsT_scale=w_scales,
-                rhs=x_codes.bitcast(FP8X4), rhs_scale=x_scales, start=True, stop=True,
+                rhs=moving_codes.bitcast(FP8X4), rhs_scale=moving_scales, start=True, stop=True,
             )
 
         def turn(dst, src, start, stop):
             nc.tensor.matmul(dst, src, ident[:], start=start, stop=stop, is_transpose=True)
+
+        def copy_on(engine, dst, src):
+            if engine == "vector":
+                nc.vector.tensor_copy(dst, src)
+            else:
+                nc.scalar.copy(dst, src)
 
         ident = keep.tile([P, P], F32, name="ident")
         make_identity(nc, ident[:])
         gate_rows = keep.tile([P, V], F32, name="gate_rows")
         nc.vector.memset(gate_rows[:], 0.0)
         up = []
-        for k in range(4):
-            up.append(keep.tile([P, U], F32, name="up%d" % k))
-            nc.vector.memset(up[k][:], 0.0)
+        for t in range(4):
+            up.append(keep.tile([P, U], F32, name="up%d" % t))
+            nc.vector.memset(up[t][:], 0.0)
 
-        x_rows = xT.rearrange("(p j) t -> j p t", j=4)
-        w1_rows = w1.rearrange("(p j) c -> p j c", j=4)
-        emb_rows = emb.rearrange("(f r a) c -> f a r c", f=2, a=2)
-        offs_t = load_list(offs, "offs_t")
-        w1_raw = [keep.tile([P, 4, 256], F32, name="w1_raw%d" % f) for f in range(2)]
-        x_plane = [keep.tile([P, T], F32, name="x_plane%d" % j) for j in range(4)]
-        emb_t = [keep.tile([P, U], F32, name="emb_t%d" % k) for k in range(4)]
-        w2_raw = keep.tile([P, 4, N], F32, name="w2_raw", tag="h3", align_bytes=64)
+        x_rows = xT.rearrange("(p j) c -> j p c", j=PACK)
+        w1_rows = w1.rearrange("(p j) c -> p j c", j=PACK)
+        emb_rows = emb.rearrange("(f r u) c -> f u r c", f=2, u=2)
+        w1_raw = [keep.tile([P, PACK, HALF], F32, name="w1_raw%d" % f) for f in range(2)]
+        x_plane = [keep.tile([P, T], F32, name="x_plane%d" % j) for j in range(PACK)]
+        emb_t = [keep.tile([P, U], F32, name="emb_t%d" % t) for t in range(4)]
+        w2_raw = keep.tile([P, PACK, N], F32, name="w2_raw")
         gate_last = keep.tile([P, V], F32, name="gate_last")
-        nc.sync.dma_start(w1_raw[0][:], w1_rows[:, :, 0:256])
-        for j in range(4):
+        nc.sync.dma_start(w1_raw[0][:], w1_rows[:, :, span(0, HALF)])
+        offs_t = load_list(offs, "offs_t")
+        for j in range(PACK):
             nc.sync.dma_start(x_plane[j][:], x_rows[j])
         cell_t = load_list(cell, "cell_t")
-        nc.sync.dma_start(w1_raw[1][:], w1_rows[:, :, 256:512])
-        for k in (0, 1, 3, 2):
-            nc.sync.dma_start(emb_t[k][:], emb_rows[k % 2, k // 2])
-            if k == 1:
-                nc.sync.dma_start(gate_rows[0:D, :], gate[:, 0, :])
-        nc.sync.dma_start(w2_raw[:], w2.rearrange("(p j) c -> p j c", j=4))
+        nc.sync.dma_start(w1_raw[1][:], w1_rows[:, :, span(1, HALF)])
+        nc.sync.dma_start(gate_rows[0:D, :], gate[:, 0, :])
+        for t, (u, f) in enumerate(ROW_TILES):
+            if t == 3:
+                nc.sync.dma_start(w2_raw[:], w2.rearrange("(p j) c -> p j c", j=PACK))
+            nc.sync.dma_start(emb_t[t][:], emb_rows[f, u])
         pos_t = [load_list(src, "pos_t%d" % d) for d, src in enumerate((pos1, pos2, pos3, pos4))]
         nc.sync.dma_start(gate_last[:], gate[D - 1])
 
-        w1_bf = [keep.tile([P, 256, 4], BF16, name="w1_bf%d" % f, align_bytes=64) for f in range(2)]
-        w1_codes = [keep.tile([P, 256], U32, name="w1_codes%d" % f, align_bytes=64) for f in range(2)]
-        w1_scales = [keep.tile([P, 256], U8, name="w1_scales%d" % f, align_bytes=64) for f in range(2)]
+        w1_bf = [keep.tile([P, HALF, PACK], BF16, name="w1_bf%d" % f, align_bytes=64) for f in range(2)]
+        w1_codes = [keep.tile([P, HALF], U32, name="w1_codes%d" % f, align_bytes=64) for f in range(2)]
+        w1_scales = [keep.tile([P, HALF], U8, name="w1_scales%d" % f, align_bytes=64) for f in range(2)]
 
         def prepare_w1(f):
             nc.scalar.copy(
-                w1_bf[f][:].rearrange("p (a r) j -> p a r j", a=2),
-                w1_raw[f][:].rearrange("p j (r a) -> p a r j", a=2),
+                w1_bf[f][:].rearrange("p (u s e) j -> p s j e u", u=2, e=2),
+                w1_raw[f][:].rearrange("p j (s e u) -> p s j e u", u=2, e=2),
             )
-            quantize(w1_codes[f][:], w1_scales[f][:], w1_bf[f][:].rearrange("p c j -> p (c j)"))
+            quantize(w1_codes[f][:], w1_scales[f][:], w1_bf[f][:])
 
         prepare_w1(0)
 
-        x_bf = keep.tile([P, S, 4], BF16, name="x_bf", align_bytes=64)
+        x_bf = keep.tile([P, S, PACK], BF16, name="x_bf", align_bytes=64)
         x_codes = keep.tile([P, S], U32, name="x_codes", align_bytes=64)
         x_scales = keep.tile([P, S], U8, name="x_scales", align_bytes=64)
-        halves = [slice(0, 256), slice(256, 512)]
-        list_halves = [slice(0, 16), slice(16, 32)]
-        h_first = []
-        for j in range(3):
+        halves = [span(c, HALF) for c in range(2)]
+        list_halves = [span(c, HALF // STRIPE) for c in range(2)]
+        for j in range(PACK - 1):
             nc.vector.tensor_copy(x_bf[:, :, j], x_plane[j][:].indirect(offs_t[:]))
-        for j in range(3, 4):
-            for s in range(2):
-                c0, c1 = ((0, 16), (14, 32))[s]
-                nc.vector.tensor_copy(x_bf[:, 16 * c0:16 * c1, j], x_plane[j][:].indirect(offs_t[:, c0:c1]))
-                if j == 3:
-                    quantize(x_codes[:, halves[s]], x_scales[:, halves[s]],
-                             x_bf[:, halves[s], :].rearrange("p c j -> p (c j)"))
-                    acc = bank(4 + s, "h_first_ps%d" % s)
-                    product(acc[:, 0:256], w1_codes[0][:, 0:P], w1_scales[0][:, 0:P],
-                            x_codes[:, halves[s]], x_scales[:, halves[s]])
-                    if s == 1:
-                        prepare_w1(1)
-                    h_first.append(keep.tile([P, 256], F32, name="h_first%d" % s, tag=("h_first0", "w1_raw1")[s]))
-                    nc.scalar.activation(h_first[s][:], acc[:, 0:256], RELU)
+        last_plane_columns = [(0, HALF // STRIPE), (HALF // STRIPE - 2, S // STRIPE)]
+        h_first = []
+        for c, (c0, c1) in enumerate(last_plane_columns):
+            nc.vector.tensor_copy(x_bf[:, STRIPE * c0:STRIPE * c1, PACK - 1],
+                                  x_plane[PACK - 1][:].indirect(offs_t[:, c0:c1]))
+            quantize(x_codes[:, halves[c]], x_scales[:, halves[c]], x_bf[:, halves[c], :])
+            acc = bank(2 + c, "h_first_ps%d" % c)
+            product(acc[:, 0:HALF], w1_codes[0][:, 0:P], w1_scales[0][:, 0:P],
+                    x_codes[:, halves[c]], x_scales[:, halves[c]])
+            if c == 1:
+                prepare_w1(1)
+            h_first.append(keep.tile([P, HALF], F32, name="h_first%d" % c, tag=("h_first0", "w1_raw1")[c]))
+            nc.scalar.activation(h_first[c][:], acc[:, 0:HALF], RELU)
 
-        h = [None]
+        h = {}
 
-        def first_product(k):
-            a, f = divmod(k, 2)
-            acc = bank(6, "h_ps%d" % k)
-            product(acc[:], w1_codes[f][:, a * P:(a + 1) * P], w1_scales[f][:, a * P:(a + 1) * P],
-                    x_codes[:], x_scales[:])
-            h.append(keep.tile([P, S], F32, name="h%d" % k, tag="h%d" % k, align_bytes=64))
-            nc.scalar.activation(h[k][:], acc[:], RELU)
+        def first_product(t):
+            u, f = ROW_TILES[t]
+            acc = bank(3 - t % 2, "h_ps%d" % t)
+            product(acc[:], w1_codes[f][:, span(u, P)], w1_scales[f][:, span(u, P)], x_codes[:], x_scales[:])
+            h[t] = keep.tile([P, S], F32, name="h%d" % t, tag="h%d" % t, align_bytes=64)
+            nc.scalar.activation(h[t][:], acc[:], RELU)
 
-        for s in range(2):
-            nc.vector.tensor_copy(up[0][:].indirect(cell_t[:, list_halves[s]]), h_first[s][:])
+        for c in range(2):
+            nc.vector.tensor_copy(up[0][:].indirect(cell_t[:, list_halves[c]]), h_first[c][:])
         first_product(1)
         nc.vector.tensor_copy(up[1][:].indirect(cell_t[:]), h[1][:])
         first_product(2)
-        w2_bf = keep.tile([P, N, 4], BF16, name="w2_bf", align_bytes=64)
+        w2_bf = keep.tile([P, N, PACK], BF16, name="w2_bf", align_bytes=64)
         nc.scalar.copy(
             w2_bf[:].rearrange("p m (u e) -> p m u e", u=2),
             w2_raw[:].rearrange("p (e u) m -> p m u e", u=2),
@@ -139,104 +152,92 @@ def tile_picked_devox_none_e_kernel(
         first_product(3)
         nc.vector.tensor_copy(up[2][:].indirect(cell_t[:]), h[2][:])
         nc.vector.tensor_copy(up[3][:].indirect(cell_t[:]), h[3][:])
-
         w2_codes = keep.tile([P, N], U32, name="w2_codes", tag="h3", align_bytes=64)
         w2_scales = keep.tile([P, N], U8, name="w2_scales", align_bytes=64)
-        quantize(w2_codes[:], w2_scales[:], w2_bf[:].rearrange("p m j -> p (m j)"))
+        quantize(w2_codes[:], w2_scales[:], w2_bf[:])
 
-        zT = [[keep.tile([P, 2, 256], BF16, name="zT%d_%d" % (u, q)) for q in range(4)] for u in range(2)]
+        zT = [[keep.tile([P, 2, HALF], BF16, name="zT%d_%d" % (u, q)) for q in range(4)] for u in range(2)]
         sums = {}
 
-        def open_sums(k, banks):
-            per = 4 // len(banks)
-            sums[k] = [(banks[q // per], (q % per) * 256, q % per == 0, q % per == per - 1) for q in range(4)]
+        def place_sums(t, banks):
+            per_bank = 4 // len(banks)
+            sums[t] = [(banks[q // per_bank], (q % per_bank) * HALF, q % per_bank == 0, q % per_bank == per_bank - 1)
+                       for q in range(4)]
 
-        def emb_turn(k, quarters):
-            for q in quarters:
-                acc, col, first, last = sums[k][q]
-                for b in range(2):
-                    cells = slice((2 * q + b) * P, (2 * q + b + 1) * P)
-                    turn(acc[:, col + b * P:col + (b + 1) * P], emb_t[k][:, cells], first and b == 0, False)
-
-        def up_turn(k):
-            a, f = divmod(k, 2)
-            ready = []
+        def turn_emb(t):
             for q in range(4):
-                acc, col, first, last = sums[k][q]
+                acc, col, opens, closes = sums[t][q]
                 for b in range(2):
-                    cells = slice((2 * q + b) * P, (2 * q + b + 1) * P)
-                    turn(acc[:, col + b * P:col + (b + 1) * P], up[k][:, cells], False, last and b == 1)
-                ready.append(q)
-                if last:
-                    for r in ready:
-                        dst = zT[a][r][:, :, f * P:(f + 1) * P]
-                        src = acc[:, sums[k][r][1]:sums[k][r][1] + 256].rearrange("p (b r) -> p b r", b=2)
-                        if k == 3 and r % 2 == 1:
-                            nc.vector.tensor_copy(dst, src)
-                        else:
-                            nc.scalar.copy(dst, src)
-                    ready = []
+                    turn(acc[:, col + b * P:col + (b + 1) * P], emb_t[t][:, span(2 * q + b, P)], opens and b == 0, False)
 
-        def back_turn(u, q):
+        def turn_up(t):
+            u, f = ROW_TILES[t]
+            summed = []
+            for q in range(4):
+                acc, col, opens, closes = sums[t][q]
+                for b in range(2):
+                    turn(acc[:, col + b * P:col + (b + 1) * P], up[t][:, span(2 * q + b, P)], False, closes and b == 1)
+                summed.append(q)
+                if closes:
+                    for done in summed:
+                        first = sums[t][done][1]
+                        copy_on("vector" if t == 3 and done % 2 == 1 else "scalar",
+                                zT[u][done][:, :, span(f, P)],
+                                acc[:, first:first + HALF].rearrange("p (b r) -> p b r", b=2))
+                    summed = []
+
+        def turn_back(u, q):
             words = zT[u][q][:].rearrange("p b r -> p (b r)").bitcast(F32)
             for b in range(2):
-                dst = back[q][:, u * 256 + b * P:u * 256 + (b + 1) * P]
-                turn(dst, words[:, b * P:(b + 1) * P], True, True)
+                turn(back[q][:, span(2 * u + b, P)], words[:, span(b, P)], True, True)
 
-        open_sums(0, [bank(0, "sum0_0"), bank(1, "sum0_1")])
-        emb_turn(0, range(4))
-        open_sums(1, [bank(4, "sum1_0"), bank(5, "sum1_1")])
-        emb_turn(1, range(4))
-        gate_ps = bank(7, "gate_ps")
+        gate_ps = bank(2, "gate_ps")
         for b in range(4):
-            turn(gate_ps[:, b * P:(b + 1) * P], gate_rows[:, b * P:(b + 1) * P], True, True)
+            turn(gate_ps[:, span(b, P)], gate_rows[:, span(b, P)], True, True)
         gate_cols = keep.tile([P, 4, D], F32, name="gate_cols")
         nc.scalar.copy(gate_cols[:], gate_ps[:].rearrange("p (b r) -> p b r", b=4)[:, :, 0:D])
-        late = [bank(2, "sum3_2"), bank(3, "sum3_3")]
-        up_turn(0)
-        open_sums(3, [bank(0, "sum3_0"), bank(1, "sum3_1")] + late)
-        emb_turn(3, (2, 3, 0, 1))
-        up_turn(1)
+
         back = [bank(4 + q, "back%d" % q) for q in range(4)]
+        place_sums(0, [bank(0, "sum0_0"), bank(1, "sum0_1")])
+        sums[1] = [(back[q], HALF, True, True) for q in range(4)]
+        place_sums(2, [bank(2, "sum2_0"), bank(3, "sum2_1")])
+        for t in range(3):
+            turn_emb(t)
+        turn_up(0)
+        turn_up(1)
         for q in range(4):
-            back_turn(0, q)
-        sums[2] = [(back[q], 256, True, True) for q in range(4)]
-        emb_turn(2, range(4))
-        up_turn(2)
+            turn_back(0, q)
+        sums[3] = [(bank(q, "sum3_%d" % q), 0, True, True) for q in range(2)] + sums[1][2:]
+        turn_emb(3)
+        turn_up(2)
 
         y = [keep.tile([P, U], F32, name="y%d" % n) for n in range(2)]
-        z_bf = [keep.tile([P, 256, 4], BF16, name="z_bf%d" % q, align_bytes=64) for q in range(4)]
-        z_codes = [keep.tile([P, 256], U32, name="z_codes%d" % q, align_bytes=64) for q in range(4)]
-        z_scales = [keep.tile([P, 256], U8, name="z_scales%d" % q, align_bytes=64) for q in range(4)]
-        up_turn(3)
+        z_bf = [keep.tile([P, HALF, PACK], BF16, name="z_bf%d" % q, align_bytes=64) for q in range(4)]
+        z_codes = [keep.tile([P, HALF], U32, name="z_codes%d" % q, align_bytes=64) for q in range(4)]
+        z_scales = [keep.tile([P, HALF], U8, name="z_scales%d" % q, align_bytes=64) for q in range(4)]
+        turn_up(3)
         for q in range(4):
-            back_turn(1, q)
-            dst = z_bf[q][:].rearrange("p c j -> p (c j)").bitcast(F32).rearrange("p (c u) -> p c u", u=2)
-            src = back[q][:].rearrange("p (u c) -> p c u", u=2)
-            if q == 1:
-                nc.vector.tensor_copy(dst, src)
-            else:
-                nc.scalar.copy(dst, src)
+            turn_back(1, q)
+            copy_on("vector" if q == 1 else "scalar",
+                    z_bf[q][:].rearrange("p c j -> p (c j)").bitcast(F32).rearrange("p (c u) -> p c u", u=2),
+                    back[q][:].rearrange("p (u c) -> p c u", u=2))
+
         for q in range(4):
-            quantize(z_codes[q][:], z_scales[q][:], z_bf[q][:].rearrange("p c j -> p (c j)"))
+            quantize(z_codes[q][:], z_scales[q][:], z_bf[q][:])
             acc = bank(q, "y0_ps%d" % q)
-            product(acc[:, 0:256], w2_codes[:, 0:P], w2_scales[:, 0:P], z_codes[q][:], z_scales[q][:])
-            if q == 2:
-                nc.vector.tensor_copy(y[0][:, q * 256:(q + 1) * 256], acc[:, 0:256])
-            else:
-                nc.scalar.copy(y[0][:, q * 256:(q + 1) * 256], acc[:, 0:256])
+            product(acc[:, 0:HALF], w2_codes[:, 0:P], w2_scales[:, 0:P], z_codes[q][:], z_scales[q][:])
+            copy_on("vector" if q == 2 else "scalar", y[0][:, span(q, HALF)], acc[:, 0:HALF])
         for c in range(2):
             acc = bank(3 - c, "y1_ps%d" % c)
             for b in range(2):
                 q = 2 * c + b
-                product(acc[:, b * 256:(b + 1) * 256], w2_codes[:, P:N], w2_scales[:, P:N],
-                        z_codes[q][:], z_scales[q][:])
-            nc.scalar.copy(y[1][:, c * 512:(c + 1) * 512], acc[:])
+                product(acc[:, span(b, HALF)], w2_codes[:, P:N], w2_scales[:, P:N], z_codes[q][:], z_scales[q][:])
+            nc.scalar.copy(y[1][:, span(c, BANK)], acc[:])
 
         total0 = bank(7, "total0")
         total1 = [bank(5 + c, "total1_%d" % c) for c in range(2)]
         steps = [(n, d) for n in range(2) for d in range(D)][:-1]
-        scaled = {}
+        gated = {}
 
         def fetch(i):
             n, d = steps[i]
@@ -244,28 +245,25 @@ def tile_picked_devox_none_e_kernel(
             in_halves = i == len(steps) - 1
             if not in_halves:
                 nc.vector.tensor_copy(got[:], y[n][:].indirect(pos_t[d][:]))
-            scaled[i] = ring.tile([P, V], F32, name="scaled")
+            gated[i] = ring.tile([P, V], F32, name="gated")
             for c in range(2):
                 if in_halves:
                     nc.vector.tensor_copy(got[:, halves[c]], y[n][:].indirect(pos_t[d][:, list_halves[c]]))
                 turned = bank((2 * i + c + 4) % 5, "turned%d_%d" % (i, c))
                 for b in range(2):
-                    v0 = (2 * c + b) * P
-                    turn(turned[:, b * P:(b + 1) * P], got[:, v0:v0 + P], True, True)
+                    turn(turned[:, span(b, P)], got[:, span(2 * c + b, P)], True, True)
                 for b in range(2):
-                    v0 = (2 * c + b) * P
-                    nc.scalar.activation(scaled[i][:, v0:v0 + P], turned[:, b * P:(b + 1) * P], COPY,
+                    nc.scalar.activation(gated[i][:, span(2 * c + b, P)], turned[:, span(b, P)], COPY,
                                          scale=gate_cols[:, 2 * c + b, d:d + 1])
 
         def add_up(i):
             n, d = steps[i]
             for b in range(4):
-                src = scaled[i][:, b * P:(b + 1) * P]
+                src = gated[i][:, span(b, P)]
                 if n == 0:
-                    turn(total0[:, b * P:(b + 1) * P], src, d == 0 and b == 0, d == D - 1 and b == 3)
+                    turn(total0[:, span(b, P)], src, d == 0 and b == 0, d == D - 1 and b == 3)
                 else:
-                    turn(total1[b // 2][:, (b % 2) * P:(b % 2 + 1) * P], src,
-                         d == 0 and b % 2 == 0, d == D - 2 and b % 2 == 1)
+                    turn(total1[b // 2][:, span(b % 2, P)], src, d == 0 and b % 2 == 0, d == D - 2 and b % 2 == 1)
             if n == 0 and d == D - 1:
                 res0 = keep.tile([P, V], F32, name="res0")
                 nc.scalar.copy(res0[:], total0[:])
@@ -278,10 +276,10 @@ def tile_picked_devox_none_e_kernel(
         add_up(len(steps) - 1)
         last_term = []
         for c in range(2):
-            last_term.append(keep.tile([P, 256], F32, name="last_term%d" % c))
+            last_term.append(keep.tile([P, HALF], F32, name="last_term%d" % c))
             nc.vector.tensor_tensor(last_term[c][:], y[1][:].indirect(pos_t[D - 1][:, list_halves[c]]),
                                     gate_last[:, halves[c]], MULT)
         for c in range(2):
-            res1 = keep.tile([P, 256], F32, name="res1_%d" % c)
-            nc.vector.tensor_tensor(res1[:], total1[c][:, 0:256], last_term[c][:], ADD)
+            res1 = keep.tile([P, HALF], F32, name="res1_%d" % c)
+            nc.vector.tensor_tensor(res1[:], total1[c][:, 0:HALF], last_term[c][:], ADD)
             nc.sync.dma_start(out[P:N, halves[c]], res1[:])

@@ -11,7 +11,6 @@ PACK = 4
 HALF = 256
 BANK = 512
 STRIPE = 16
-ROW_TILES = ((0, 0), (0, 1), (1, 1), (1, 0))
 
 F32 = mybir.dt.float32
 BF16 = mybir.dt.bfloat16
@@ -36,7 +35,6 @@ def tile_picked_devox_none_e_kernel(
     with ExitStack() as ctx:
         lists = ctx.enter_context(tc.tile_pool(name="lists", bufs=1))
         keep = ctx.enter_context(tc.tile_pool(name="keep", bufs=1))
-        ring = ctx.enter_context(tc.tile_pool(name="ring", bufs=3))
         psum = ctx.enter_context(tc.psum_pool(name="psum", bufs=1))
 
         def bank(b, name):
@@ -76,210 +74,168 @@ def tile_picked_devox_none_e_kernel(
 
         x_rows = xT.rearrange("(p j) c -> j p c", j=PACK)
         w1_rows = w1.rearrange("(p j) c -> p j c", j=PACK)
-        emb_rows = emb.rearrange("(f r u) c -> f u r c", f=2, u=2)
+        emb_rows = emb.rearrange("(f r u) c -> f r u c", f=2, u=2)
         w1_raw = [keep.tile([P, PACK, HALF], F32, name="w1_raw%d" % f) for f in range(2)]
         x_plane = [keep.tile([P, T], F32, name="x_plane%d" % j) for j in range(PACK)]
-        emb_t = [keep.tile([P, U], F32, name="emb_t%d" % t) for t in range(4)]
+        emb_t = [keep.tile([P, 2, U], F32, name="emb_t%d" % f) for f in range(2)]
         w2_raw = keep.tile([P, PACK, N], F32, name="w2_raw")
-        gate_last = keep.tile([P, V], F32, name="gate_last")
-        nc.sync.dma_start(w1_raw[0][:], w1_rows[:, :, span(0, HALF)])
+        gate_t = keep.tile([P, D, V], F32, name="gate_t")
+        nc.sync.dma_start(x_plane[0][:], x_rows[0])
         offs_t = load_list(offs, "offs_t")
-        for j in range(PACK):
-            nc.sync.dma_start(x_plane[j][:], x_rows[j])
+        nc.sync.dma_start(x_plane[1][:], x_rows[1])
         cell_t = load_list(cell, "cell_t")
-        nc.sync.dma_start(w1_raw[1][:], w1_rows[:, :, span(1, HALF)])
+        for j in range(2, PACK):
+            nc.sync.dma_start(x_plane[j][:], x_rows[j])
+        for f in range(2):
+            nc.sync.dma_start(w1_raw[f][:], w1_rows[:, :, span(f, HALF)])
         nc.sync.dma_start(gate_rows[0:D, :], gate[:, 0, :])
-        for t, (u, f) in enumerate(ROW_TILES):
-            if t == 3:
-                nc.sync.dma_start(w2_raw[:], w2.rearrange("(p j) c -> p j c", j=PACK))
-            nc.sync.dma_start(emb_t[t][:], emb_rows[f, u])
+        for f in range(2):
+            nc.sync.dma_start(emb_t[f][:], emb_rows[f])
+        nc.sync.dma_start(w2_raw[:], w2.rearrange("(p j) c -> p j c", j=PACK))
         pos_t = [load_list(src, "pos_t%d" % d) for d, src in enumerate((pos1, pos2, pos3, pos4))]
-        nc.sync.dma_start(gate_last[:], gate[D - 1])
-
-        w1_bf = [keep.tile([P, HALF, PACK], BF16, name="w1_bf%d" % f, align_bytes=64) for f in range(2)]
-        w1_codes = [keep.tile([P, HALF], U32, name="w1_codes%d" % f, align_bytes=64) for f in range(2)]
-        w1_scales = [keep.tile([P, HALF], U8, name="w1_scales%d" % f, align_bytes=64) for f in range(2)]
-
-        def prepare_w1(f):
-            nc.scalar.copy(
-                w1_bf[f][:].rearrange("p (u s e) j -> p s j e u", u=2, e=2),
-                w1_raw[f][:].rearrange("p j (s e u) -> p s j e u", u=2, e=2),
-            )
-            quantize(w1_codes[f][:], w1_scales[f][:], w1_bf[f][:])
-
-        prepare_w1(0)
+        nc.sync.dma_start(gate_t[:], gate.rearrange("d p v -> p d v"))
 
         x_bf = keep.tile([P, S, PACK], BF16, name="x_bf", align_bytes=64)
         x_codes = keep.tile([P, S], U32, name="x_codes", align_bytes=64)
         x_scales = keep.tile([P, S], U8, name="x_scales", align_bytes=64)
         halves = [span(c, HALF) for c in range(2)]
         list_halves = [span(c, HALF // STRIPE) for c in range(2)]
-        for j in range(PACK - 1):
+        for j in range(PACK):
             nc.vector.tensor_copy(x_bf[:, :, j], x_plane[j][:].indirect(offs_t[:]))
-        last_plane_columns = [(0, HALF // STRIPE), (HALF // STRIPE - 2, S // STRIPE)]
-        h_first = []
-        for c, (c0, c1) in enumerate(last_plane_columns):
-            nc.vector.tensor_copy(x_bf[:, STRIPE * c0:STRIPE * c1, PACK - 1],
-                                  x_plane[PACK - 1][:].indirect(offs_t[:, c0:c1]))
-            quantize(x_codes[:, halves[c]], x_scales[:, halves[c]], x_bf[:, halves[c], :])
-            acc = bank(2 + c, "h_first_ps%d" % c)
-            product(acc[:, 0:HALF], w1_codes[0][:, 0:P], w1_scales[0][:, 0:P],
-                    x_codes[:, halves[c]], x_scales[:, halves[c]])
-            if c == 1:
-                prepare_w1(1)
-            h_first.append(keep.tile([P, HALF], F32, name="h_first%d" % c, tag=("h_first0", "w1_raw1")[c]))
-            nc.scalar.activation(h_first[c][:], acc[:, 0:HALF], RELU)
+        quantize(x_codes[:], x_scales[:], x_bf[:])
 
-        h = {}
+        w1_bf = [keep.tile([P, HALF, PACK], BF16, name="w1_bf%d" % f, align_bytes=64) for f in range(2)]
+        w1_codes = [keep.tile([P, HALF], U32, name="w1_codes%d" % f, align_bytes=64) for f in range(2)]
+        w1_scales = [keep.tile([P, HALF], U8, name="w1_scales%d" % f, align_bytes=64) for f in range(2)]
+        for f in range(2):
+            nc.scalar.copy(
+                w1_bf[f][:].rearrange("p (u s e) j -> p s j e u", u=2, e=2),
+                w1_raw[f][:].rearrange("p j (s e u) -> p s j e u", u=2, e=2),
+            )
 
-        def first_product(t):
-            u, f = ROW_TILES[t]
-            acc = bank(3 - t % 2, "h_ps%d" % t)
+        def first_product(f, u):
+            acc = bank(u, "h_ps%d_%d" % (f, u))
             product(acc[:], w1_codes[f][:, span(u, P)], w1_scales[f][:, span(u, P)], x_codes[:], x_scales[:])
-            h[t] = keep.tile([P, S], F32, name="h%d" % t, tag="h%d" % t, align_bytes=64)
-            nc.scalar.activation(h[t][:], acc[:], RELU)
+            h = keep.tile([P, S], F32, name="h%d_%d" % (f, u), tag="h%d" % u)
+            if u == 0:
+                nc.scalar.activation(h[:], acc[:], RELU)
+            else:
+                nc.vector.tensor_scalar_max(h[:], acc[:], 0.0)
+            return h
 
-        for c in range(2):
-            nc.vector.tensor_copy(up[0][:].indirect(cell_t[:, list_halves[c]]), h_first[c][:])
-        first_product(1)
-        nc.vector.tensor_copy(up[1][:].indirect(cell_t[:]), h[1][:])
-        first_product(2)
-        w2_bf = keep.tile([P, N, PACK], BF16, name="w2_bf", align_bytes=64)
-        nc.scalar.copy(
-            w2_bf[:].rearrange("p m (u e) -> p m u e", u=2),
-            w2_raw[:].rearrange("p (e u) m -> p m u e", u=2),
-        )
-        first_product(3)
-        nc.vector.tensor_copy(up[2][:].indirect(cell_t[:]), h[2][:])
-        nc.vector.tensor_copy(up[3][:].indirect(cell_t[:]), h[3][:])
-        w2_codes = keep.tile([P, N], U32, name="w2_codes", tag="h3", align_bytes=64)
-        w2_scales = keep.tile([P, N], U8, name="w2_scales", align_bytes=64)
-        quantize(w2_codes[:], w2_scales[:], w2_bf[:])
+        def scatter(f, u, h):
+            if u == 0:
+                for c in range(2):
+                    nc.scalar.activation(up[2 * f][:].indirect(cell_t[:, list_halves[c]]), h[:, halves[c]], COPY)
+            else:
+                nc.vector.tensor_copy(up[2 * f + 1][:].indirect(cell_t[:]), h[:])
 
-        zT = [[keep.tile([P, 2, HALF], BF16, name="zT%d_%d" % (u, q)) for q in range(4)] for u in range(2)]
-        sums = {}
+        quantize(w1_codes[0][:], w1_scales[0][:], w1_bf[0][:])
+        h_first = [first_product(0, u) for u in range(2)]
+        quantize(w1_codes[1][:], w1_scales[1][:], w1_bf[1][:])
+        for u in range(2):
+            scatter(0, u, h_first[u])
+        for u in range(2):
+            scatter(1, u, first_product(1, u))
 
-        def place_sums(t, banks):
-            per_bank = 4 // len(banks)
-            sums[t] = [(banks[q // per_bank], (q % per_bank) * HALF, q % per_bank == 0, q % per_bank == per_bank - 1)
-                       for q in range(4)]
-
-        def turn_emb(t):
-            for q in range(4):
-                acc, col, opens, closes = sums[t][q]
-                for b in range(2):
-                    turn(acc[:, col + b * P:col + (b + 1) * P], emb_t[t][:, span(2 * q + b, P)], opens and b == 0, False)
-
-        def turn_up(t):
-            u, f = ROW_TILES[t]
-            summed = []
-            for q in range(4):
-                acc, col, opens, closes = sums[t][q]
-                for b in range(2):
-                    turn(acc[:, col + b * P:col + (b + 1) * P], up[t][:, span(2 * q + b, P)], False, closes and b == 1)
-                summed.append(q)
-                if closes:
-                    for done in summed:
-                        first = sums[t][done][1]
-                        copy_on("vector" if t == 3 and done % 2 == 1 else "scalar",
-                                zT[u][done][:, :, span(f, P)],
-                                acc[:, first:first + HALF].rearrange("p (b r) -> p b r", b=2))
-                    summed = []
-
-        def turn_back(u, q):
-            words = zT[u][q][:].rearrange("p b r -> p (b r)").bitcast(F32)
-            for b in range(2):
-                turn(back[q][:, span(2 * u + b, P)], words[:, span(b, P)], True, True)
-
-        gate_ps = bank(2, "gate_ps")
+        gate_ps = bank(7, "gate_ps")
         for b in range(4):
             turn(gate_ps[:, span(b, P)], gate_rows[:, span(b, P)], True, True)
         gate_cols = keep.tile([P, 4, D], F32, name="gate_cols")
         nc.scalar.copy(gate_cols[:], gate_ps[:].rearrange("p (b r) -> p b r", b=4)[:, :, 0:D])
 
-        back = [bank(4 + q, "back%d" % q) for q in range(4)]
-        place_sums(0, [bank(0, "sum0_0"), bank(1, "sum0_1")])
-        sums[1] = [(back[q], HALF, True, True) for q in range(4)]
-        place_sums(2, [bank(2, "sum2_0"), bank(3, "sum2_1")])
-        for t in range(3):
-            turn_emb(t)
-        turn_up(0)
-        turn_up(1)
-        for q in range(4):
-            turn_back(0, q)
-        sums[3] = [(bank(q, "sum3_%d" % q), 0, True, True) for q in range(2)] + sums[1][2:]
+        zT = [[keep.tile([P, 4, HALF], BF16, name="zT%d_%d" % (u, c)) for c in range(2)] for u in range(2)]
+        sums = {}
+
+        def turn_emb(t):
+            sums[t] = [bank((2 + 2 * t + c) % 8, "sum%d_%d" % (t, c)) for c in range(2)]
+            for c in range(2):
+                for b in range(4):
+                    turn(sums[t][c][:, span(b, P)], emb_t[t // 2][:, t % 2, span(4 * c + b, P)], b == 0, False)
+
+        def turn_up(t, c, engine):
+            for b in range(4):
+                turn(sums[t][c][:, span(b, P)], up[t][:, span(4 * c + b, P)], False, b == 3)
+            copy_on(engine, zT[t % 2][c][:, :, span(t // 2, P)], sums[t][c][:].rearrange("p (b r) -> p b r", b=4))
+
+        turn_emb(0)
+        turn_emb(1)
+        for c in range(2):
+            turn_up(0, c, "scalar")
+            turn_up(1, c, "vector")
+        w2_bf = keep.tile([P, N, PACK], BF16, name="w2_bf", align_bytes=64)
+        nc.vector.tensor_copy(
+            w2_bf[:].rearrange("p m (u e) -> p m u e", u=2),
+            w2_raw[:].rearrange("p (e u) m -> p m u e", u=2),
+        )
+        w2_codes = keep.tile([P, N], U32, name="w2_codes", align_bytes=64)
+        w2_scales = keep.tile([P, N], U8, name="w2_scales", align_bytes=64)
+        quantize(w2_codes[:], w2_scales[:], w2_bf[:])
+        turn_emb(2)
         turn_emb(3)
-        turn_up(2)
+        turn_up(2, 0, "scalar")
+        turn_up(3, 0, "scalar")
+        turn_up(2, 1, "scalar")
+        turn_up(3, 1, "vector")
 
         y = [keep.tile([P, U], F32, name="y%d" % n) for n in range(2)]
         z_bf = [keep.tile([P, HALF, PACK], BF16, name="z_bf%d" % q, align_bytes=64) for q in range(4)]
         z_codes = [keep.tile([P, HALF], U32, name="z_codes%d" % q, align_bytes=64) for q in range(4)]
         z_scales = [keep.tile([P, HALF], U8, name="z_scales%d" % q, align_bytes=64) for q in range(4)]
-        turn_up(3)
+        y_ps = []
         for q in range(4):
-            turn_back(1, q)
+            back = bank(2 + q, "back%d" % q)
+            for u in range(2):
+                words = zT[u][q // 2][:].rearrange("p b r -> p (b r)").bitcast(F32)
+                for b in range(2):
+                    turn(back[:, span(2 * u + b, P)], words[:, span(2 * (q % 2) + b, P)], True, True)
             copy_on("vector" if q == 1 else "scalar",
                     z_bf[q][:].rearrange("p c j -> p (c j)").bitcast(F32).rearrange("p (c u) -> p c u", u=2),
-                    back[q][:].rearrange("p (u c) -> p c u", u=2))
-
-        for q in range(4):
+                    back[:].rearrange("p (u c) -> p c u", u=2))
             quantize(z_codes[q][:], z_scales[q][:], z_bf[q][:])
-            acc = bank(q, "y0_ps%d" % q)
-            product(acc[:, 0:HALF], w2_codes[:, 0:P], w2_scales[:, 0:P], z_codes[q][:], z_scales[q][:])
-            copy_on("vector" if q == 2 else "scalar", y[0][:, span(q, HALF)], acc[:, 0:HALF])
-        for c in range(2):
-            acc = bank(3 - c, "y1_ps%d" % c)
-            for b in range(2):
-                q = 2 * c + b
-                product(acc[:, span(b, HALF)], w2_codes[:, P:N], w2_scales[:, P:N], z_codes[q][:], z_scales[q][:])
-            nc.scalar.copy(y[1][:, span(c, BANK)], acc[:])
+            y_ps.append(bank((6 + q) % 8, "y_ps%d" % q))
+            for n in range(2):
+                product(y_ps[q][:, span(n, HALF)], w2_codes[:, span(n, P)], w2_scales[:, span(n, P)],
+                        z_codes[q][:], z_scales[q][:])
+            for n in range(2):
+                copy_on("scalar" if n == 0 else "vector", y[n][:, span(q, HALF)], y_ps[q][:, span(n, HALF)])
 
-        total0 = bank(7, "total0")
-        total1 = [bank(5 + c, "total1_%d" % c) for c in range(2)]
-        steps = [(n, d) for n in range(2) for d in range(D)][:-1]
-        gated = {}
-
-        def fetch(i):
-            n, d = steps[i]
-            got = keep.tile([P, V], F32, name="got%d" % i, tag="got%d" % i)
-            in_halves = i == len(steps) - 1
-            if not in_halves:
-                nc.vector.tensor_copy(got[:], y[n][:].indirect(pos_t[d][:]))
-            gated[i] = ring.tile([P, V], F32, name="gated")
-            for c in range(2):
-                if in_halves:
-                    nc.vector.tensor_copy(got[:, halves[c]], y[n][:].indirect(pos_t[d][:, list_halves[c]]))
-                turned = bank((2 * i + c + 4) % 5, "turned%d_%d" % (i, c))
-                for b in range(2):
-                    turn(turned[:, span(b, P)], got[:, span(2 * c + b, P)], True, True)
-                for b in range(2):
-                    nc.scalar.activation(gated[i][:, span(2 * c + b, P)], turned[:, span(b, P)], COPY,
-                                         scale=gate_cols[:, 2 * c + b, d:d + 1])
-
-        def add_up(i):
-            n, d = steps[i]
+        total = [bank(6 + c, "total%d" % c) for c in range(2)]
+        for d in range(D):
+            got = keep.tile([P, V], F32, name="got%d" % d)
+            if d == 0:
+                nc.vector.tensor_copy(got[:], y[0][:].indirect(pos_t[d][:]))
+            else:
+                nc.scalar.activation(got[:], y[0][:].indirect(pos_t[d][:]), COPY)
+            turned = bank(2 + d, "turned%d" % d)
             for b in range(4):
-                src = gated[i][:, span(b, P)]
-                if n == 0:
-                    turn(total0[:, span(b, P)], src, d == 0 and b == 0, d == D - 1 and b == 3)
-                else:
-                    turn(total1[b // 2][:, span(b % 2, P)], src, d == 0 and b % 2 == 0, d == D - 2 and b % 2 == 1)
-            if n == 0 and d == D - 1:
-                res0 = keep.tile([P, V], F32, name="res0")
-                nc.scalar.copy(res0[:], total0[:])
-                nc.sync.dma_start(out[0:P, :], res0[:])
-
-        fetch(0)
-        for i in range(1, len(steps)):
-            fetch(i)
-            add_up(i - 1)
-        add_up(len(steps) - 1)
-        last_term = []
+                turn(turned[:, span(b, P)], got[:, span(b, P)], True, True)
+            gated = keep.tile([P, V], F32, name="gated%d" % d)
+            for b in range(4):
+                nc.scalar.activation(gated[:, span(b, P)], turned[:, span(b, P)], COPY, scale=gate_cols[:, b, d:d + 1])
+            for b in range(4):
+                turn(total[b // 2][:, span(b % 2, P)], gated[:, span(b, P)], d == 0 and b % 2 == 0,
+                     d == D - 1 and b % 2 == 1)
         for c in range(2):
-            last_term.append(keep.tile([P, HALF], F32, name="last_term%d" % c))
-            nc.vector.tensor_tensor(last_term[c][:], y[1][:].indirect(pos_t[D - 1][:, list_halves[c]]),
-                                    gate_last[:, halves[c]], MULT)
+            res0 = keep.tile([P, HALF], F32, name="res0_%d" % c)
+            nc.scalar.copy(res0[:], total[c][:, 0:HALF])
+            nc.sync.dma_start(out[0:P, halves[c]], res0[:])
+
+        terms = []
+        for d in range(D - 1):
+            terms.append(keep.tile([P, V], F32, name="term%d" % d))
+            nc.vector.tensor_tensor(terms[d][:], y[1][:].indirect(pos_t[d][:]), gate_t[:, d, :], MULT)
+        part = terms[0]
+        for d in range(1, D - 1):
+            more = keep.tile([P, V], F32, name="part%d" % d)
+            nc.vector.tensor_tensor(more[:], part[:], terms[d][:], ADD)
+            part = more
+        last = []
+        for c in range(2):
+            last.append(keep.tile([P, HALF], F32, name="last%d" % c))
+            nc.vector.tensor_tensor(last[c][:], y[1][:].indirect(pos_t[D - 1][:, list_halves[c]]),
+                                    gate_t[:, D - 1, halves[c]], MULT)
         for c in range(2):
             res1 = keep.tile([P, HALF], F32, name="res1_%d" % c)
-            nc.vector.tensor_tensor(res1[:], total1[c][:, 0:HALF], last_term[c][:], ADD)
+            nc.vector.tensor_tensor(res1[:], part[:, halves[c]], last[c][:], ADD)
             nc.sync.dma_start(out[P:N, halves[c]], res1[:])

@@ -80,63 +80,82 @@ def tile_picked_devox_none_e_kernel(
         emb_t = [keep.tile([P, 2, U], F32, name="emb_t%d" % f) for f in range(2)]
         w2_raw = keep.tile([P, PACK, N], F32, name="w2_raw")
         gate_t = keep.tile([P, D, V], F32, name="gate_t")
+        nc.sync.dma_start(w1_raw[0][:], w1_rows[:, :, span(0, HALF)])
         nc.sync.dma_start(x_plane[0][:], x_rows[0])
         offs_t = load_list(offs, "offs_t")
         nc.sync.dma_start(x_plane[1][:], x_rows[1])
         cell_t = load_list(cell, "cell_t")
         for j in range(2, PACK):
             nc.sync.dma_start(x_plane[j][:], x_rows[j])
-        for f in range(2):
-            nc.sync.dma_start(w1_raw[f][:], w1_rows[:, :, span(f, HALF)])
+        nc.sync.dma_start(w1_raw[1][:], w1_rows[:, :, span(1, HALF)])
         nc.sync.dma_start(gate_rows[0:D, :], gate[:, 0, :])
-        for f in range(2):
-            nc.sync.dma_start(emb_t[f][:], emb_rows[f])
+        nc.sync.dma_start(emb_t[0][:], emb_rows[0])
         nc.sync.dma_start(w2_raw[:], w2.rearrange("(p j) c -> p j c", j=PACK))
+        nc.sync.dma_start(emb_t[1][:], emb_rows[1])
         pos_t = [load_list(src, "pos_t%d" % d) for d, src in enumerate((pos1, pos2, pos3, pos4))]
         nc.sync.dma_start(gate_t[:], gate.rearrange("d p v -> p d v"))
+
+        w1_bf = [keep.tile([P, HALF, PACK], BF16, name="w1_bf%d" % f, align_bytes=64) for f in range(2)]
+        w1_codes = [keep.tile([P, HALF], U32, name="w1_codes%d" % f, align_bytes=64) for f in range(2)]
+        w1_scales = [keep.tile([P, HALF], U8, name="w1_scales%d" % f, align_bytes=64) for f in range(2)]
+
+        def round_w1(f, engine):
+            copy_on(engine,
+                    w1_bf[f][:].rearrange("p (u s e) j -> p s j e u", u=2, e=2),
+                    w1_raw[f][:].rearrange("p j (s e u) -> p s j e u", u=2, e=2))
+
+        round_w1(0, "scalar")
+        quantize(w1_codes[0][:], w1_scales[0][:], w1_bf[0][:])
 
         x_bf = keep.tile([P, S, PACK], BF16, name="x_bf", align_bytes=64)
         x_codes = keep.tile([P, S], U32, name="x_codes", align_bytes=64)
         x_scales = keep.tile([P, S], U8, name="x_scales", align_bytes=64)
         halves = [span(c, HALF) for c in range(2)]
         list_halves = [span(c, HALF // STRIPE) for c in range(2)]
-        for j in range(PACK):
+        for j in range(PACK - 1):
             nc.vector.tensor_copy(x_bf[:, :, j], x_plane[j][:].indirect(offs_t[:]))
-        quantize(x_codes[:], x_scales[:], x_bf[:])
 
-        w1_bf = [keep.tile([P, HALF, PACK], BF16, name="w1_bf%d" % f, align_bytes=64) for f in range(2)]
-        w1_codes = [keep.tile([P, HALF], U32, name="w1_codes%d" % f, align_bytes=64) for f in range(2)]
-        w1_scales = [keep.tile([P, HALF], U8, name="w1_scales%d" % f, align_bytes=64) for f in range(2)]
-        for f in range(2):
-            nc.scalar.copy(
-                w1_bf[f][:].rearrange("p (u s e) j -> p s j e u", u=2, e=2),
-                w1_raw[f][:].rearrange("p j (s e u) -> p s j e u", u=2, e=2),
-            )
+        def gather_last(c0, c1):
+            nc.vector.tensor_copy(x_bf[:, STRIPE * c0:STRIPE * c1, PACK - 1],
+                                  x_plane[PACK - 1][:].indirect(offs_t[:, c0:c1]))
 
-        def first_product(f, u):
-            acc = bank(u, "h_ps%d_%d" % (f, u))
-            product(acc[:], w1_codes[f][:, span(u, P)], w1_scales[f][:, span(u, P)], x_codes[:], x_scales[:])
-            h = keep.tile([P, S], F32, name="h%d_%d" % (f, u), tag="h%d" % u)
-            if u == 0:
-                nc.scalar.activation(h[:], acc[:], RELU)
+        gather_last(0, 16)
+        quantize(x_codes[:, halves[0]], x_scales[:, halves[0]], x_bf[:, halves[0], :])
+        nc.gpsimd.tensor_scalar(
+            w1_bf[1][:].rearrange("p (u r) j -> p u r j", u=2),
+            w1_raw[1][:].rearrange("p j (r u) -> p u r j", u=2), 1.0, 0.0, MULT, ADD)
+        gather_last(14, 32)
+        quantize(x_codes[:, halves[1]], x_scales[:, halves[1]], x_bf[:, halves[1], :])
+        quantize(w1_codes[1][:], w1_scales[1][:], w1_bf[1][:])
+
+        def make_h(f, u, b, entries, engine):
+            width = entries.stop - entries.start
+            name = "h%d_%d_%d" % (f, u, entries.start)
+            acc = bank(b, name + "_ps")
+            product(acc[:, 0:width], w1_codes[f][:, span(u, P)], w1_scales[f][:, span(u, P)],
+                    x_codes[:, entries], x_scales[:, entries])
+            h = keep.tile([P, width], F32, name=name, tag=name, align_bytes=64)
+            if engine == "scalar":
+                nc.scalar.activation(h[:], acc[:, 0:width], RELU)
             else:
-                nc.vector.tensor_scalar_max(h[:], acc[:], 0.0)
+                nc.vector.tensor_scalar_max(h[:], acc[:, 0:width], 0.0)
             return h
 
-        def scatter(f, u, h):
-            if u == 0:
-                for c in range(2):
-                    nc.scalar.activation(up[2 * f][:].indirect(cell_t[:, list_halves[c]]), h[:, halves[c]], COPY)
-            else:
-                nc.vector.tensor_copy(up[2 * f + 1][:].indirect(cell_t[:]), h[:])
+        def scatter_scalar(t, c, src):
+            nc.scalar.activation(up[t][:].indirect(cell_t[:, list_halves[c]]), src, COPY)
 
-        quantize(w1_codes[0][:], w1_scales[0][:], w1_bf[0][:])
-        h_first = [first_product(0, u) for u in range(2)]
-        quantize(w1_codes[1][:], w1_scales[1][:], w1_bf[1][:])
-        for u in range(2):
-            scatter(0, u, h_first[u])
-        for u in range(2):
-            scatter(1, u, first_product(1, u))
+        for c in range(2):
+            h = [make_h(0, u, (u + c) % 2, halves[c], "vector" if u + c == 2 else "scalar") for u in range(2)]
+            scatter_scalar(0, c, h[0][:])
+            nc.vector.tensor_copy(up[1][:].indirect(cell_t[:, list_halves[c]]), h[1][:])
+        h = [make_h(1, u, u, slice(0, S), ("scalar", "vector")[u]) for u in range(2)]
+        w2_bf = keep.tile([P, N, PACK], BF16, name="w2_bf", align_bytes=64)
+        nc.gpsimd.tensor_scalar(
+            w2_bf[:].rearrange("p m (u e) -> p m u e", u=2),
+            w2_raw[:].rearrange("p (e u) m -> p m u e", u=2), 1.0, 0.0, MULT, ADD)
+        for c in range(2):
+            scatter_scalar(2, c, h[0][:, halves[c]])
+        nc.vector.tensor_copy(up[3][:].indirect(cell_t[:]), h[1][:])
 
         gate_ps = bank(7, "gate_ps")
         for b in range(4):
@@ -144,7 +163,8 @@ def tile_picked_devox_none_e_kernel(
         gate_cols = keep.tile([P, 4, D], F32, name="gate_cols")
         nc.scalar.copy(gate_cols[:], gate_ps[:].rearrange("p (b r) -> p b r", b=4)[:, :, 0:D])
 
-        zT = [[keep.tile([P, 4, HALF], BF16, name="zT%d_%d" % (u, c)) for c in range(2)] for u in range(2)]
+        zT = [[keep.tile([P, 4, HALF], BF16, name="zT%d_%d" % (u, c), align_bytes=64,
+                         tag="h1_0_0" if u + c == 0 else "zT%d_%d" % (u, c)) for c in range(2)] for u in range(2)]
         sums = {}
 
         def turn_emb(t):
@@ -158,56 +178,51 @@ def tile_picked_devox_none_e_kernel(
                 turn(sums[t][c][:, span(b, P)], up[t][:, span(4 * c + b, P)], False, b == 3)
             copy_on(engine, zT[t % 2][c][:, :, span(t // 2, P)], sums[t][c][:].rearrange("p (b r) -> p b r", b=4))
 
-        turn_emb(0)
-        turn_emb(1)
-        for c in range(2):
-            turn_up(0, c, "scalar")
-            turn_up(1, c, "vector")
-        w2_bf = keep.tile([P, N, PACK], BF16, name="w2_bf", align_bytes=64)
-        nc.vector.tensor_copy(
-            w2_bf[:].rearrange("p m (u e) -> p m u e", u=2),
-            w2_raw[:].rearrange("p (e u) m -> p m u e", u=2),
-        )
+        for t in range(4):
+            turn_emb(t)
         w2_codes = keep.tile([P, N], U32, name="w2_codes", align_bytes=64)
         w2_scales = keep.tile([P, N], U8, name="w2_scales", align_bytes=64)
-        quantize(w2_codes[:], w2_scales[:], w2_bf[:])
-        turn_emb(2)
-        turn_emb(3)
-        turn_up(2, 0, "scalar")
-        turn_up(3, 0, "scalar")
-        turn_up(2, 1, "scalar")
-        turn_up(3, 1, "vector")
+        for c in range(2):
+            for u in range(2):
+                turn_up(u, c, ("scalar", "vector")[u])
+        for c in range(2):
+            for u in range(2):
+                turn_up(2 + u, c, ("scalar", "vector")[u])
+            if c == 0:
+                quantize(w2_codes[:], w2_scales[:], w2_bf[:])
 
         y = [keep.tile([P, U], F32, name="y%d" % n) for n in range(2)]
-        z_bf = [keep.tile([P, HALF, PACK], BF16, name="z_bf%d" % q, align_bytes=64) for q in range(4)]
-        z_codes = [keep.tile([P, HALF], U32, name="z_codes%d" % q, align_bytes=64) for q in range(4)]
-        z_scales = [keep.tile([P, HALF], U8, name="z_scales%d" % q, align_bytes=64) for q in range(4)]
-        y_ps = []
-        for q in range(4):
-            back = bank(2 + q, "back%d" % q)
+        pieces = ((0, 2, 2, (7, 7), "scalar"), (2, 2, 3, (0, 0), "vector"), (4, 2, 4, (1, 1), "scalar"),
+                  (6, 1, 5, (2, 3), "scalar"), (7, 1, 6, (4, 5), "scalar"))
+        for i, (first, count, back_bank, y_banks, engine) in enumerate(pieces):
+            width = count * P
+            z_bf = keep.tile([P, width, PACK], BF16, name="z_bf%d" % i, align_bytes=64)
+            z_codes = keep.tile([P, width], U32, name="z_codes%d" % i, align_bytes=64)
+            z_scales = keep.tile([P, width], U8, name="z_scales%d" % i, align_bytes=64)
+            back = bank(back_bank, "back%d" % i)
             for u in range(2):
-                words = zT[u][q // 2][:].rearrange("p b r -> p (b r)").bitcast(F32)
-                for b in range(2):
-                    turn(back[:, span(2 * u + b, P)], words[:, span(2 * (q % 2) + b, P)], True, True)
-            copy_on("vector" if q == 1 else "scalar",
-                    z_bf[q][:].rearrange("p c j -> p (c j)").bitcast(F32).rearrange("p (c u) -> p c u", u=2),
-                    back[:].rearrange("p (u c) -> p c u", u=2))
-            quantize(z_codes[q][:], z_scales[q][:], z_bf[q][:])
-            y_ps.append(bank((6 + q) % 8, "y_ps%d" % q))
+                words = zT[u][first // 4][:].rearrange("p b r -> p (b r)").bitcast(F32)
+                for b in range(count):
+                    turn(back[:, span(count * u + b, P)], words[:, span(first % 4 + b, P)], True, True)
+            copy_on(engine, z_bf[:].rearrange("p c j -> p (c j)").bitcast(F32).rearrange("p (c u) -> p c u", u=2),
+                    back[:, 0:2 * width].rearrange("p (u c) -> p c u", u=2))
+            quantize(z_codes[:], z_scales[:], z_bf[:])
+            acc = [bank(y_banks[0], "y_ps%d" % i)]
+            acc.append(acc[0] if y_banks[1] == y_banks[0] else bank(y_banks[1], "y1_ps%d" % i))
             for n in range(2):
-                product(y_ps[q][:, span(n, HALF)], w2_codes[:, span(n, P)], w2_scales[:, span(n, P)],
-                        z_codes[q][:], z_scales[q][:])
+                product(acc[n][:, span(n, width)], w2_codes[:, span(n, P)], w2_scales[:, span(n, P)], z_codes[:], z_scales[:])
             for n in range(2):
-                copy_on("scalar" if n == 0 else "vector", y[n][:, span(q, HALF)], y_ps[q][:, span(n, HALF)])
+                copy_on("scalar" if n == 0 else "vector", y[n][:, first * P:first * P + width], acc[n][:, span(n, width)])
 
-        total = [bank(6 + c, "total%d" % c) for c in range(2)]
+        total = [bank((7 + c) % 8, "total%d" % c) for c in range(2)]
         for d in range(D):
             got = keep.tile([P, V], F32, name="got%d" % d)
             if d == 0:
-                nc.vector.tensor_copy(got[:], y[0][:].indirect(pos_t[d][:]))
+                nc.vector.tensor_copy(got[:, halves[1]], y[0][:].indirect(pos_t[d][:, list_halves[1]]))
+                nc.scalar.activation(got[:, halves[0]], y[0][:].indirect(pos_t[d][:, list_halves[0]]), COPY)
             else:
                 nc.scalar.activation(got[:], y[0][:].indirect(pos_t[d][:]), COPY)
-            turned = bank(2 + d, "turned%d" % d)
+            turned = bank((1, 6, 2, 3)[d], "turned%d" % d)
             for b in range(4):
                 turn(turned[:, span(b, P)], got[:, span(b, P)], True, True)
             gated = keep.tile([P, V], F32, name="gated%d" % d)
@@ -216,10 +231,6 @@ def tile_picked_devox_none_e_kernel(
             for b in range(4):
                 turn(total[b // 2][:, span(b % 2, P)], gated[:, span(b, P)], d == 0 and b % 2 == 0,
                      d == D - 1 and b % 2 == 1)
-        for c in range(2):
-            res0 = keep.tile([P, HALF], F32, name="res0_%d" % c)
-            nc.scalar.copy(res0[:], total[c][:, 0:HALF])
-            nc.sync.dma_start(out[0:P, halves[c]], res0[:])
 
         terms = []
         for d in range(D - 1):
@@ -239,3 +250,7 @@ def tile_picked_devox_none_e_kernel(
             res1 = keep.tile([P, HALF], F32, name="res1_%d" % c)
             nc.vector.tensor_tensor(res1[:], part[:, halves[c]], last[c][:], ADD)
             nc.sync.dma_start(out[P:N, halves[c]], res1[:])
+        for c in range(2):
+            res0 = keep.tile([P, HALF], F32, name="res0_%d" % c)
+            copy_on(("scalar", "vector")[c], res0[:], total[c][:, 0:HALF])
+            nc.sync.dma_start(out[0:P, halves[c]], res0[:])

@@ -69,7 +69,7 @@ def tile_picked_devox_none_e_kernel(
         nc.vector.memset(gate_rows[:], 0.0)
         up = []
         for t in range(4):
-            up.append(keep.tile([P, U], F32, name="up%d" % t))
+            up.append(keep.tile([P, U], F32, name="up%d" % t, tag="up%d" % t, align_bytes=64))
             nc.vector.memset(up[t][:], 0.0)
 
         x_rows = xT.rearrange("(p j) c -> j p c", j=PACK)
@@ -121,12 +121,13 @@ def tile_picked_devox_none_e_kernel(
 
         gather_last(0, 16)
         quantize(x_codes[:, halves[0]], x_scales[:, halves[0]], x_bf[:, halves[0], :])
-        nc.gpsimd.tensor_scalar(
-            w1_bf[1][:].rearrange("p (u r) j -> p u r j", u=2),
-            w1_raw[1][:].rearrange("p j (r u) -> p u r j", u=2), 1.0, 0.0, MULT, ADD)
+        for u in range(2):
+            copy_on(("scalar", "vector")[u],
+                    w1_bf[1][:, span(u, P), :].rearrange("p (s e) j -> p s j e", e=2),
+                    w1_raw[1][:].rearrange("p j (s e u) -> p u s j e", u=2, e=2)[:, u])
         gather_last(14, 32)
-        quantize(x_codes[:, halves[1]], x_scales[:, halves[1]], x_bf[:, halves[1], :])
         quantize(w1_codes[1][:], w1_scales[1][:], w1_bf[1][:])
+        quantize(x_codes[:, halves[1]], x_scales[:, halves[1]], x_bf[:, halves[1], :])
 
         def make_h(f, u, b, entries, engine):
             width = entries.stop - entries.start
@@ -149,10 +150,6 @@ def tile_picked_devox_none_e_kernel(
             scatter_scalar(0, c, h[0][:])
             nc.vector.tensor_copy(up[1][:].indirect(cell_t[:, list_halves[c]]), h[1][:])
         h = [make_h(1, u, u, slice(0, S), ("scalar", "vector")[u]) for u in range(2)]
-        w2_bf = keep.tile([P, N, PACK], BF16, name="w2_bf", align_bytes=64)
-        nc.gpsimd.tensor_scalar(
-            w2_bf[:].rearrange("p m (u e) -> p m u e", u=2),
-            w2_raw[:].rearrange("p (e u) m -> p m u e", u=2), 1.0, 0.0, MULT, ADD)
         for c in range(2):
             scatter_scalar(2, c, h[0][:, halves[c]])
         nc.vector.tensor_copy(up[3][:].indirect(cell_t[:]), h[1][:])
@@ -188,12 +185,16 @@ def tile_picked_devox_none_e_kernel(
         for c in range(2):
             for u in range(2):
                 turn_up(2 + u, c, ("scalar", "vector")[u])
-            if c == 0:
-                quantize(w2_codes[:], w2_scales[:], w2_bf[:])
+        w2_bf = keep.tile([P, N, PACK], BF16, name="w2_bf", tag="up3", align_bytes=64)
+        nc.vector.tensor_copy(
+            w2_bf[:].rearrange("p m (u e) -> p m u e", u=2),
+            w2_raw[:].rearrange("p (e u) m -> p m u e", u=2),
+        )
+        quantize(w2_codes[:], w2_scales[:], w2_bf[:])
 
         y = [keep.tile([P, U], F32, name="y%d" % n) for n in range(2)]
-        pieces = ((0, 2, 2, (7, 7), "scalar"), (2, 2, 3, (0, 0), "vector"), (4, 2, 4, (1, 1), "scalar"),
-                  (6, 1, 5, (2, 3), "scalar"), (7, 1, 6, (4, 5), "scalar"))
+        pieces = ((0, 2, 2, (7, 7), "scalar"), (2, 2, 3, (0, 0), "scalar"), (4, 2, 4, (1, 1), "scalar"),
+                  (6, 1, 5, (2, 3), "vector"), (7, 1, 6, (4, 5), "scalar"))
         for i, (first, count, back_bank, y_banks, engine) in enumerate(pieces):
             width = count * P
             z_bf = keep.tile([P, width, PACK], BF16, name="z_bf%d" % i, align_bytes=64)

@@ -219,8 +219,7 @@ def tile_picked_devox_none_e_kernel(
         for d in range(D):
             got = keep.tile([P, V], F32, name="got%d" % d)
             if d == 0:
-                nc.vector.tensor_copy(got[:, halves[1]], y[0][:].indirect(pos_t[d][:, list_halves[1]]))
-                nc.scalar.activation(got[:, halves[0]], y[0][:].indirect(pos_t[d][:, list_halves[0]]), COPY)
+                nc.vector.tensor_copy(got[:], y[0][:].indirect(pos_t[d][:]))
             else:
                 nc.scalar.activation(got[:], y[0][:].indirect(pos_t[d][:]), COPY)
             turned = bank((1, 6, 2, 3)[d], "turned%d" % d)
@@ -232,6 +231,10 @@ def tile_picked_devox_none_e_kernel(
             for b in range(4):
                 turn(total[b // 2][:, span(b % 2, P)], gated[:, span(b, P)], d == 0 and b % 2 == 0,
                      d == D - 1 and b % 2 == 1)
+        for c in range(2):
+            res0 = keep.tile([P, HALF], F32, name="res0_%d" % c)
+            nc.scalar.copy(res0[:], total[c][:, 0:HALF])
+            nc.sync.dma_start(out[0:P, halves[c]], res0[:])
 
         terms = []
         for d in range(D - 1):
@@ -251,7 +254,3 @@ def tile_picked_devox_none_e_kernel(
             res1 = keep.tile([P, HALF], F32, name="res1_%d" % c)
             nc.vector.tensor_tensor(res1[:], part[:, halves[c]], last[c][:], ADD)
             nc.sync.dma_start(out[P:N, halves[c]], res1[:])
-        for c in range(2):
-            res0 = keep.tile([P, HALF], F32, name="res0_%d" % c)
-            copy_on(("scalar", "vector")[c], res0[:], total[c][:, 0:HALF])
-            nc.sync.dma_start(out[0:P, halves[c]], res0[:])

@@ -74,24 +74,24 @@ def tile_picked_devox_none_e_kernel(
 
         x_rows = xT.rearrange("(p j) c -> j p c", j=PACK)
         w1_rows = w1.rearrange("(p j) c -> p j c", j=PACK)
-        emb_rows = emb.rearrange("(f r u) c -> f r u c", f=2, u=2)
+        emb_rows = emb.rearrange("(f r u) c -> f u r c", f=2, u=2)
         w1_raw = [keep.tile([P, PACK, HALF], F32, name="w1_raw%d" % f) for f in range(2)]
         x_plane = [keep.tile([P, T], F32, name="x_plane%d" % j) for j in range(PACK)]
-        emb_t = [keep.tile([P, 2, U], F32, name="emb_t%d" % f) for f in range(2)]
+        emb_t = [keep.tile([P, U], F32, name="emb_t%d" % t) for t in range(4)]
         w2_raw = keep.tile([P, PACK, N], F32, name="w2_raw")
         gate_t = keep.tile([P, D, V], F32, name="gate_t")
         nc.sync.dma_start(w1_raw[0][:], w1_rows[:, :, span(0, HALF)])
         nc.sync.dma_start(x_plane[0][:], x_rows[0])
         offs_t = load_list(offs, "offs_t")
+        nc.sync.dma_start(gate_rows[0:D, :], gate[:, 0, :])
         nc.sync.dma_start(x_plane[1][:], x_rows[1])
         cell_t = load_list(cell, "cell_t")
         for j in range(2, PACK):
             nc.sync.dma_start(x_plane[j][:], x_rows[j])
         nc.sync.dma_start(w1_raw[1][:], w1_rows[:, :, span(1, HALF)])
-        nc.sync.dma_start(gate_rows[0:D, :], gate[:, 0, :])
-        nc.sync.dma_start(emb_t[0][:], emb_rows[0])
+        for t in range(4):
+            nc.sync.dma_start(emb_t[t][:], emb_rows[t // 2, t % 2])
         nc.sync.dma_start(w2_raw[:], w2.rearrange("(p j) c -> p j c", j=PACK))
-        nc.sync.dma_start(emb_t[1][:], emb_rows[1])
         pos_t = [load_list(src, "pos_t%d" % d) for d, src in enumerate((pos1, pos2, pos3, pos4))]
         nc.sync.dma_start(gate_t[:], gate.rearrange("d p v -> p d v"))
 
@@ -168,7 +168,7 @@ def tile_picked_devox_none_e_kernel(
             sums[t] = [bank((2 + 2 * t + c) % 8, "sum%d_%d" % (t, c)) for c in range(2)]
             for c in range(2):
                 for b in range(4):
-                    turn(sums[t][c][:, span(b, P)], emb_t[t // 2][:, t % 2, span(4 * c + b, P)], b == 0, False)
+                    turn(sums[t][c][:, span(b, P)], emb_t[t][:, span(4 * c + b, P)], b == 0, False)
 
         def turn_up(t, c, engine):
             for b in range(4):

@@ -83,12 +83,11 @@ def tile_picked_devox_none_e_kernel(
         nc.sync.dma_start(w1_raw[0][:], w1_rows[:, :, span(0, HALF)])
         nc.sync.dma_start(x_plane[0][:], x_rows[0])
         offs_t = load_list(offs, "offs_t")
-        nc.sync.dma_start(gate_rows[0:D, :], gate[:, 0, :])
-        nc.sync.dma_start(x_plane[1][:], x_rows[1])
-        cell_t = load_list(cell, "cell_t")
-        for j in range(2, PACK):
+        for j in range(1, PACK):
             nc.sync.dma_start(x_plane[j][:], x_rows[j])
         nc.sync.dma_start(w1_raw[1][:], w1_rows[:, :, span(1, HALF)])
+        cell_t = load_list(cell, "cell_t")
+        nc.sync.dma_start(gate_rows[0:D, :], gate[:, 0, :])
         for t in range(4):
             nc.sync.dma_start(emb_t[t][:], emb_rows[t // 2, t % 2])
         nc.sync.dma_start(w2_raw[:], w2.rearrange("(p j) c -> p j c", j=PACK))
@@ -107,27 +106,20 @@ def tile_picked_devox_none_e_kernel(
         round_w1(0, "scalar")
         quantize(w1_codes[0][:], w1_scales[0][:], w1_bf[0][:])
 
-        x_bf = keep.tile([P, S, PACK], BF16, name="x_bf", align_bytes=64)
+        x_bf = [keep.tile([P, HALF, PACK], BF16, name="x_bf%d" % c, align_bytes=64) for c in range(2)]
+        x_planes = keep.tile([P, PACK, HALF], BF16, name="x_planes")
         x_codes = keep.tile([P, S], U32, name="x_codes", align_bytes=64)
         x_scales = keep.tile([P, S], U8, name="x_scales", align_bytes=64)
         halves = [span(c, HALF) for c in range(2)]
         list_halves = [span(c, HALF // STRIPE) for c in range(2)]
-        for j in range(PACK - 1):
-            nc.vector.tensor_copy(x_bf[:, :, j], x_plane[j][:].indirect(offs_t[:]))
-
-        def gather_last(c0, c1):
-            nc.vector.tensor_copy(x_bf[:, STRIPE * c0:STRIPE * c1, PACK - 1],
-                                  x_plane[PACK - 1][:].indirect(offs_t[:, c0:c1]))
-
-        gather_last(0, 16)
-        quantize(x_codes[:, halves[0]], x_scales[:, halves[0]], x_bf[:, halves[0], :])
-        for u in range(2):
-            copy_on(("scalar", "vector")[u],
-                    w1_bf[1][:, span(u, P), :].rearrange("p (s e) j -> p s j e", e=2),
-                    w1_raw[1][:].rearrange("p j (s e u) -> p u s j e", u=2, e=2)[:, u])
-        gather_last(14, 32)
+        for j in range(PACK):
+            nc.vector.tensor_copy(x_bf[0][:, :, j], x_plane[j][:].indirect(offs_t[:, list_halves[0]]))
+            nc.scalar.activation(x_planes[:, j, :], x_plane[j][:].indirect(offs_t[:, list_halves[1]]), COPY)
+        nc.scalar.copy(x_bf[1][:].rearrange("p (c i) j -> p c j i", i=4), x_planes[:].rearrange("p j (c i) -> p c j i", i=4))
+        quantize(x_codes[:, halves[0]], x_scales[:, halves[0]], x_bf[0][:])
+        round_w1(1, "vector")
+        quantize(x_codes[:, halves[1]], x_scales[:, halves[1]], x_bf[1][:])
         quantize(w1_codes[1][:], w1_scales[1][:], w1_bf[1][:])
-        quantize(x_codes[:, halves[1]], x_scales[:, halves[1]], x_bf[:, halves[1], :])
 
         def make_h(f, u, b, entries, engine):
             width = entries.stop - entries.start

@@ -74,37 +74,39 @@ def tile_picked_devox_none_e_kernel(
 
         x_rows = xT.rearrange("(p j) c -> j p c", j=PACK)
         w1_rows = w1.rearrange("(p j) c -> p j c", j=PACK)
-        emb_rows = emb.rearrange("(f r u) c -> f u r c", f=2, u=2)
-        w1_raw = [keep.tile([P, PACK, HALF], F32, name="w1_raw%d" % f) for f in range(2)]
+        w1_parts = (slice(0, P), slice(P, 2 * P), slice(2 * P, H))
+        w1_raw = [keep.tile([P, PACK, part.stop - part.start], F32, name="w1_raw%d" % i) for i, part in enumerate(w1_parts)]
         x_plane = [keep.tile([P, T], F32, name="x_plane%d" % j) for j in range(PACK)]
         emb_t = [keep.tile([P, U], F32, name="emb_t%d" % t) for t in range(4)]
         w2_raw = keep.tile([P, PACK, N], F32, name="w2_raw")
         gate_t = keep.tile([P, D, V], F32, name="gate_t")
-        nc.sync.dma_start(w1_raw[0][:], w1_rows[:, :, span(0, HALF)])
-        nc.sync.dma_start(x_plane[0][:], x_rows[0])
+        nc.sync.dma_start(w1_raw[0][:], w1_rows[:, :, w1_parts[0]])
         offs_t = load_list(offs, "offs_t")
-        for j in range(1, PACK):
+        for j in range(PACK):
             nc.sync.dma_start(x_plane[j][:], x_rows[j])
-        nc.sync.dma_start(w1_raw[1][:], w1_rows[:, :, span(1, HALF)])
+        for i in (1, 2):
+            nc.sync.dma_start(w1_raw[i][:], w1_rows[:, :, w1_parts[i]])
         cell_t = load_list(cell, "cell_t")
         nc.sync.dma_start(gate_rows[0:D, :], gate[:, 0, :])
         for t in range(4):
-            nc.sync.dma_start(emb_t[t][:], emb_rows[t // 2, t % 2])
+            nc.sync.dma_start(emb_t[t][:], emb[span(t, P), :])
         nc.sync.dma_start(w2_raw[:], w2.rearrange("(p j) c -> p j c", j=PACK))
         pos_t = [load_list(src, "pos_t%d" % d) for d, src in enumerate((pos1, pos2, pos3, pos4))]
         nc.sync.dma_start(gate_t[:], gate.rearrange("d p v -> p d v"))
 
-        w1_bf = [keep.tile([P, HALF, PACK], BF16, name="w1_bf%d" % f, align_bytes=64) for f in range(2)]
-        w1_codes = [keep.tile([P, HALF], U32, name="w1_codes%d" % f, align_bytes=64) for f in range(2)]
-        w1_scales = [keep.tile([P, HALF], U8, name="w1_scales%d" % f, align_bytes=64) for f in range(2)]
+        w1_codes = keep.tile([P, H], U32, name="w1_codes", align_bytes=64)
+        w1_scales = keep.tile([P, H], U8, name="w1_scales", align_bytes=64)
+        w1_bf = [keep.tile([P, part.stop - part.start, PACK], BF16, name="w1_bf%d" % i, align_bytes=64)
+                 for i, part in enumerate(w1_parts)]
 
-        def round_w1(f, engine):
-            copy_on(engine,
-                    w1_bf[f][:].rearrange("p (u s e) j -> p s j e u", u=2, e=2),
-                    w1_raw[f][:].rearrange("p j (s e u) -> p s j e u", u=2, e=2))
+        def interleave(engine, dst, src):
+            copy_on(engine, dst.rearrange("p (c i) j -> p c j i", i=4), src.rearrange("p j (c i) -> p c j i", i=4))
 
-        round_w1(0, "scalar")
-        quantize(w1_codes[0][:], w1_scales[0][:], w1_bf[0][:])
+        def quantize_w1(i):
+            quantize(w1_codes[:, w1_parts[i]], w1_scales[:, w1_parts[i]], w1_bf[i][:])
+
+        interleave("scalar", w1_bf[0][:], w1_raw[0][:])
+        quantize_w1(0)
 
         x_bf = [keep.tile([P, HALF, PACK], BF16, name="x_bf%d" % c, align_bytes=64) for c in range(2)]
         x_planes = keep.tile([P, PACK, HALF], BF16, name="x_planes")
@@ -115,17 +117,19 @@ def tile_picked_devox_none_e_kernel(
         for j in range(PACK):
             nc.vector.tensor_copy(x_bf[0][:, :, j], x_plane[j][:].indirect(offs_t[:, list_halves[0]]))
             nc.scalar.activation(x_planes[:, j, :], x_plane[j][:].indirect(offs_t[:, list_halves[1]]), COPY)
-        nc.scalar.copy(x_bf[1][:].rearrange("p (c i) j -> p c j i", i=4), x_planes[:].rearrange("p j (c i) -> p c j i", i=4))
+        interleave("scalar", x_bf[1][:], x_planes[:])
+        interleave("vector", w1_bf[1][:], w1_raw[1][:])
         quantize(x_codes[:, halves[0]], x_scales[:, halves[0]], x_bf[0][:])
-        round_w1(1, "vector")
+        quantize_w1(1)
+        interleave("vector", w1_bf[2][:], w1_raw[2][:])
         quantize(x_codes[:, halves[1]], x_scales[:, halves[1]], x_bf[1][:])
-        quantize(w1_codes[1][:], w1_scales[1][:], w1_bf[1][:])
+        quantize_w1(2)
 
         def make_h(f, u, b, entries, engine):
             width = entries.stop - entries.start
             name = "h%d_%d_%d" % (f, u, entries.start)
             acc = bank(b, name + "_ps")
-            product(acc[:, 0:width], w1_codes[f][:, span(u, P)], w1_scales[f][:, span(u, P)],
+            product(acc[:, 0:width], w1_codes[:, span(2 * f + u, P)], w1_scales[:, span(2 * f + u, P)],
                     x_codes[:, entries], x_scales[:, entries])
             h = keep.tile([P, width], F32, name=name, tag=name, align_bytes=64)
             if engine == "scalar":
@@ -137,23 +141,27 @@ def tile_picked_devox_none_e_kernel(
         def scatter_scalar(t, c, src):
             nc.scalar.activation(up[t][:].indirect(cell_t[:, list_halves[c]]), src, COPY)
 
-        for c in range(2):
-            h = [make_h(0, u, (u + c) % 2, halves[c], "vector" if u + c == 2 else "scalar") for u in range(2)]
-            scatter_scalar(0, c, h[0][:])
-            nc.vector.tensor_copy(up[1][:].indirect(cell_t[:, list_halves[c]]), h[1][:])
-        h = [make_h(1, u, u, slice(0, S), ("scalar", "vector")[u]) for u in range(2)]
+        def scatter_vector(t, columns, src):
+            nc.vector.tensor_copy(up[t][:].indirect(cell_t[:, columns]), src)
+
+        h = [make_h(0, u, u, halves[0], "scalar") for u in range(2)]
+        scatter_scalar(0, 0, h[0][:])
+        scatter_vector(1, list_halves[0], h[1][:])
+        h = [make_h(0, u, 1 - u, halves[1], "scalar") for u in range(2)]
+        scatter_scalar(0, 1, h[0][:])
+        scatter_vector(1, list_halves[1], h[1][:])
+        h = [make_h(1, u, 6 + u, slice(0, S), ("scalar", "vector")[u]) for u in range(2)]
         for c in range(2):
             scatter_scalar(2, c, h[0][:, halves[c]])
         nc.vector.tensor_copy(up[3][:].indirect(cell_t[:]), h[1][:])
 
-        gate_ps = bank(7, "gate_ps")
+        gate_ps = bank(5, "gate_ps")
         for b in range(4):
             turn(gate_ps[:, span(b, P)], gate_rows[:, span(b, P)], True, True)
         gate_cols = keep.tile([P, 4, D], F32, name="gate_cols")
         nc.scalar.copy(gate_cols[:], gate_ps[:].rearrange("p (b r) -> p b r", b=4)[:, :, 0:D])
 
-        zT = [[keep.tile([P, 4, HALF], BF16, name="zT%d_%d" % (u, c), align_bytes=64,
-                         tag="h1_0_0" if u + c == 0 else "zT%d_%d" % (u, c)) for c in range(2)] for u in range(2)]
+        zT = [keep.tile([P, 4, 2, HALF], BF16, name="zT%d" % c, align_bytes=64, tag=("h1_0_0", "zT1")[c]) for c in range(2)]
         sums = {}
 
         def turn_emb(t):
@@ -165,7 +173,8 @@ def tile_picked_devox_none_e_kernel(
         def turn_up(t, c, engine):
             for b in range(4):
                 turn(sums[t][c][:, span(b, P)], up[t][:, span(4 * c + b, P)], False, b == 3)
-            copy_on(engine, zT[t % 2][c][:, :, span(t // 2, P)], sums[t][c][:].rearrange("p (b r) -> p b r", b=4))
+            copy_on(engine, zT[c][:, :, :, span(t, 64)].rearrange("p b u (s e) -> p b u s e", e=2),
+                    sums[t][c][:].rearrange("p (b s u e) -> p b u s e", b=4, u=2, e=2))
 
         for t in range(4):
             turn_emb(t)
@@ -178,10 +187,7 @@ def tile_picked_devox_none_e_kernel(
             for u in range(2):
                 turn_up(2 + u, c, ("scalar", "vector")[u])
         w2_bf = keep.tile([P, N, PACK], BF16, name="w2_bf", tag="up3", align_bytes=64)
-        nc.vector.tensor_copy(
-            w2_bf[:].rearrange("p m (u e) -> p m u e", u=2),
-            w2_raw[:].rearrange("p (e u) m -> p m u e", u=2),
-        )
+        interleave("vector", w2_bf[:], w2_raw[:])
         quantize(w2_codes[:], w2_scales[:], w2_bf[:])
 
         y = [keep.tile([P, U], F32, name="y%d" % n) for n in range(2)]
@@ -194,9 +200,9 @@ def tile_picked_devox_none_e_kernel(
             z_scales = keep.tile([P, width], U8, name="z_scales%d" % i, align_bytes=64)
             back = bank(back_bank, "back%d" % i)
             for u in range(2):
-                words = zT[u][first // 4][:].rearrange("p b r -> p (b r)").bitcast(F32)
+                words = zT[first // 4][:].rearrange("p b u r -> p (b u r)").bitcast(F32)
                 for b in range(count):
-                    turn(back[:, span(count * u + b, P)], words[:, span(first % 4 + b, P)], True, True)
+                    turn(back[:, span(count * u + b, P)], words[:, span(2 * (first % 4 + b) + u, P)], True, True)
             copy_on(engine, z_bf[:].rearrange("p c j -> p (c j)").bitcast(F32).rearrange("p (c u) -> p c u", u=2),
                     back[:, 0:2 * width].rearrange("p (u c) -> p c u", u=2))
             quantize(z_codes[:], z_scales[:], z_bf[:])

@@ -65,8 +65,6 @@ def tile_picked_devox_none_e_kernel(
 
         ident = keep.tile([P, P], F32, name="ident")
         make_identity(nc, ident[:])
-        gate_rows = keep.tile([P, V], F32, name="gate_rows")
-        nc.vector.memset(gate_rows[:], 0.0)
         up = []
         for t in range(4):
             up.append(keep.tile([P, U], F32, name="up%d" % t, tag="up%d" % t, align_bytes=64))
@@ -87,12 +85,15 @@ def tile_picked_devox_none_e_kernel(
         for i in (1, 2):
             nc.sync.dma_start(w1_raw[i][:], w1_rows[:, :, w1_parts[i]])
         cell_t = load_list(cell, "cell_t")
-        nc.sync.dma_start(gate_rows[0:D, :], gate[:, 0, :])
         for t in range(4):
             nc.sync.dma_start(emb_t[t][:], emb[span(t, P), :])
         nc.sync.dma_start(w2_raw[:], w2.rearrange("(p j) c -> p j c", j=PACK))
         pos_t = [load_list(src, "pos_t%d" % d) for d, src in enumerate((pos1, pos2, pos3, pos4))]
         nc.sync.dma_start(gate_t[:], gate.rearrange("d p v -> p d v"))
+        gate_cols = keep.tile([P, D, 8], F32, name="gate_cols")
+        with nc.allow_non_contiguous_dma(reason="one gate value a partition"):
+            for d in range(D):
+                nc.sync.dma_start(gate_cols[:, d, 0:4], gate[d, 0, :].rearrange("(b p) -> p b", p=P))
 
         w1_codes = keep.tile([P, H], U32, name="w1_codes", align_bytes=64)
         w1_scales = keep.tile([P, H], U8, name="w1_scales", align_bytes=64)
@@ -155,12 +156,6 @@ def tile_picked_devox_none_e_kernel(
             scatter_scalar(2, c, h[0][:, halves[c]])
         nc.vector.tensor_copy(up[3][:].indirect(cell_t[:]), h[1][:])
 
-        gate_ps = bank(5, "gate_ps")
-        for b in range(4):
-            turn(gate_ps[:, span(b, P)], gate_rows[:, span(b, P)], True, True)
-        gate_cols = keep.tile([P, 4, D], F32, name="gate_cols")
-        nc.scalar.copy(gate_cols[:], gate_ps[:].rearrange("p (b r) -> p b r", b=4)[:, :, 0:D])
-
         zT = [keep.tile([P, 4, 2, HALF], BF16, name="zT%d" % c, align_bytes=64, tag=("h1_0_0", "zT1")[c]) for c in range(2)]
         sums = {}
 
@@ -192,7 +187,7 @@ def tile_picked_devox_none_e_kernel(
 
         y = [keep.tile([P, U], F32, name="y%d" % n) for n in range(2)]
         pieces = ((0, 2, 2, (7, 7), "scalar"), (2, 2, 3, (0, 0), "scalar"), (4, 2, 4, (1, 1), "scalar"),
-                  (6, 1, 5, (2, 3), "vector"), (7, 1, 6, (4, 5), "scalar"))
+                  (6, 1, 5, (2, 3), "scalar"), (7, 1, 6, (4, 5), "scalar"))
         for i, (first, count, back_bank, y_banks, engine) in enumerate(pieces):
             width = count * P
             z_bf = keep.tile([P, width, PACK], BF16, name="z_bf%d" % i, align_bytes=64)
@@ -213,42 +208,41 @@ def tile_picked_devox_none_e_kernel(
             for n in range(2):
                 copy_on("scalar" if n == 0 else "vector", y[n][:, first * P:first * P + width], acc[n][:, span(n, width)])
 
-        total = [bank((7 + c) % 8, "total%d" % c) for c in range(2)]
-        for d in range(D):
-            got = keep.tile([P, V], F32, name="got%d" % d)
-            if d == 0:
-                nc.vector.tensor_copy(got[:], y[0][:].indirect(pos_t[d][:]))
-            else:
-                nc.scalar.activation(got[:], y[0][:].indirect(pos_t[d][:]), COPY)
-            turned = bank((1, 6, 2, 3)[d], "turned%d" % d)
-            for b in range(4):
-                turn(turned[:, span(b, P)], got[:, span(b, P)], True, True)
-            gated = keep.tile([P, V], F32, name="gated%d" % d)
-            for b in range(4):
-                nc.scalar.activation(gated[:, span(b, P)], turned[:, span(b, P)], COPY, scale=gate_cols[:, b, d:d + 1])
-            for b in range(4):
-                turn(total[b // 2][:, span(b % 2, P)], gated[:, span(b, P)], d == 0 and b % 2 == 0,
-                     d == D - 1 and b % 2 == 1)
-        for c in range(2):
-            res0 = keep.tile([P, HALF], F32, name="res0_%d" % c)
-            nc.scalar.copy(res0[:], total[c][:, 0:HALF])
-            nc.sync.dma_start(out[0:P, halves[c]], res0[:])
+        def fetch_gated(n, d, cols, name):
+            term = keep.tile([P, cols.stop - cols.start], F32, name=name)
+            offsets = pos_t[d][:, cols.start // STRIPE:cols.stop // STRIPE]
+            nc.vector.tensor_tensor(term[:], y[n][:].indirect(offsets), gate_t[:, d, cols], MULT)
+            return term
 
-        terms = []
-        for d in range(D - 1):
-            terms.append(keep.tile([P, V], F32, name="term%d" % d))
-            nc.vector.tensor_tensor(terms[d][:], y[1][:].indirect(pos_t[d][:]), gate_t[:, d, :], MULT)
+        total = [bank((7 + c) % 8, "total%d" % c) for c in range(2)]
+        last0 = fetch_gated(0, D - 1, halves[1], "last0")
+        for d in range(D):
+            blocks = 4 if d < D - 1 else 2
+            got = keep.tile([P, blocks * P], F32, name="got%d" % d)
+            nc.scalar.activation(got[:], y[0][:].indirect(pos_t[d][:, 0:blocks * P // STRIPE]), COPY)
+            turned = bank((1, 6, 2, 3)[d], "turned%d" % d)
+            for b in range(blocks):
+                turn(turned[:, span(b, P)], got[:, span(b, P)], True, True)
+            gated = keep.tile([P, blocks * P], F32, name="gated%d" % d)
+            for b in range(blocks):
+                nc.scalar.activation(gated[:, span(b, P)], turned[:, span(b, P)], COPY, scale=gate_cols[:, d, b:b + 1])
+            for b in range(blocks):
+                turn(total[b // 2][:, span(b % 2, P)], gated[:, span(b, P)], d == 0 and b % 2 == 0,
+                     d == D - 1 - b // 2 and b % 2 == 1)
+
+        terms = [fetch_gated(1, d, slice(0, V), "term%d" % d) for d in range(D - 1)]
         part = terms[0]
         for d in range(1, D - 1):
             more = keep.tile([P, V], F32, name="part%d" % d)
             nc.vector.tensor_tensor(more[:], part[:], terms[d][:], ADD)
             part = more
-        last = []
-        for c in range(2):
-            last.append(keep.tile([P, HALF], F32, name="last%d" % c))
-            nc.vector.tensor_tensor(last[c][:], y[1][:].indirect(pos_t[D - 1][:, list_halves[c]]),
-                                    gate_t[:, D - 1, halves[c]], MULT)
+        last = [fetch_gated(1, D - 1, halves[c], "last1_%d" % c) for c in range(2)]
         for c in range(2):
             res1 = keep.tile([P, HALF], F32, name="res1_%d" % c)
             nc.vector.tensor_tensor(res1[:], part[:, halves[c]], last[c][:], ADD)
             nc.sync.dma_start(out[P:N, halves[c]], res1[:])
+        res0 = [keep.tile([P, HALF], F32, name="res0_%d" % c) for c in range(2)]
+        nc.vector.tensor_tensor(res0[1][:], total[1][:, 0:HALF], last0[:], ADD)
+        nc.sync.dma_start(out[0:P, halves[1]], res0[1][:])
+        nc.scalar.copy(res0[0][:], total[0][:, 0:HALF])
+        nc.sync.dma_start(out[0:P, halves[0]], res0[0][:])

@@ -75,7 +75,9 @@ def tile_picked_devox_none_e_kernel(
         w1_parts = (slice(0, P), slice(P, 2 * P), slice(2 * P, H))
         w1_raw = [keep.tile([P, PACK, part.stop - part.start], F32, name="w1_raw%d" % i) for i, part in enumerate(w1_parts)]
         x_plane = [keep.tile([P, T], F32, name="x_plane%d" % j) for j in range(PACK)]
-        emb_t = [keep.tile([P, U], F32, name="emb_t%d" % t) for t in range(4)]
+        emb_t = [keep.tile([P, U], F32, name="emb_t%d" % t)[:] for t in range(2)]
+        emb_late = keep.tile([P, 2, U], F32, name="emb_late")
+        emb_t = emb_t + [emb_late[:, t, :] for t in range(2)]
         w2_raw = keep.tile([P, PACK, N], F32, name="w2_raw")
         gate_t = keep.tile([P, D, V], F32, name="gate_t")
         nc.sync.dma_start(w1_raw[0][:], w1_rows[:, :, w1_parts[0]])
@@ -85,8 +87,9 @@ def tile_picked_devox_none_e_kernel(
         for i in (1, 2):
             nc.sync.dma_start(w1_raw[i][:], w1_rows[:, :, w1_parts[i]])
         cell_t = load_list(cell, "cell_t")
-        for t in range(4):
-            nc.sync.dma_start(emb_t[t][:], emb[span(t, P), :])
+        for t in range(2):
+            nc.sync.dma_start(emb_t[t], emb[span(t, P), :])
+        nc.sync.dma_start(emb_late[:], emb[2 * P:H, :].rearrange("(t p) c -> p t c", p=P))
         nc.sync.dma_start(w2_raw[:], w2.rearrange("(p j) c -> p j c", j=PACK))
         pos_t = [load_list(src, "pos_t%d" % d) for d, src in enumerate((pos1, pos2, pos3, pos4))]
         nc.sync.dma_start(gate_t[:], gate.rearrange("d p v -> p d v"))
@@ -118,45 +121,52 @@ def tile_picked_devox_none_e_kernel(
         for j in range(PACK):
             nc.vector.tensor_copy(x_bf[0][:, :, j], x_plane[j][:].indirect(offs_t[:, list_halves[0]]))
             nc.scalar.activation(x_planes[:, j, :], x_plane[j][:].indirect(offs_t[:, list_halves[1]]), COPY)
-        interleave("scalar", x_bf[1][:], x_planes[:])
-        interleave("vector", w1_bf[1][:], w1_raw[1][:])
+            if j == PACK - 2:
+                interleave("scalar", x_bf[1][:, :, 0:PACK - 1], x_planes[:, 0:PACK - 1, :])
+        nc.scalar.copy(x_bf[1][:, :, PACK - 1], x_planes[:, PACK - 1, :])
         quantize(x_codes[:, halves[0]], x_scales[:, halves[0]], x_bf[0][:])
+        interleave("vector", w1_bf[1][:], w1_raw[1][:])
+        quantize(x_codes[:, halves[1]], x_scales[:, halves[1]], x_bf[1][:])
         quantize_w1(1)
         interleave("vector", w1_bf[2][:], w1_raw[2][:])
-        quantize(x_codes[:, halves[1]], x_scales[:, halves[1]], x_bf[1][:])
-        quantize_w1(2)
 
-        def make_h(f, u, b, entries, engine):
+        def make_h(t, b, entries):
             width = entries.stop - entries.start
-            name = "h%d_%d_%d" % (f, u, entries.start)
-            acc = bank(b, name + "_ps")
-            product(acc[:, 0:width], w1_codes[:, span(2 * f + u, P)], w1_scales[:, span(2 * f + u, P)],
+            acc = bank(b, "h%d_%d_ps" % (t, entries.start))
+            product(acc[:, 0:width], w1_codes[:, span(t, P)], w1_scales[:, span(t, P)],
                     x_codes[:, entries], x_scales[:, entries])
-            h = keep.tile([P, width], F32, name=name, tag=name, align_bytes=64)
+            return acc[:, 0:width]
+
+        def relu(engine, dst, acc):
             if engine == "scalar":
-                nc.scalar.activation(h[:], acc[:, 0:width], RELU)
+                nc.scalar.activation(dst, acc, RELU)
             else:
-                nc.vector.tensor_scalar_max(h[:], acc[:, 0:width], 0.0)
-            return h
+                nc.vector.tensor_scalar_max(dst, acc, 0.0)
 
-        def scatter_scalar(t, c, src):
-            nc.scalar.activation(up[t][:].indirect(cell_t[:, list_halves[c]]), src, COPY)
+        def scatter_scalar(t, c):
+            nc.scalar.activation(up[t][:].indirect(cell_t[:, list_halves[c]]), h[t][:, halves[c]], COPY)
 
-        def scatter_vector(t, columns, src):
-            nc.vector.tensor_copy(up[t][:].indirect(cell_t[:, columns]), src)
+        def scatter_vector(t):
+            nc.vector.tensor_copy(up[t][:].indirect(cell_t[:]), h[t][:])
 
-        h = [make_h(0, u, u, halves[0], "scalar") for u in range(2)]
-        scatter_scalar(0, 0, h[0][:])
-        scatter_vector(1, list_halves[0], h[1][:])
-        h = [make_h(0, u, 1 - u, halves[1], "scalar") for u in range(2)]
-        scatter_scalar(0, 1, h[0][:])
-        scatter_vector(1, list_halves[1], h[1][:])
-        h = [make_h(1, u, 6 + u, slice(0, S), ("scalar", "vector")[u]) for u in range(2)]
+        h = [keep.tile([P, S], F32, name="h%d" % t, tag="h%d" % t, align_bytes=64) for t in range(4)]
+        whole = slice(0, S)
+        relu("scalar", h[0][:, halves[0]], make_h(0, 0, halves[0]))
+        scatter_scalar(0, 0)
+        relu("vector", h[0][:, halves[1]], make_h(0, 1, halves[1]))
+        relu("vector", h[1][:], make_h(1, 6, whole))
+        quantize_w1(2)
+        scatter_vector(1)
+        scatter_scalar(0, 1)
+        relu("scalar", h[3][:], make_h(3, 7, whole))
+        acc = make_h(2, 6, whole)
         for c in range(2):
-            scatter_scalar(2, c, h[0][:, halves[c]])
-        nc.vector.tensor_copy(up[3][:].indirect(cell_t[:]), h[1][:])
+            relu("scalar", h[2][:, halves[c]], acc[:, halves[c]])
+        scatter_vector(3)
+        for c in range(2):
+            scatter_scalar(2, c)
 
-        zT = [keep.tile([P, 4, 2, HALF], BF16, name="zT%d" % c, align_bytes=64, tag=("h1_0_0", "zT1")[c]) for c in range(2)]
+        zT = [keep.tile([P, 4, 2, HALF], BF16, name="zT%d" % c, align_bytes=64, tag=("h2", "zT1")[c]) for c in range(2)]
         sums = {}
 
         def turn_emb(t):

@@ -65,6 +65,8 @@ def tile_picked_devox_none_e_kernel(
 
         ident = keep.tile([P, P], F32, name="ident")
         make_identity(nc, ident[:])
+        ident_bf = keep.tile([P, P], BF16, name="ident_bf")
+        make_identity(nc, ident_bf[:])
         up = []
         for t in range(4):
             up.append(keep.tile([P, U], F32, name="up%d" % t, tag="up%d" % t, align_bytes=64))
@@ -75,9 +77,9 @@ def tile_picked_devox_none_e_kernel(
         w1_parts = (slice(0, P), slice(P, 2 * P), slice(2 * P, H))
         w1_raw = [keep.tile([P, PACK, part.stop - part.start], F32, name="w1_raw%d" % i) for i, part in enumerate(w1_parts)]
         x_plane = [keep.tile([P, T], F32, name="x_plane%d" % j) for j in range(PACK)]
-        emb_t = [keep.tile([P, U], F32, name="emb_t%d" % t)[:] for t in range(2)]
-        emb_late = keep.tile([P, 2, U], F32, name="emb_late")
-        emb_t = emb_t + [emb_late[:, t, :] for t in range(2)]
+        emb0 = [keep.tile([P, BANK], F32, name="emb0_%d" % c) for c in range(2)]
+        emb_rest = keep.tile([P, 3, U], F32, name="emb_rest")
+        emb_t = [None] + [emb_rest[:, t, :] for t in range(3)]
         w2_raw = keep.tile([P, PACK, N], F32, name="w2_raw")
         gate_t = keep.tile([P, D, V], F32, name="gate_t")
         nc.sync.dma_start(w1_raw[0][:], w1_rows[:, :, w1_parts[0]])
@@ -87,9 +89,9 @@ def tile_picked_devox_none_e_kernel(
         for i in (1, 2):
             nc.sync.dma_start(w1_raw[i][:], w1_rows[:, :, w1_parts[i]])
         cell_t = load_list(cell, "cell_t")
-        for t in range(2):
-            nc.sync.dma_start(emb_t[t], emb[span(t, P), :])
-        nc.sync.dma_start(emb_late[:], emb[2 * P:H, :].rearrange("(t p) c -> p t c", p=P))
+        nc.sync.dma_start(emb_rest[:], emb[P:H, :].rearrange("(t p) c -> p t c", p=P))
+        for c in range(2):
+            nc.sync.dma_start(emb0[c][:], emb[0:P, span(c, BANK)])
         nc.sync.dma_start(w2_raw[:], w2.rearrange("(p j) c -> p j c", j=PACK))
         pos_t = [load_list(src, "pos_t%d" % d) for d, src in enumerate((pos1, pos2, pos3, pos4))]
         nc.sync.dma_start(gate_t[:], gate.rearrange("d p v -> p d v"))
@@ -181,13 +183,21 @@ def tile_picked_devox_none_e_kernel(
             copy_on(engine, zT[c][:, :, :, span(t, 64)].rearrange("p b u (s e) -> p b u s e", e=2),
                     sums[t][c][:].rearrange("p (b s u e) -> p b u s e", b=4, u=2, e=2))
 
-        for t in range(4):
+        for t in range(1, 4):
             turn_emb(t)
         w2_codes = keep.tile([P, N], U32, name="w2_codes", align_bytes=64)
         w2_scales = keep.tile([P, N], U8, name="w2_scales", align_bytes=64)
         for c in range(2):
-            for u in range(2):
-                turn_up(u, c, ("scalar", "vector")[u])
+            turn_up(1, c, "vector")
+        for c in range(2):
+            z0 = keep.tile([P, BANK], BF16, name="z0_%d" % c)
+            nc.gpsimd.tensor_tensor(z0[:], up[0][:, span(c, BANK)], emb0[c][:], ADD)
+            turned0 = psum.tile([P, 2 * BANK], BF16, name="turned0_%d" % c, tag="bank%d" % (2 + c))
+            for b in range(4):
+                nc.tensor.transpose(turned0[:, span(b, P)], z0[:, span(b, P)], ident_bf[:])
+            nc.scalar.copy(
+                zT[c][:].rearrange("p b u r -> p (b u r)").bitcast(F32).rearrange("p (b u s) -> p b u s", b=4, u=2)[:, :, :, span(0, 32)],
+                turned0[:, 0:BANK].bitcast(F32).rearrange("p (b s u) -> p b u s", b=4, u=2))
         for c in range(2):
             for u in range(2):
                 turn_up(2 + u, c, ("scalar", "vector")[u])

@@ -77,9 +77,9 @@ def tile_picked_devox_none_e_kernel(
         w1_parts = (slice(0, P), slice(P, 2 * P), slice(2 * P, H))
         w1_raw = [keep.tile([P, PACK, part.stop - part.start], F32, name="w1_raw%d" % i) for i, part in enumerate(w1_parts)]
         x_plane = [keep.tile([P, T], F32, name="x_plane%d" % j) for j in range(PACK)]
-        emb0 = [keep.tile([P, BANK], F32, name="emb0_%d" % c) for c in range(2)]
-        emb_rest = keep.tile([P, 3, U], F32, name="emb_rest")
-        emb_t = [None] + [emb_rest[:, t, :] for t in range(3)]
+        emb_early = [[keep.tile([P, BANK], F32, name="emb%d_%d" % (t, c)) for c in range(2)] for t in range(2)]
+        emb2 = keep.tile([P, U], F32, name="emb2")
+        emb3 = [keep.tile([P, 4, P], F32, name="emb3_%d" % b) for b in range(2)]
         w2_raw = keep.tile([P, PACK, N], F32, name="w2_raw")
         gate_t = keep.tile([P, D, V], F32, name="gate_t")
         nc.sync.dma_start(w1_raw[0][:], w1_rows[:, :, w1_parts[0]])
@@ -89,12 +89,16 @@ def tile_picked_devox_none_e_kernel(
         for i in (1, 2):
             nc.sync.dma_start(w1_raw[i][:], w1_rows[:, :, w1_parts[i]])
         cell_t = load_list(cell, "cell_t")
-        nc.sync.dma_start(emb_rest[:], emb[P:H, :].rearrange("(t p) c -> p t c", p=P))
-        for c in range(2):
-            nc.sync.dma_start(emb0[c][:], emb[0:P, span(c, BANK)])
         nc.sync.dma_start(w2_raw[:], w2.rearrange("(p j) c -> p j c", j=PACK))
+        emb3_blocks = emb[span(3, P), :].rearrange("p (q b r) -> b p q r", q=4, b=2)
+        nc.sync.dma_start(emb2[:], emb[span(2, P), :])
+        nc.sync.dma_start(emb3[0][:], emb3_blocks[0])
+        for t in range(2):
+            for c in range(2):
+                nc.sync.dma_start(emb_early[t][c][:], emb[span(t, P), span(c, BANK)])
         pos_t = [load_list(src, "pos_t%d" % d) for d, src in enumerate((pos1, pos2, pos3, pos4))]
         nc.sync.dma_start(gate_t[:], gate.rearrange("d p v -> p d v"))
+        nc.sync.dma_start(emb3[1][:], emb3_blocks[1])
         gate_cols = keep.tile([P, D, 8], F32, name="gate_cols")
         with nc.allow_non_contiguous_dma(reason="one gate value a partition"):
             for d in range(D):
@@ -102,7 +106,7 @@ def tile_picked_devox_none_e_kernel(
 
         w1_codes = keep.tile([P, H], U32, name="w1_codes", align_bytes=64)
         w1_scales = keep.tile([P, H], U8, name="w1_scales", align_bytes=64)
-        w1_bf = [keep.tile([P, part.stop - part.start, PACK], BF16, name="w1_bf%d" % i, align_bytes=64)
+        w1_bf = [keep.tile([P, part.stop - part.start, PACK], BF16, name="w1_bf%d" % i, tag="w1_bf%d" % i, align_bytes=64)
                  for i, part in enumerate(w1_parts)]
 
         def interleave(engine, dst, src):
@@ -168,46 +172,57 @@ def tile_picked_devox_none_e_kernel(
         for c in range(2):
             scatter_scalar(2, c)
 
-        zT = [keep.tile([P, 4, 2, HALF], BF16, name="zT%d" % c, align_bytes=64, tag=("h2", "zT1")[c]) for c in range(2)]
-        sums = {}
+        zT = [keep.tile([P, 4, 2, HALF], BF16, name="zT%d" % c, align_bytes=64) for c in range(2)]
+        late = [bank(2 + q, "late%d" % q) for q in range(4)]
 
-        def turn_emb(t):
-            sums[t] = [bank((2 + 2 * t + c) % 8, "sum%d_%d" % (t, c)) for c in range(2)]
-            for c in range(2):
-                for b in range(4):
-                    turn(sums[t][c][:, span(b, P)], emb_t[t][:, span(4 * c + b, P)], b == 0, False)
+        def turn_late(block, first):
+            for q in range(4):
+                for i in range(4):
+                    t, b = divmod(i, 2)
+                    turn(late[q][:, span(2 * b + t, P)], block(t, q, b), first and i == 0, not first and i == 3)
 
-        def turn_up(t, c, engine):
+        def round_late(q, engine):
+            c, pair = divmod(q, 2)
+            copy_on(engine, zT[c][:, span(pair, 2), :, P:HALF].rearrange("p b u (s e) -> p b u s e", e=2),
+                    late[q][:].rearrange("p (b s u e) -> p b u s e", b=2, u=2, e=2))
+
+        def turn_early(t, c):
+            z = keep.tile([P, BANK], BF16, name="z%d_%d" % (t, c))
+            nc.gpsimd.tensor_tensor(z[:], up[t][:, span(c, BANK)], emb_early[t][c][:], ADD)
+            turned = psum.tile([P, 2 * BANK], BF16, name="early%d_%d" % (t, c), tag="bank%d" % ((0, 1), (7, 6))[c][t])
             for b in range(4):
-                turn(sums[t][c][:, span(b, P)], up[t][:, span(4 * c + b, P)], False, b == 3)
-            copy_on(engine, zT[c][:, :, :, span(t, 64)].rearrange("p b u (s e) -> p b u s e", e=2),
-                    sums[t][c][:].rearrange("p (b s u e) -> p b u s e", b=4, u=2, e=2))
+                nc.tensor.transpose(turned[:, span(b, P)], z[:, span(b, P)], ident_bf[:])
+            return turned
 
-        for t in range(1, 4):
-            turn_emb(t)
-        w2_codes = keep.tile([P, N], U32, name="w2_codes", align_bytes=64)
+        def move_early(t, c, engine):
+            copy_on(
+                engine,
+                zT[c][:].rearrange("p b u r -> p (b u r)").bitcast(F32).rearrange("p (b u s) -> p b u s", b=4, u=2)[:, :, :, span(t, 32)],
+                early[t, c][:, 0:BANK].bitcast(F32).rearrange("p (b s u) -> p b u s", b=4, u=2))
+
+        turn_late(lambda t, q, b: emb3[b][:, q, :] if t else emb2[:, span(2 * q + b, P)], True)
+        sum11 = bank(6, "sum11")
+        for first, src in ((True, emb_early[1][1]), (False, up[1][:, span(1, BANK)])):
+            for b in range(4):
+                turn(sum11[:, span(b, P)], src[:, span(b, P)], first and b == 0, not first and b == 3)
+        early = {(t, c): turn_early(t, c) for t, c in ((0, 0), (0, 1), (1, 0))}
+        turn_late(lambda t, q, b: up[2 + t][:, span(2 * q + b, P)], False)
+        w2_codes = keep.tile([P, N], U32, name="w2_codes", tag="up3", align_bytes=64)
+        w2_bf = keep.tile([P, N, PACK], BF16, name="w2_bf", tag="h3", align_bytes=64)
         w2_scales = keep.tile([P, N], U8, name="w2_scales", align_bytes=64)
-        for c in range(2):
-            turn_up(1, c, "vector")
-        for c in range(2):
-            z0 = keep.tile([P, BANK], BF16, name="z0_%d" % c)
-            nc.gpsimd.tensor_tensor(z0[:], up[0][:, span(c, BANK)], emb0[c][:], ADD)
-            turned0 = psum.tile([P, 2 * BANK], BF16, name="turned0_%d" % c, tag="bank%d" % (2 + c))
-            for b in range(4):
-                nc.tensor.transpose(turned0[:, span(b, P)], z0[:, span(b, P)], ident_bf[:])
-            nc.scalar.copy(
-                zT[c][:].rearrange("p b u r -> p (b u r)").bitcast(F32).rearrange("p (b u s) -> p b u s", b=4, u=2)[:, :, :, span(0, 32)],
-                turned0[:, 0:BANK].bitcast(F32).rearrange("p (b s u) -> p b u s", b=4, u=2))
-        for c in range(2):
-            for u in range(2):
-                turn_up(2 + u, c, ("scalar", "vector")[u])
-        w2_bf = keep.tile([P, N, PACK], BF16, name="w2_bf", tag="up3", align_bytes=64)
         interleave("vector", w2_bf[:], w2_raw[:])
+        move_early(0, 0, "scalar")
+        move_early(1, 0, "vector")
+        move_early(0, 1, "vector")
+        copy_on("scalar", zT[1][:, :, :, span(1, 64)].rearrange("p b u (s e) -> p b u s e", e=2),
+                sum11[:].rearrange("p (b s u e) -> p b u s e", b=4, u=2, e=2))
+        for q in range(4):
+            round_late(q, ("scalar", "vector")[q % 2])
         quantize(w2_codes[:], w2_scales[:], w2_bf[:])
 
         y = [keep.tile([P, U], F32, name="y%d" % n) for n in range(2)]
-        pieces = ((0, 2, 2, (7, 7), "scalar"), (2, 2, 3, (0, 0), "scalar"), (4, 2, 4, (1, 1), "scalar"),
-                  (6, 1, 5, (2, 3), "scalar"), (7, 1, 6, (4, 5), "scalar"))
+        pieces = ((0, 2, 0, (2, 2), "scalar"), (2, 2, 1, (3, 3), "scalar"), (4, 2, 7, (0, 0), "scalar"),
+                  (6, 1, 4, (1, 6), "scalar"), (7, 1, 5, (7, 2), "scalar"))
         for i, (first, count, back_bank, y_banks, engine) in enumerate(pieces):
             width = count * P
             z_bf = keep.tile([P, width, PACK], BF16, name="z_bf%d" % i, align_bytes=64)

@@ -74,31 +74,31 @@ def tile_picked_devox_none_e_kernel(
 
         x_rows = xT.rearrange("(p j) c -> j p c", j=PACK)
         w1_rows = w1.rearrange("(p j) c -> p j c", j=PACK)
-        w1_parts = (slice(0, P), slice(P, 2 * P), slice(2 * P, H))
-        w1_raw = [keep.tile([P, PACK, part.stop - part.start], F32, name="w1_raw%d" % i) for i, part in enumerate(w1_parts)]
+        w1_parts = [span(t, P) for t in range(4)]
+        w1_raw = [keep.tile([P, PACK, part.stop - part.start], F32, name="w1_raw%d" % i, tag="w1_raw%d" % i, align_bytes=64) for i, part in enumerate(w1_parts)]
         x_plane = [keep.tile([P, T], F32, name="x_plane%d" % j) for j in range(PACK)]
         emb_early = [[keep.tile([P, BANK], F32, name="emb%d_%d" % (t, c)) for c in range(2)] for t in range(2)]
         emb2 = keep.tile([P, U], F32, name="emb2")
         emb3 = [keep.tile([P, 4, P], F32, name="emb3_%d" % b) for b in range(2)]
         w2_raw = keep.tile([P, PACK, N], F32, name="w2_raw")
         gate_t = keep.tile([P, D, V], F32, name="gate_t")
-        nc.sync.dma_start(w1_raw[0][:], w1_rows[:, :, w1_parts[0]])
         offs_t = load_list(offs, "offs_t")
         for j in range(PACK):
             nc.sync.dma_start(x_plane[j][:], x_rows[j])
-        for i in (1, 2):
+        for i in range(3):
             nc.sync.dma_start(w1_raw[i][:], w1_rows[:, :, w1_parts[i]])
         cell_t = load_list(cell, "cell_t")
+        nc.sync.dma_start(w1_raw[3][:], w1_rows[:, :, w1_parts[3]])
         nc.sync.dma_start(w2_raw[:], w2.rearrange("(p j) c -> p j c", j=PACK))
         emb3_blocks = emb[span(3, P), :].rearrange("p (q b r) -> b p q r", q=4, b=2)
         nc.sync.dma_start(emb2[:], emb[span(2, P), :])
         nc.sync.dma_start(emb3[0][:], emb3_blocks[0])
-        for t in range(2):
-            for c in range(2):
-                nc.sync.dma_start(emb_early[t][c][:], emb[span(t, P), span(c, BANK)])
+        for t, c in ((0, 0), (1, 0), (1, 1)):
+            nc.sync.dma_start(emb_early[t][c][:], emb[span(t, P), span(c, BANK)])
         pos_t = [load_list(src, "pos_t%d" % d) for d, src in enumerate((pos1, pos2, pos3, pos4))]
-        nc.sync.dma_start(gate_t[:], gate.rearrange("d p v -> p d v"))
+        nc.sync.dma_start(emb_early[0][1][:], emb[span(0, P), span(1, BANK)])
         nc.sync.dma_start(emb3[1][:], emb3_blocks[1])
+        nc.sync.dma_start(gate_t[:], gate.rearrange("d p v -> p d v"))
         gate_cols = keep.tile([P, D, 8], F32, name="gate_cols")
         with nc.allow_non_contiguous_dma(reason="one gate value a partition"):
             for d in range(D):
@@ -115,13 +115,9 @@ def tile_picked_devox_none_e_kernel(
         def quantize_w1(i):
             quantize(w1_codes[:, w1_parts[i]], w1_scales[:, w1_parts[i]], w1_bf[i][:])
 
-        interleave("scalar", w1_bf[0][:], w1_raw[0][:])
-        quantize_w1(0)
 
         x_bf = [keep.tile([P, HALF, PACK], BF16, name="x_bf%d" % c, align_bytes=64) for c in range(2)]
         x_planes = keep.tile([P, PACK, HALF], BF16, name="x_planes")
-        x_codes = keep.tile([P, S], U32, name="x_codes", align_bytes=64)
-        x_scales = keep.tile([P, S], U8, name="x_scales", align_bytes=64)
         halves = [span(c, HALF) for c in range(2)]
         list_halves = [span(c, HALF // STRIPE) for c in range(2)]
         for j in range(PACK):
@@ -129,19 +125,25 @@ def tile_picked_devox_none_e_kernel(
             nc.scalar.activation(x_planes[:, j, :], x_plane[j][:].indirect(offs_t[:, list_halves[1]]), COPY)
             if j == PACK - 2:
                 interleave("scalar", x_bf[1][:, :, 0:PACK - 1], x_planes[:, 0:PACK - 1, :])
+        x_codes = keep.tile([P, S], U32, name="x_codes", align_bytes=64)
         nc.scalar.copy(x_bf[1][:, :, PACK - 1], x_planes[:, PACK - 1, :])
-        quantize(x_codes[:, halves[0]], x_scales[:, halves[0]], x_bf[0][:])
+        interleave("vector", w1_bf[0][:], w1_raw[0][:])
+        x_scales = [keep.tile([P, HALF], U8, name="x_scales0", tag="w1_raw0", align_bytes=64)]
+        quantize(x_codes[:, halves[0]], x_scales[0][:], x_bf[0][:])
+        quantize_w1(0)
         interleave("vector", w1_bf[1][:], w1_raw[1][:])
-        quantize(x_codes[:, halves[1]], x_scales[:, halves[1]], x_bf[1][:])
+        x_scales.append(keep.tile([P, HALF], U8, name="x_scales1", tag="w1_bf0", align_bytes=64))
+        quantize(x_codes[:, halves[1]], x_scales[1][:], x_bf[1][:])
         quantize_w1(1)
-        interleave("vector", w1_bf[2][:], w1_raw[2][:])
+        interleave("scalar", w1_bf[2][:], w1_raw[2][:])
+        quantize_w1(2)
+        interleave("vector", w1_bf[3][:], w1_raw[3][:])
 
-        def make_h(t, b, entries):
-            width = entries.stop - entries.start
-            acc = bank(b, "h%d_%d_ps" % (t, entries.start))
-            product(acc[:, 0:width], w1_codes[:, span(t, P)], w1_scales[:, span(t, P)],
-                    x_codes[:, entries], x_scales[:, entries])
-            return acc[:, 0:width]
+        def make_h(t, b, c):
+            acc = bank(b, "h%d_%d_ps" % (t, c))
+            product(acc[:, 0:HALF], w1_codes[:, span(t, P)], w1_scales[:, span(t, P)],
+                    x_codes[:, halves[c]], x_scales[c][:])
+            return acc[:, 0:HALF]
 
         def relu(engine, dst, acc):
             if engine == "scalar":
@@ -152,23 +154,28 @@ def tile_picked_devox_none_e_kernel(
         def scatter_scalar(t, c):
             nc.scalar.activation(up[t][:].indirect(cell_t[:, list_halves[c]]), h[t][:, halves[c]], COPY)
 
-        def scatter_vector(t):
-            nc.vector.tensor_copy(up[t][:].indirect(cell_t[:]), h[t][:])
+        def scatter_vector(t, entries):
+            columns = slice(entries.start // STRIPE, entries.stop // STRIPE)
+            nc.vector.tensor_copy(up[t][:].indirect(cell_t[:, columns]), h[t][:, entries])
 
-        h = [keep.tile([P, S], F32, name="h%d" % t, tag="h%d" % t, align_bytes=64) for t in range(4)]
+        h = [keep.tile([P, S], F32, name="h%d" % t, tag=("w1_raw2", "h1", "h2", "h3")[t], align_bytes=64) for t in range(4)]
         whole = slice(0, S)
-        relu("scalar", h[0][:, halves[0]], make_h(0, 0, halves[0]))
+        relu("scalar", h[0][:, halves[0]], make_h(0, 0, 0))
         scatter_scalar(0, 0)
-        relu("vector", h[0][:, halves[1]], make_h(0, 1, halves[1]))
-        relu("vector", h[1][:], make_h(1, 6, whole))
-        quantize_w1(2)
-        scatter_vector(1)
+        relu("scalar", h[0][:, halves[1]], make_h(0, 6, 1))
+        relu("vector", h[1][:, halves[0]], make_h(1, 1, 0))
+        quantize_w1(3)
+        w2_bf = keep.tile([P, N, PACK], BF16, name="w2_bf", tag="w1_bf3", align_bytes=64)
+        nc.gpsimd.tensor_scalar(w2_bf[:], w2_raw[:].rearrange("p j c -> p c j"), 1.0, 0.0, MULT, ADD)
+        scatter_vector(1, halves[0])
+        relu("scalar", h[1][:, halves[1]], make_h(1, 7, 1))
         scatter_scalar(0, 1)
-        relu("scalar", h[3][:], make_h(3, 7, whole))
-        acc = make_h(2, 6, whole)
-        for c in range(2):
-            relu("scalar", h[2][:, halves[c]], acc[:, halves[c]])
-        scatter_vector(3)
+        relu("vector", h[3][:, halves[0]], make_h(3, 0, 0))
+        scatter_vector(1, halves[1])
+        relu("scalar", h[2][:, halves[0]], make_h(2, 1, 0))
+        relu("vector", h[2][:, halves[1]], make_h(2, 6, 1))
+        relu("scalar", h[3][:, halves[1]], make_h(3, 7, 1))
+        scatter_vector(3, whole)
         for c in range(2):
             scatter_scalar(2, c)
 
@@ -205,12 +212,11 @@ def tile_picked_devox_none_e_kernel(
         for first, src in ((True, emb_early[1][1]), (False, up[1][:, span(1, BANK)])):
             for b in range(4):
                 turn(sum11[:, span(b, P)], src[:, span(b, P)], first and b == 0, not first and b == 3)
-        early = {(t, c): turn_early(t, c) for t, c in ((0, 0), (0, 1), (1, 0))}
+        early = {(t, c): turn_early(t, c) for t, c in ((0, 0), (1, 0), (0, 1))}
         turn_late(lambda t, q, b: up[2 + t][:, span(2 * q + b, P)], False)
-        w2_codes = keep.tile([P, N], U32, name="w2_codes", tag="up3", align_bytes=64)
-        w2_bf = keep.tile([P, N, PACK], BF16, name="w2_bf", tag="h3", align_bytes=64)
+        w2_codes = keep.tile([P, N], U32, name="w2_codes", tag="h3", align_bytes=64)
         w2_scales = keep.tile([P, N], U8, name="w2_scales", align_bytes=64)
-        interleave("vector", w2_bf[:], w2_raw[:])
+        quantize(w2_codes[:], w2_scales[:], w2_bf[:])
         move_early(0, 0, "scalar")
         move_early(1, 0, "vector")
         move_early(0, 1, "vector")
@@ -218,10 +224,9 @@ def tile_picked_devox_none_e_kernel(
                 sum11[:].rearrange("p (b s u e) -> p b u s e", b=4, u=2, e=2))
         for q in range(4):
             round_late(q, ("scalar", "vector")[q % 2])
-        quantize(w2_codes[:], w2_scales[:], w2_bf[:])
 
         y = [keep.tile([P, U], F32, name="y%d" % n) for n in range(2)]
-        pieces = ((0, 2, 0, (2, 2), "scalar"), (2, 2, 1, (3, 3), "scalar"), (4, 2, 7, (0, 0), "scalar"),
+        pieces = ((0, 2, 0, (2, 2), "scalar"), (2, 2, 1, (3, 3), "vector"), (4, 2, 7, (0, 0), "scalar"),
                   (6, 1, 4, (1, 6), "scalar"), (7, 1, 5, (7, 2), "scalar"))
         for i, (first, count, back_bank, y_banks, engine) in enumerate(pieces):
             width = count * P

@@ -82,8 +82,9 @@ def tile_picked_devox_none_e_kernel(
         emb3 = [keep.tile([P, 4, P], F32, name="emb3_%d" % b) for b in range(2)]
         w2_raw = keep.tile([P, PACK, N], F32, name="w2_raw")
         gate_t = keep.tile([P, D, V], F32, name="gate_t")
+        nc.sync.dma_start(x_plane[0][:], x_rows[0])
         offs_t = load_list(offs, "offs_t")
-        for j in range(PACK):
+        for j in range(1, PACK):
             nc.sync.dma_start(x_plane[j][:], x_rows[j])
         for i in range(3):
             nc.sync.dma_start(w1_raw[i][:], w1_rows[:, :, w1_parts[i]])
@@ -93,12 +94,13 @@ def tile_picked_devox_none_e_kernel(
         emb3_blocks = emb[span(3, P), :].rearrange("p (q b r) -> b p q r", q=4, b=2)
         nc.sync.dma_start(emb2[:], emb[span(2, P), :])
         nc.sync.dma_start(emb3[0][:], emb3_blocks[0])
-        for t, c in ((0, 0), (1, 0), (1, 1)):
+        for t, c in ((0, 0), (0, 1), (1, 1), (1, 0)):
             nc.sync.dma_start(emb_early[t][c][:], emb[span(t, P), span(c, BANK)])
         pos_t = [load_list(src, "pos_t%d" % d) for d, src in enumerate((pos1, pos2, pos3, pos4))]
-        nc.sync.dma_start(emb_early[0][1][:], emb[span(0, P), span(1, BANK)])
+        gate_rows = gate.rearrange("d p v -> p d v")
+        nc.sync.dma_start(gate_t[:, 0:2, :], gate_rows[:, 0:2, :])
         nc.sync.dma_start(emb3[1][:], emb3_blocks[1])
-        nc.sync.dma_start(gate_t[:], gate.rearrange("d p v -> p d v"))
+        nc.sync.dma_start(gate_t[:, 2:D, :], gate_rows[:, 2:D, :])
         gate_cols = keep.tile([P, D, 8], F32, name="gate_cols")
         with nc.allow_non_contiguous_dma(reason="one gate value a partition"):
             for d in range(D):
@@ -139,11 +141,9 @@ def tile_picked_devox_none_e_kernel(
         quantize_w1(2)
         interleave("vector", w1_bf[3][:], w1_raw[3][:])
 
-        def make_h(t, b, c):
-            acc = bank(b, "h%d_%d_ps" % (t, c))
-            product(acc[:, 0:HALF], w1_codes[:, span(t, P)], w1_scales[:, span(t, P)],
-                    x_codes[:, halves[c]], x_scales[c][:])
-            return acc[:, 0:HALF]
+        def make_h(t, c, acc):
+            product(acc, w1_codes[:, span(t, P)], w1_scales[:, span(t, P)], x_codes[:, halves[c]], x_scales[c][:])
+            return acc
 
         def relu(engine, dst, acc):
             if engine == "scalar":
@@ -158,23 +158,29 @@ def tile_picked_devox_none_e_kernel(
             columns = slice(entries.start // STRIPE, entries.stop // STRIPE)
             nc.vector.tensor_copy(up[t][:].indirect(cell_t[:, columns]), h[t][:, entries])
 
-        h = [keep.tile([P, S], F32, name="h%d" % t, tag=("w1_raw2", "h1", "h2", "h3")[t], align_bytes=64) for t in range(4)]
+        h = [keep.tile([P, S], F32, name="h%d" % t, tag=("w1_raw2", "w1_raw3", "h2", "h3")[t], align_bytes=64) for t in range(4)]
         whole = slice(0, S)
-        relu("scalar", h[0][:, halves[0]], make_h(0, 0, 0))
+        relu("scalar", h[0][:, halves[0]], make_h(0, 0, bank(0, "h00")[:, halves[0]]))
         scatter_scalar(0, 0)
-        relu("scalar", h[0][:, halves[1]], make_h(0, 6, 1))
-        relu("vector", h[1][:, halves[0]], make_h(1, 1, 0))
+        relu("scalar", h[0][:, halves[1]], make_h(0, 1, bank(6, "h01")[:, halves[0]]))
+        relu("vector", h[1][:, halves[0]], make_h(1, 0, bank(1, "h10")[:, halves[0]]))
         quantize_w1(3)
         w2_bf = keep.tile([P, N, PACK], BF16, name="w2_bf", tag="w1_bf3", align_bytes=64)
         nc.gpsimd.tensor_scalar(w2_bf[:], w2_raw[:].rearrange("p j c -> p c j"), 1.0, 0.0, MULT, ADD)
         scatter_vector(1, halves[0])
-        relu("scalar", h[1][:, halves[1]], make_h(1, 7, 1))
+        relu("scalar", h[1][:, halves[1]], make_h(1, 1, bank(0, "h11")[:, halves[0]]))
         scatter_scalar(0, 1)
-        relu("vector", h[3][:, halves[0]], make_h(3, 0, 0))
+        for_scalar = bank(7, "h_scalar")
+        for_vector = bank(1, "h_vector")
+        acc = {(2, 0): for_scalar[:, halves[0]], (2, 1): for_vector[:, halves[0]],
+               (3, 0): for_vector[:, halves[1]], (3, 1): for_scalar[:, halves[1]]}
+        for t, c in acc:
+            make_h(t, c, acc[t, c])
+        relu("vector", h[3][:, halves[0]], acc[3, 0])
         scatter_vector(1, halves[1])
-        relu("scalar", h[2][:, halves[0]], make_h(2, 1, 0))
-        relu("vector", h[2][:, halves[1]], make_h(2, 6, 1))
-        relu("scalar", h[3][:, halves[1]], make_h(3, 7, 1))
+        relu("scalar", h[2][:, halves[0]], acc[2, 0])
+        relu("vector", h[2][:, halves[1]], acc[2, 1])
+        relu("scalar", h[3][:, halves[1]], acc[3, 1])
         scatter_vector(3, whole)
         for c in range(2):
             scatter_scalar(2, c)
@@ -196,7 +202,7 @@ def tile_picked_devox_none_e_kernel(
         def turn_early(t, c):
             z = keep.tile([P, BANK], BF16, name="z%d_%d" % (t, c))
             nc.gpsimd.tensor_tensor(z[:], up[t][:, span(c, BANK)], emb_early[t][c][:], ADD)
-            turned = psum.tile([P, 2 * BANK], BF16, name="early%d_%d" % (t, c), tag="bank%d" % ((0, 1), (7, 6))[c][t])
+            turned = psum.tile([P, 2 * BANK], BF16, name="early%d_%d" % (t, c), tag="bank%d" % t)
             for b in range(4):
                 nc.tensor.transpose(turned[:, span(b, P)], z[:, span(b, P)], ident_bf[:])
             return turned
@@ -208,20 +214,21 @@ def tile_picked_devox_none_e_kernel(
                 early[t, c][:, 0:BANK].bitcast(F32).rearrange("p (b s u) -> p b u s", b=4, u=2))
 
         turn_late(lambda t, q, b: emb3[b][:, q, :] if t else emb2[:, span(2 * q + b, P)], True)
-        sum11 = bank(6, "sum11")
-        for first, src in ((True, emb_early[1][1]), (False, up[1][:, span(1, BANK)])):
-            for b in range(4):
-                turn(sum11[:, span(b, P)], src[:, span(b, P)], first and b == 0, not first and b == 3)
-        early = {(t, c): turn_early(t, c) for t, c in ((0, 0), (1, 0), (0, 1))}
+        sums = [bank(6 + t, "sum%d" % t) for t in range(2)]
+        for t in range(2):
+            for first, src in ((True, emb_early[t][1]), (False, up[t][:, span(1, BANK)])):
+                for b in range(4):
+                    turn(sums[t][:, span(b, P)], src[:, span(b, P)], first and b == 0, not first and b == 3)
+        early = {(t, 0): turn_early(t, 0) for t in range(2)}
         turn_late(lambda t, q, b: up[2 + t][:, span(2 * q + b, P)], False)
         w2_codes = keep.tile([P, N], U32, name="w2_codes", tag="h3", align_bytes=64)
         w2_scales = keep.tile([P, N], U8, name="w2_scales", align_bytes=64)
         quantize(w2_codes[:], w2_scales[:], w2_bf[:])
         move_early(0, 0, "scalar")
         move_early(1, 0, "vector")
-        move_early(0, 1, "vector")
-        copy_on("scalar", zT[1][:, :, :, span(1, 64)].rearrange("p b u (s e) -> p b u s e", e=2),
-                sum11[:].rearrange("p (b s u e) -> p b u s e", b=4, u=2, e=2))
+        for t in range(2):
+            copy_on(("vector", "scalar")[t], zT[1][:, :, :, span(t, 64)].rearrange("p b u (s e) -> p b u s e", e=2),
+                    sums[t][:].rearrange("p (b s u e) -> p b u s e", b=4, u=2, e=2))
         for q in range(4):
             round_late(q, ("scalar", "vector")[q % 2])
 
@@ -248,14 +255,13 @@ def tile_picked_devox_none_e_kernel(
             for n in range(2):
                 copy_on("scalar" if n == 0 else "vector", y[n][:, first * P:first * P + width], acc[n][:, span(n, width)])
 
-        def fetch_gated(n, d, cols, name):
-            term = keep.tile([P, cols.stop - cols.start], F32, name=name)
+        def fetch_gated(n, d, cols, name, tag=None):
+            term = keep.tile([P, cols.stop - cols.start], F32, name=name, tag=tag or name)
             offsets = pos_t[d][:, cols.start // STRIPE:cols.stop // STRIPE]
             nc.vector.tensor_tensor(term[:], y[n][:].indirect(offsets), gate_t[:, d, cols], MULT)
             return term
 
         total = [bank((7 + c) % 8, "total%d" % c) for c in range(2)]
-        last0 = fetch_gated(0, D - 1, halves[1], "last0")
         for d in range(D):
             blocks = 4 if d < D - 1 else 2
             got = keep.tile([P, blocks * P], F32, name="got%d" % d)
@@ -281,8 +287,11 @@ def tile_picked_devox_none_e_kernel(
             res1 = keep.tile([P, HALF], F32, name="res1_%d" % c)
             nc.vector.tensor_tensor(res1[:], part[:, halves[c]], last[c][:], ADD)
             nc.sync.dma_start(out[P:N, halves[c]], res1[:])
-        res0 = [keep.tile([P, HALF], F32, name="res0_%d" % c) for c in range(2)]
-        nc.vector.tensor_tensor(res0[1][:], total[1][:, 0:HALF], last0[:], ADD)
-        nc.sync.dma_start(out[0:P, halves[1]], res0[1][:])
-        nc.scalar.copy(res0[0][:], total[0][:, 0:HALF])
-        nc.sync.dma_start(out[0:P, halves[0]], res0[0][:])
+        last0 = [fetch_gated(0, D - 1, span(2 + b, P), "last0_%d" % b, (None, "last1_0")[b]) for b in range(2)]
+        for b in range(2):
+            res0 = keep.tile([P, P], F32, name="res0_%d" % b)
+            nc.vector.tensor_tensor(res0[:], total[1][:, span(b, P)], last0[b][:], ADD)
+            nc.sync.dma_start(out[0:P, span(2 + b, P)], res0[:])
+        first0 = keep.tile([P, HALF], F32, name="first0")
+        nc.scalar.copy(first0[:], total[0][:, 0:HALF])
+        nc.scalar.dma_start(out[0:P, halves[0]], first0[:])

@@ -219,7 +219,12 @@ def tile_picked_devox_none_e_kernel(
             for first, src in ((True, emb_early[t][1]), (False, up[t][:, span(1, BANK)])):
                 for b in range(4):
                     turn(sums[t][:, span(b, P)], src[:, span(b, P)], first and b == 0, not first and b == 3)
-        early = {(t, 0): turn_early(t, 0) for t in range(2)}
+        early = {}
+        for t in range(2):
+            early[t, 0] = turn_early(t, 0)
+            spare = early[t, 0][:, BANK:2 * BANK].bitcast(F32)
+            for i in range(2):
+                product(spare, w1_codes[:, span(i, P)], w1_scales[:, span(i, P)], x_codes[:, halves[0]], x_scales[0][:])
         turn_late(lambda t, q, b: up[2 + t][:, span(2 * q + b, P)], False)
         w2_codes = keep.tile([P, N], U32, name="w2_codes", tag="h3", align_bytes=64)
         w2_scales = keep.tile([P, N], U8, name="w2_scales", align_bytes=64)

@@ -219,12 +219,10 @@ def tile_picked_devox_none_e_kernel(
             for first, src in ((True, emb_early[t][1]), (False, up[t][:, span(1, BANK)])):
                 for b in range(4):
                     turn(sums[t][:, span(b, P)], src[:, span(b, P)], first and b == 0, not first and b == 3)
-        early = {}
-        for t in range(2):
-            early[t, 0] = turn_early(t, 0)
-            spare = early[t, 0][:, BANK:2 * BANK].bitcast(F32)
-            for i in range(2):
-                product(spare, w1_codes[:, span(i, P)], w1_scales[:, span(i, P)], x_codes[:, halves[0]], x_scales[0][:])
+        early = {(t, 0): turn_early(t, 0) for t in range(2)}
+        spare = early[1, 0][:, BANK:2 * BANK].bitcast(F32)
+        for i in range(4):
+            product(spare, w1_codes[:, span(i, P)], w1_scales[:, span(i, P)], x_codes[:, halves[0]], x_scales[0][:])
         turn_late(lambda t, q, b: up[2 + t][:, span(2 * q + b, P)], False)
         w2_codes = keep.tile([P, N], U32, name="w2_codes", tag="h3", align_bytes=64)
         w2_scales = keep.tile([P, N], U8, name="w2_scales", align_bytes=64)

@@ -219,18 +219,19 @@ def tile_picked_devox_none_e_kernel(
             for first, src in ((True, emb_early[t][1]), (False, up[t][:, span(1, BANK)])):
                 for b in range(4):
                     turn(sums[t][:, span(b, P)], src[:, span(b, P)], first and b == 0, not first and b == 3)
-        early = {(t, 0): turn_early(t, 0) for t in range(2)}
-        spare = early[1, 0][:, BANK:2 * BANK].bitcast(F32)
+        early = {(0, 0): turn_early(0, 0)}
+        spare = early[0, 0][:, BANK:2 * BANK].bitcast(F32)
         for i in range(4):
             product(spare, w1_codes[:, span(i, P)], w1_scales[:, span(i, P)], x_codes[:, halves[0]], x_scales[0][:])
+        early[1, 0] = turn_early(1, 0)
         turn_late(lambda t, q, b: up[2 + t][:, span(2 * q + b, P)], False)
         w2_codes = keep.tile([P, N], U32, name="w2_codes", tag="h3", align_bytes=64)
         w2_scales = keep.tile([P, N], U8, name="w2_scales", align_bytes=64)
         quantize(w2_codes[:], w2_scales[:], w2_bf[:])
-        move_early(0, 0, "scalar")
+        move_early(0, 0, "vector")
         move_early(1, 0, "vector")
         for t in range(2):
-            copy_on(("vector", "scalar")[t], zT[1][:, :, :, span(t, 64)].rearrange("p b u (s e) -> p b u s e", e=2),
+            copy_on("scalar", zT[1][:, :, :, span(t, 64)].rearrange("p b u (s e) -> p b u s e", e=2),
                     sums[t][:].rearrange("p (b s u e) -> p b u s e", b=4, u=2, e=2))
         for q in range(4):
             round_late(q, ("scalar", "vector")[q % 2])

@@ -40,6 +40,9 @@ def tile_picked_devox_none_e_kernel(
         def bank(b, name):
             return psum.tile([P, BANK], F32, name=name, tag="bank%d" % b)
 
+        def sbuf(shape, dtype, name, tag=None):
+            return keep.tile([P] + shape, dtype, name=name, tag=tag or name, align_bytes=64)
+
         def load_list(src, name):
             offsets = lists.tile([P, S // STRIPE], U16, name=name)
             nc.sync.dma_start(offsets[:], src)
@@ -54,8 +57,8 @@ def tile_picked_devox_none_e_kernel(
                 rhs=moving_codes.bitcast(FP8X4), rhs_scale=moving_scales, start=True, stop=True,
             )
 
-        def turn(dst, src, start, stop):
-            nc.tensor.matmul(dst, src, ident[:], start=start, stop=stop, is_transpose=True)
+        def turn(dst, src, start, stop, identity):
+            nc.tensor.matmul(dst, src, identity[:], start=start, stop=stop, is_transpose=True)
 
         def copy_on(engine, dst, src):
             if engine == "vector":
@@ -63,87 +66,79 @@ def tile_picked_devox_none_e_kernel(
             else:
                 nc.scalar.copy(dst, src)
 
-        ident = keep.tile([P, P], F32, name="ident")
+        def weave(engine, dst, src):
+            copy_on(engine, dst.rearrange("p (c i) j -> p c j i", i=4), src.rearrange("p j (c i) -> p c j i", i=4))
+
+        def weave_gpsimd(dst, src):
+            nc.gpsimd.tensor_scalar(dst, src.rearrange("p j c -> p c j"), 1.0, 0.0, MULT, ADD)
+
+        ident = sbuf([P], F32, "ident")
         make_identity(nc, ident[:])
-        ident_bf = keep.tile([P, P], BF16, name="ident_bf")
+        ident_bf = sbuf([P], BF16, "ident_bf")
         make_identity(nc, ident_bf[:])
-        up = []
+        up = [sbuf([U], F32, "up%d" % t) for t in range(4)]
         for t in range(4):
-            up.append(keep.tile([P, U], F32, name="up%d" % t, tag="up%d" % t, align_bytes=64))
             nc.vector.memset(up[t][:], 0.0)
 
         x_rows = xT.rearrange("(p j) c -> j p c", j=PACK)
         w1_rows = w1.rearrange("(p j) c -> p j c", j=PACK)
-        w1_parts = [span(t, P) for t in range(4)]
-        w1_raw = [keep.tile([P, PACK, part.stop - part.start], F32, name="w1_raw%d" % i, tag="w1_raw%d" % i, align_bytes=64) for i, part in enumerate(w1_parts)]
-        x_plane = [keep.tile([P, T], F32, name="x_plane%d" % j) for j in range(PACK)]
-        emb_early = [[keep.tile([P, BANK], F32, name="emb%d_%d" % (t, c)) for c in range(2)] for t in range(2)]
-        emb2 = keep.tile([P, U], F32, name="emb2")
-        emb3 = [keep.tile([P, 4, P], F32, name="emb3_%d" % b) for b in range(2)]
-        w2_raw = keep.tile([P, PACK, N], F32, name="w2_raw")
-        gate_t = keep.tile([P, D, V], F32, name="gate_t")
+        w1_parts = [slice(0, P), slice(P, HALF), slice(HALF, H)]
+        w1_raw = [sbuf([PACK, part.stop - part.start], F32, "w1_raw%d" % i) for i, part in enumerate(w1_parts)]
+        x_plane = [sbuf([T], F32, "x_plane%d" % j) for j in range(PACK)]
+        emb_early = [[sbuf([BANK], F32, "emb%d_%d" % (t, c)) for c in range(2)] for t in range(2)]
+        emb_late = [sbuf([U], F32, "emb%d" % t) for t in (2, 3)]
+        w2_raw = sbuf([PACK, N], F32, "w2_raw")
+        gate_t = sbuf([D, V], F32, "gate_t")
         nc.sync.dma_start(x_plane[0][:], x_rows[0])
         offs_t = load_list(offs, "offs_t")
         for j in range(1, PACK):
             nc.sync.dma_start(x_plane[j][:], x_rows[j])
-        for i in range(3):
+        for i in range(2):
             nc.sync.dma_start(w1_raw[i][:], w1_rows[:, :, w1_parts[i]])
         cell_t = load_list(cell, "cell_t")
-        nc.sync.dma_start(w1_raw[3][:], w1_rows[:, :, w1_parts[3]])
+        nc.sync.dma_start(w1_raw[2][:], w1_rows[:, :, w1_parts[2]])
+        for t in range(2):
+            nc.sync.dma_start(emb_late[t][:], emb[span(2 + t, P), :])
         nc.sync.dma_start(w2_raw[:], w2.rearrange("(p j) c -> p j c", j=PACK))
-        emb3_blocks = emb[span(3, P), :].rearrange("p (q b r) -> b p q r", q=4, b=2)
-        nc.sync.dma_start(emb2[:], emb[span(2, P), :])
-        nc.sync.dma_start(emb3[0][:], emb3_blocks[0])
-        for t, c in ((0, 0), (0, 1), (1, 1), (1, 0)):
-            nc.sync.dma_start(emb_early[t][c][:], emb[span(t, P), span(c, BANK)])
+        for c in range(2):
+            for t in range(2):
+                nc.sync.dma_start(emb_early[t][c][:], emb[span(t, P), span(c, BANK)])
         pos_t = [load_list(src, "pos_t%d" % d) for d, src in enumerate((pos1, pos2, pos3, pos4))]
-        gate_rows = gate.rearrange("d p v -> p d v")
-        nc.sync.dma_start(gate_t[:, 0:2, :], gate_rows[:, 0:2, :])
-        nc.sync.dma_start(emb3[1][:], emb3_blocks[1])
-        nc.sync.dma_start(gate_t[:, 2:D, :], gate_rows[:, 2:D, :])
-        gate_cols = keep.tile([P, D, 8], F32, name="gate_cols")
+        nc.sync.dma_start(gate_t[:], gate.rearrange("d p v -> p d v"))
+        gate_cols = sbuf([D, 8], F32, "gate_cols")
         with nc.allow_non_contiguous_dma(reason="one gate value a partition"):
             for d in range(D):
                 nc.sync.dma_start(gate_cols[:, d, 0:4], gate[d, 0, :].rearrange("(b p) -> p b", p=P))
 
-        w1_codes = keep.tile([P, H], U32, name="w1_codes", align_bytes=64)
-        w1_scales = keep.tile([P, H], U8, name="w1_scales", align_bytes=64)
-        w1_bf = [keep.tile([P, part.stop - part.start, PACK], BF16, name="w1_bf%d" % i, tag="w1_bf%d" % i, align_bytes=64)
-                 for i, part in enumerate(w1_parts)]
-
-        def interleave(engine, dst, src):
-            copy_on(engine, dst.rearrange("p (c i) j -> p c j i", i=4), src.rearrange("p j (c i) -> p c j i", i=4))
-
-        def quantize_w1(i):
-            quantize(w1_codes[:, w1_parts[i]], w1_scales[:, w1_parts[i]], w1_bf[i][:])
-
-
-        x_bf = [keep.tile([P, HALF, PACK], BF16, name="x_bf%d" % c, align_bytes=64) for c in range(2)]
-        x_planes = keep.tile([P, PACK, HALF], BF16, name="x_planes")
         halves = [span(c, HALF) for c in range(2)]
         list_halves = [span(c, HALF // STRIPE) for c in range(2)]
+        x_bf = [sbuf([HALF, PACK], BF16, "x_bf%d" % c) for c in range(2)]
+        x_planes = sbuf([PACK, HALF], BF16, "x_planes")
         for j in range(PACK):
             nc.vector.tensor_copy(x_bf[0][:, :, j], x_plane[j][:].indirect(offs_t[:, list_halves[0]]))
             nc.scalar.activation(x_planes[:, j, :], x_plane[j][:].indirect(offs_t[:, list_halves[1]]), COPY)
-            if j == PACK - 2:
-                interleave("scalar", x_bf[1][:, :, 0:PACK - 1], x_planes[:, 0:PACK - 1, :])
-        x_codes = keep.tile([P, S], U32, name="x_codes", align_bytes=64)
-        nc.scalar.copy(x_bf[1][:, :, PACK - 1], x_planes[:, PACK - 1, :])
-        interleave("vector", w1_bf[0][:], w1_raw[0][:])
-        x_scales = [keep.tile([P, HALF], U8, name="x_scales0", tag="w1_raw0", align_bytes=64)]
+            if j == 1:
+                weave("scalar", x_bf[1][:, :, 0:2], x_planes[:, 0:2, :])
+        x_codes = sbuf([S], U32, "x_codes")
+        x_scales = [sbuf([HALF], U8, "x_scales0")]
+        w1_codes = sbuf([H], U32, "w1_codes")
+        w1_scales = sbuf([H], U8, "w1_scales")
+        w1_bf = [sbuf([P, PACK], BF16, "w1_bf%d" % i) for i in range(2)]
+        for i in range(2):
+            weave("scalar", w1_bf[i][:], w1_raw[i][:])
+        weave("vector", x_bf[1][:, :, 2:PACK], x_planes[:, 2:PACK, :])
         quantize(x_codes[:, halves[0]], x_scales[0][:], x_bf[0][:])
-        quantize_w1(0)
-        interleave("vector", w1_bf[1][:], w1_raw[1][:])
-        x_scales.append(keep.tile([P, HALF], U8, name="x_scales1", tag="w1_bf0", align_bytes=64))
+        quantize(w1_codes[:, w1_parts[0]], w1_scales[:, w1_parts[0]], w1_bf[0][:])
+        x_scales.append(sbuf([HALF], U8, "x_scales1", tag="w1_raw0"))
         quantize(x_codes[:, halves[1]], x_scales[1][:], x_bf[1][:])
-        quantize_w1(1)
-        interleave("scalar", w1_bf[2][:], w1_raw[2][:])
-        quantize_w1(2)
-        interleave("vector", w1_bf[3][:], w1_raw[3][:])
+        quantize(w1_codes[:, w1_parts[1]], w1_scales[:, w1_parts[1]], w1_bf[1][:])
+        w1_bf.append(sbuf([HALF, PACK], BF16, "w1_bf2", tag="w1_bf1"))
+        weave_gpsimd(w1_bf[2][:], w1_raw[2][:])
 
-        def make_h(t, c, acc):
-            product(acc, w1_codes[:, span(t, P)], w1_scales[:, span(t, P)], x_codes[:, halves[c]], x_scales[c][:])
-            return acc
+        def make_h(t, start, stop, acc):
+            c, first = divmod(start, HALF)
+            product(acc, w1_codes[:, span(t, P)], w1_scales[:, span(t, P)], x_codes[:, start:stop],
+                    x_scales[c][:, first:first + stop - start])
 
         def relu(engine, dst, acc):
             if engine == "scalar":
@@ -151,104 +146,103 @@ def tile_picked_devox_none_e_kernel(
             else:
                 nc.vector.tensor_scalar_max(dst, acc, 0.0)
 
-        def scatter_scalar(t, c):
-            nc.scalar.activation(up[t][:].indirect(cell_t[:, list_halves[c]]), h[t][:, halves[c]], COPY)
+        def scatter(engine, t, columns, values):
+            if engine == "scalar":
+                nc.scalar.activation(up[t][:].indirect(cell_t[:, columns]), values, COPY)
+            else:
+                nc.vector.tensor_copy(up[t][:].indirect(cell_t[:, columns]), values)
 
-        def scatter_vector(t, entries):
-            columns = slice(entries.start // STRIPE, entries.stop // STRIPE)
-            nc.vector.tensor_copy(up[t][:].indirect(cell_t[:, columns]), h[t][:, entries])
+        def entries(start, stop):
+            return slice(start // STRIPE, stop // STRIPE)
 
-        h = [keep.tile([P, S], F32, name="h%d" % t, tag=("w1_raw2", "w1_raw3", "h2", "h3")[t], align_bytes=64) for t in range(4)]
-        whole = slice(0, S)
-        relu("scalar", h[0][:, halves[0]], make_h(0, 0, bank(0, "h00")[:, halves[0]]))
-        scatter_scalar(0, 0)
-        relu("scalar", h[0][:, halves[1]], make_h(0, 1, bank(6, "h01")[:, halves[0]]))
-        relu("vector", h[1][:, halves[0]], make_h(1, 0, bank(1, "h10")[:, halves[0]]))
-        quantize_w1(3)
-        w2_bf = keep.tile([P, N, PACK], BF16, name="w2_bf", tag="w1_bf3", align_bytes=64)
-        nc.gpsimd.tensor_scalar(w2_bf[:], w2_raw[:].rearrange("p j c -> p c j"), 1.0, 0.0, MULT, ADD)
-        scatter_vector(1, halves[0])
-        relu("scalar", h[1][:, halves[1]], make_h(1, 1, bank(0, "h11")[:, halves[0]]))
-        scatter_scalar(0, 1)
-        for_scalar = bank(7, "h_scalar")
-        for_vector = bank(1, "h_vector")
-        acc = {(2, 0): for_scalar[:, halves[0]], (2, 1): for_vector[:, halves[0]],
-               (3, 0): for_vector[:, halves[1]], (3, 1): for_scalar[:, halves[1]]}
-        for t, c in acc:
-            make_h(t, c, acc[t, c])
-        relu("vector", h[3][:, halves[0]], acc[3, 0])
-        scatter_vector(1, halves[1])
-        relu("scalar", h[2][:, halves[0]], acc[2, 0])
-        relu("vector", h[2][:, halves[1]], acc[2, 1])
-        relu("scalar", h[3][:, halves[1]], acc[3, 1])
-        scatter_vector(3, whole)
+        h0 = sbuf([S], F32, "h0")
+        acc0 = [bank(0, "h_ps0_head"), bank(7, "h_ps0_rest")]
+        acc1 = bank(1, "h_ps1")
+        h1_head = sbuf([P], F32, "h1_head")
+        make_h(0, 0, P, acc0[0][:, 0:P])
+        relu("scalar", h0[:, 0:P], acc0[0][:, 0:P])
+        make_h(0, P, HALF, acc0[1][:, P:HALF])
+        make_h(1, 0, P, acc1[:, 0:P])
+        relu("vector", h1_head[:], acc1[:, 0:P])
+        make_h(0, HALF, S, acc0[1][:, halves[1]])
+        relu("vector", h0[:, P:S], acc0[1][:, P:S])
+        make_h(1, P, HALF, acc1[:, P:HALF])
+        make_h(1, HALF, S, acc1[:, halves[1]])
+        scatter("scalar", 0, entries(0, P), h0[:, 0:P])
+        scatter("scalar", 0, entries(P, S), h0[:, P:S])
+        scatter("vector", 1, entries(0, P), h1_head[:])
+        h1_rest = sbuf([S - P], F32, "h1_rest", tag="w1_raw2")
+        relu("vector", h1_rest[:], acc1[:, P:S])
+        quantize(w1_codes[:, w1_parts[2]], w1_scales[:, w1_parts[2]], w1_bf[2][:])
+        scatter("vector", 1, entries(P, S), h1_rest[:])
+        w2_bf = sbuf([N, PACK], BF16, "w2_bf", tag="w1_bf1")
+        weave_gpsimd(w2_bf[:], w2_raw[:])
+
+        h2 = sbuf([S], F32, "h2")
+        h3 = sbuf([S], F32, "h3")
+        for b, t, c in ((6, 2, 0), (7, 3, 0), (1, 3, 1), (0, 2, 1)):
+            acc = bank(b, "h_ps%d%d" % (t, c))[:, halves[0]]
+            make_h(t, c * HALF, (c + 1) * HALF, acc)
+            relu("scalar", (h2, h3)[t - 2][:, halves[c]], acc)
+        scatter("vector", 3, slice(0, S // STRIPE), h3[:])
         for c in range(2):
-            scatter_scalar(2, c)
+            scatter("scalar", 2, list_halves[c], h2[:, halves[c]])
 
-        zT = [keep.tile([P, 4, 2, HALF], BF16, name="zT%d" % c, align_bytes=64) for c in range(2)]
+        zT = [sbuf([4, 2, HALF], BF16, "zT%d" % c) for c in range(2)]
         late = [bank(2 + q, "late%d" % q) for q in range(4)]
 
-        def turn_late(block, first):
+        def turn_late(source, first, identity):
             for q in range(4):
                 for i in range(4):
                     t, b = divmod(i, 2)
-                    turn(late[q][:, span(2 * b + t, P)], block(t, q, b), first and i == 0, not first and i == 3)
+                    turn(late[q][:, span(2 * b + t, P)], source[t][:, span(2 * q + b, P)],
+                         first and i == 0, not first and i == 3, identity)
 
         def round_late(q, engine):
             c, pair = divmod(q, 2)
             copy_on(engine, zT[c][:, span(pair, 2), :, P:HALF].rearrange("p b u (s e) -> p b u s e", e=2),
                     late[q][:].rearrange("p (b s u e) -> p b u s e", b=2, u=2, e=2))
 
-        def turn_early(t, c):
-            z = keep.tile([P, BANK], BF16, name="z%d_%d" % (t, c))
-            nc.gpsimd.tensor_tensor(z[:], up[t][:, span(c, BANK)], emb_early[t][c][:], ADD)
-            turned = psum.tile([P, 2 * BANK], BF16, name="early%d_%d" % (t, c), tag="bank%d" % t)
-            for b in range(4):
-                nc.tensor.transpose(turned[:, span(b, P)], z[:, span(b, P)], ident_bf[:])
-            return turned
-
-        def move_early(t, c, engine):
-            copy_on(
-                engine,
-                zT[c][:].rearrange("p b u r -> p (b u r)").bitcast(F32).rearrange("p (b u s) -> p b u s", b=4, u=2)[:, :, :, span(t, 32)],
-                early[t, c][:, 0:BANK].bitcast(F32).rearrange("p (b s u) -> p b u s", b=4, u=2))
-
-        turn_late(lambda t, q, b: emb3[b][:, q, :] if t else emb2[:, span(2 * q + b, P)], True)
-        sums = [bank(6 + t, "sum%d" % t) for t in range(2)]
+        sums = [bank((7, 1)[t], "sum%d" % t) for t in range(2)]
         for t in range(2):
             for first, src in ((True, emb_early[t][1]), (False, up[t][:, span(1, BANK)])):
                 for b in range(4):
-                    turn(sums[t][:, span(b, P)], src[:, span(b, P)], first and b == 0, not first and b == 3)
-        early = {(0, 0): turn_early(0, 0)}
-        spare = early[0, 0][:, BANK:2 * BANK].bitcast(F32)
-        for i in range(4):
-            product(spare, w1_codes[:, span(i, P)], w1_scales[:, span(i, P)], x_codes[:, halves[0]], x_scales[0][:])
-        early[1, 0] = turn_early(1, 0)
-        turn_late(lambda t, q, b: up[2 + t][:, span(2 * q + b, P)], False)
-        w2_codes = keep.tile([P, N], U32, name="w2_codes", tag="h3", align_bytes=64)
-        w2_scales = keep.tile([P, N], U8, name="w2_scales", align_bytes=64)
+                    turn(sums[t][:, span(b, P)], src[:, span(b, P)], first and b == 0, not first and b == 3, ident)
+        turn_late(emb_late, True, ident)
+        early = psum.tile([P, 2 * BANK], BF16, name="early", tag="bank0")
+        for t in range(2):
+            z = sbuf([BANK], BF16, "z%d" % t)
+            nc.gpsimd.tensor_tensor(z[:], up[t][:, 0:BANK], emb_early[t][0][:], ADD)
+            for b in range(4):
+                nc.tensor.transpose(early[:, span(4 * t + b, P)], z[:, span(b, P)], ident_bf[:])
+        ident_late = sbuf([P], F32, "ident_late", tag="emb1_0")
+        make_identity(nc, ident_late[:])
+        turn_late(up[2:], False, ident_late)
+        w2_codes = sbuf([N], U32, "w2_codes", tag="h3")
+        w2_scales = sbuf([N], U8, "w2_scales")
         quantize(w2_codes[:], w2_scales[:], w2_bf[:])
-        move_early(0, 0, "vector")
-        move_early(1, 0, "vector")
+        nc.vector.tensor_copy(
+            zT[0][:].rearrange("p b u r -> p (b u r)").bitcast(F32).rearrange("p (b u t s) -> p b u t s", b=4, u=2, t=4)[:, :, :, 0:2, :],
+            early[:].bitcast(F32).rearrange("p (t b s u) -> p b u t s", t=2, b=4, u=2))
         for t in range(2):
             copy_on("scalar", zT[1][:, :, :, span(t, 64)].rearrange("p b u (s e) -> p b u s e", e=2),
                     sums[t][:].rearrange("p (b s u e) -> p b u s e", b=4, u=2, e=2))
         for q in range(4):
             round_late(q, ("scalar", "vector")[q % 2])
 
-        y = [keep.tile([P, U], F32, name="y%d" % n) for n in range(2)]
-        pieces = ((0, 2, 0, (2, 2), "scalar"), (2, 2, 1, (3, 3), "vector"), (4, 2, 7, (0, 0), "scalar"),
-                  (6, 1, 4, (1, 6), "scalar"), (7, 1, 5, (7, 2), "scalar"))
+        y = [sbuf([U], F32, "y%d" % n) for n in range(2)]
+        pieces = ((0, 2, 6, (2, 2), "scalar"), (2, 2, 0, (3, 3), "vector"), (4, 2, 7, (6, 6), "scalar"),
+                  (6, 1, 4, (0, 1), "scalar"), (7, 1, 5, (7, 2), "scalar"))
         for i, (first, count, back_bank, y_banks, engine) in enumerate(pieces):
             width = count * P
-            z_bf = keep.tile([P, width, PACK], BF16, name="z_bf%d" % i, align_bytes=64)
-            z_codes = keep.tile([P, width], U32, name="z_codes%d" % i, align_bytes=64)
-            z_scales = keep.tile([P, width], U8, name="z_scales%d" % i, align_bytes=64)
+            z_bf = sbuf([width, PACK], BF16, "z_bf%d" % i)
+            z_codes = sbuf([width], U32, "z_codes%d" % i)
+            z_scales = sbuf([width], U8, "z_scales%d" % i)
             back = bank(back_bank, "back%d" % i)
             for u in range(2):
                 words = zT[first // 4][:].rearrange("p b u r -> p (b u r)").bitcast(F32)
                 for b in range(count):
-                    turn(back[:, span(count * u + b, P)], words[:, span(2 * (first % 4 + b) + u, P)], True, True)
+                    turn(back[:, span(count * u + b, P)], words[:, span(2 * (first % 4 + b) + u, P)], True, True, ident)
             copy_on(engine, z_bf[:].rearrange("p c j -> p (c j)").bitcast(F32).rearrange("p (c u) -> p c u", u=2),
                     back[:, 0:2 * width].rearrange("p (u c) -> p c u", u=2))
             quantize(z_codes[:], z_scales[:], z_bf[:])
@@ -260,42 +254,42 @@ def tile_picked_devox_none_e_kernel(
                 copy_on("scalar" if n == 0 else "vector", y[n][:, first * P:first * P + width], acc[n][:, span(n, width)])
 
         def fetch_gated(n, d, cols, name, tag=None):
-            term = keep.tile([P, cols.stop - cols.start], F32, name=name, tag=tag or name)
+            term = sbuf([cols.stop - cols.start], F32, name, tag)
             offsets = pos_t[d][:, cols.start // STRIPE:cols.stop // STRIPE]
             nc.vector.tensor_tensor(term[:], y[n][:].indirect(offsets), gate_t[:, d, cols], MULT)
             return term
 
-        total = [bank((7 + c) % 8, "total%d" % c) for c in range(2)]
+        total = [bank((7, 6)[c], "total%d" % c) for c in range(2)]
         for d in range(D):
             blocks = 4 if d < D - 1 else 2
-            got = keep.tile([P, blocks * P], F32, name="got%d" % d)
+            got = sbuf([blocks * P], F32, "got%d" % d)
             nc.scalar.activation(got[:], y[0][:].indirect(pos_t[d][:, 0:blocks * P // STRIPE]), COPY)
-            turned = bank((1, 6, 2, 3)[d], "turned%d" % d)
+            turned = bank((0, 1, 2, 3)[d], "turned%d" % d)
             for b in range(blocks):
-                turn(turned[:, span(b, P)], got[:, span(b, P)], True, True)
-            gated = keep.tile([P, blocks * P], F32, name="gated%d" % d)
+                turn(turned[:, span(b, P)], got[:, span(b, P)], True, True, ident)
+            gated = sbuf([blocks * P], F32, "gated%d" % d)
             for b in range(blocks):
                 nc.scalar.activation(gated[:, span(b, P)], turned[:, span(b, P)], COPY, scale=gate_cols[:, d, b:b + 1])
             for b in range(blocks):
                 turn(total[b // 2][:, span(b % 2, P)], gated[:, span(b, P)], d == 0 and b % 2 == 0,
-                     d == D - 1 - b // 2 and b % 2 == 1)
+                     d == D - 1 - b // 2 and b % 2 == 1, ident)
 
         terms = [fetch_gated(1, d, slice(0, V), "term%d" % d) for d in range(D - 1)]
         part = terms[0]
         for d in range(1, D - 1):
-            more = keep.tile([P, V], F32, name="part%d" % d)
+            more = sbuf([V], F32, "part%d" % d)
             nc.vector.tensor_tensor(more[:], part[:], terms[d][:], ADD)
             part = more
         last = [fetch_gated(1, D - 1, halves[c], "last1_%d" % c) for c in range(2)]
         for c in range(2):
-            res1 = keep.tile([P, HALF], F32, name="res1_%d" % c)
+            res1 = sbuf([HALF], F32, "res1_%d" % c)
             nc.vector.tensor_tensor(res1[:], part[:, halves[c]], last[c][:], ADD)
             nc.sync.dma_start(out[P:N, halves[c]], res1[:])
         last0 = [fetch_gated(0, D - 1, span(2 + b, P), "last0_%d" % b, (None, "last1_0")[b]) for b in range(2)]
         for b in range(2):
-            res0 = keep.tile([P, P], F32, name="res0_%d" % b)
+            res0 = sbuf([P], F32, "res0_%d" % b)
             nc.vector.tensor_tensor(res0[:], total[1][:, span(b, P)], last0[b][:], ADD)
             nc.sync.dma_start(out[0:P, span(2 + b, P)], res0[:])
-        first0 = keep.tile([P, HALF], F32, name="first0")
+        first0 = sbuf([HALF], F32, "first0")
         nc.scalar.copy(first0[:], total[0][:, 0:HALF])
         nc.scalar.dma_start(out[0:P, halves[0]], first0[:])

@@ -104,7 +104,11 @@ def tile_picked_devox_none_e_kernel(
             for t in range(2):
                 nc.sync.dma_start(emb_early[t][c][:], emb[span(t, P), span(c, BANK)])
         pos_t = [load_list(src, "pos_t%d" % d) for d, src in enumerate((pos1, pos2, pos3, pos4))]
-        nc.sync.dma_start(gate_t[:], gate.rearrange("d p v -> p d v"))
+        gate_rows = gate.rearrange("d p v -> p d v")
+        nc.sync.dma_start(gate_t[:, 0:2, :], gate_rows[:, 0:2, :])
+        ident_late = sbuf([P], F32, "ident_late")
+        nc.sync.dma_start(ident_late[:], ident[:])
+        nc.sync.dma_start(gate_t[:, 2:D, :], gate_rows[:, 2:D, :])
         gate_cols = sbuf([D, 8], F32, "gate_cols")
         with nc.allow_non_contiguous_dma(reason="one gate value a partition"):
             for d in range(D):
@@ -209,21 +213,24 @@ def tile_picked_devox_none_e_kernel(
                 for b in range(4):
                     turn(sums[t][:, span(b, P)], src[:, span(b, P)], first and b == 0, not first and b == 3, ident)
         turn_late(emb_late, True, ident)
-        early = psum.tile([P, 2 * BANK], BF16, name="early", tag="bank0")
+        early = []
         for t in range(2):
+            early.append(psum.tile([P, 2 * BANK], BF16, name="early%d" % t, tag="bank%d" % (0, 6)[t]))
             z = sbuf([BANK], BF16, "z%d" % t)
             nc.gpsimd.tensor_tensor(z[:], up[t][:, 0:BANK], emb_early[t][0][:], ADD)
             for b in range(4):
-                nc.tensor.transpose(early[:, span(4 * t + b, P)], z[:, span(b, P)], ident_bf[:])
-        ident_late = sbuf([P], F32, "ident_late", tag="emb1_0")
-        make_identity(nc, ident_late[:])
+                nc.tensor.transpose(early[t][:, span(b, P)], z[:, span(b, P)], ident_bf[:])
+        spare = early[1][:, BANK:2 * BANK].bitcast(F32)
+        for i in range(4):
+            product(spare, w1_codes[:, span(i, P)], w1_scales[:, span(i, P)], x_codes[:, halves[0]], x_scales[0][:])
         turn_late(up[2:], False, ident_late)
         w2_codes = sbuf([N], U32, "w2_codes", tag="h3")
         w2_scales = sbuf([N], U8, "w2_scales")
         quantize(w2_codes[:], w2_scales[:], w2_bf[:])
-        nc.vector.tensor_copy(
-            zT[0][:].rearrange("p b u r -> p (b u r)").bitcast(F32).rearrange("p (b u t s) -> p b u t s", b=4, u=2, t=4)[:, :, :, 0:2, :],
-            early[:].bitcast(F32).rearrange("p (t b s u) -> p b u t s", t=2, b=4, u=2))
+        for t in range(2):
+            nc.vector.tensor_copy(
+                zT[0][:].rearrange("p b u r -> p (b u r)").bitcast(F32).rearrange("p (b u s) -> p b u s", b=4, u=2)[:, :, :, span(t, 32)],
+                early[t][:, 0:BANK].bitcast(F32).rearrange("p (b s u) -> p b u s", b=4, u=2))
         for t in range(2):
             copy_on("scalar", zT[1][:, :, :, span(t, 64)].rearrange("p b u (s e) -> p b u s e", e=2),
                     sums[t][:].rearrange("p (b s u e) -> p b u s e", b=4, u=2, e=2))
@@ -231,8 +238,8 @@ def tile_picked_devox_none_e_kernel(
             round_late(q, ("scalar", "vector")[q % 2])
 
         y = [sbuf([U], F32, "y%d" % n) for n in range(2)]
-        pieces = ((0, 2, 6, (2, 2), "scalar"), (2, 2, 0, (3, 3), "vector"), (4, 2, 7, (6, 6), "scalar"),
-                  (6, 1, 4, (0, 1), "scalar"), (7, 1, 5, (7, 2), "scalar"))
+        pieces = ((0, 2, 0, (2, 2), "scalar"), (2, 2, 6, (3, 3), "vector"), (4, 2, 7, (0, 0), "scalar"),
+                  (6, 1, 4, (6, 1), "scalar"), (7, 1, 5, (7, 2), "scalar"))
         for i, (first, count, back_bank, y_banks, engine) in enumerate(pieces):
             width = count * P
             z_bf = sbuf([width, PACK], BF16, "z_bf%d" % i)
@@ -259,12 +266,12 @@ def tile_picked_devox_none_e_kernel(
             nc.vector.tensor_tensor(term[:], y[n][:].indirect(offsets), gate_t[:, d, cols], MULT)
             return term
 
-        total = [bank((7, 6)[c], "total%d" % c) for c in range(2)]
+        total = [bank((7, 0)[c], "total%d" % c) for c in range(2)]
         for d in range(D):
             blocks = 4 if d < D - 1 else 2
             got = sbuf([blocks * P], F32, "got%d" % d)
             nc.scalar.activation(got[:], y[0][:].indirect(pos_t[d][:, 0:blocks * P // STRIPE]), COPY)
-            turned = bank((0, 1, 2, 3)[d], "turned%d" % d)
+            turned = bank((6, 1, 2, 3)[d], "turned%d" % d)
             for b in range(blocks):
                 turn(turned[:, span(b, P)], got[:, span(b, P)], True, True, ident)
             gated = sbuf([blocks * P], F32, "gated%d" % d)

@@ -85,8 +85,7 @@ def tile_picked_devox_none_e_kernel(
         w1_parts = [slice(0, P), slice(P, HALF), slice(HALF, H)]
         w1_raw = [sbuf([PACK, part.stop - part.start], F32, "w1_raw%d" % i) for i, part in enumerate(w1_parts)]
         x_plane = [sbuf([T], F32, "x_plane%d" % j) for j in range(PACK)]
-        emb_early = [[sbuf([BANK], F32, "emb%d_%d" % (t, c)) for c in range(2)] for t in range(2)]
-        emb_late = [sbuf([U], F32, "emb%d" % t) for t in (2, 3)]
+        emb_t = [sbuf([U], F32, "emb%d" % t) for t in range(4)]
         w2_raw = sbuf([PACK, N], F32, "w2_raw")
         gate_t = sbuf([D, V], F32, "gate_t")
         nc.sync.dma_start(x_plane[0][:], x_rows[0])
@@ -97,18 +96,13 @@ def tile_picked_devox_none_e_kernel(
             nc.sync.dma_start(w1_raw[i][:], w1_rows[:, :, w1_parts[i]])
         cell_t = load_list(cell, "cell_t")
         nc.sync.dma_start(w1_raw[2][:], w1_rows[:, :, w1_parts[2]])
-        for t in range(2):
-            nc.sync.dma_start(emb_late[t][:], emb[span(2 + t, P), :])
+        for t in (2, 0, 3, 1):
+            nc.sync.dma_start(emb_t[t][:], emb[span(t, P), :])
         nc.sync.dma_start(w2_raw[:], w2.rearrange("(p j) c -> p j c", j=PACK))
-        for c in range(2):
-            for t in range(2):
-                nc.sync.dma_start(emb_early[t][c][:], emb[span(t, P), span(c, BANK)])
         pos_t = [load_list(src, "pos_t%d" % d) for d, src in enumerate((pos1, pos2, pos3, pos4))]
-        gate_rows = gate.rearrange("d p v -> p d v")
-        nc.sync.dma_start(gate_t[:, 0:2, :], gate_rows[:, 0:2, :])
         ident_late = sbuf([P], F32, "ident_late")
         nc.sync.dma_start(ident_late[:], ident[:])
-        nc.sync.dma_start(gate_t[:, 2:D, :], gate_rows[:, 2:D, :])
+        nc.sync.dma_start(gate_t[:], gate.rearrange("d p v -> p d v"))
         gate_cols = sbuf([D, 8], F32, "gate_cols")
         with nc.allow_non_contiguous_dma(reason="one gate value a partition"):
             for d in range(D):
@@ -179,8 +173,6 @@ def tile_picked_devox_none_e_kernel(
         relu("vector", h1_rest[:], acc1[:, P:S])
         quantize(w1_codes[:, w1_parts[2]], w1_scales[:, w1_parts[2]], w1_bf[2][:])
         scatter("vector", 1, entries(P, S), h1_rest[:])
-        w2_bf = sbuf([N, PACK], BF16, "w2_bf", tag="w1_bf1")
-        weave_gpsimd(w2_bf[:], w2_raw[:])
 
         h2 = sbuf([S], F32, "h2")
         h3 = sbuf([S], F32, "h3")
@@ -209,17 +201,19 @@ def tile_picked_devox_none_e_kernel(
 
         sums = [bank((7, 1)[t], "sum%d" % t) for t in range(2)]
         for t in range(2):
-            for first, src in ((True, emb_early[t][1]), (False, up[t][:, span(1, BANK)])):
+            for first, src in ((True, emb_t[t][:, span(1, BANK)]), (False, up[t][:, span(1, BANK)])):
                 for b in range(4):
                     turn(sums[t][:, span(b, P)], src[:, span(b, P)], first and b == 0, not first and b == 3, ident)
-        turn_late(emb_late, True, ident)
+        turn_late(emb_t[2:], True, ident)
         early = []
         for t in range(2):
             early.append(psum.tile([P, 2 * BANK], BF16, name="early%d" % t, tag="bank%d" % (0, 6)[t]))
             z = sbuf([BANK], BF16, "z%d" % t)
-            nc.gpsimd.tensor_tensor(z[:], up[t][:, 0:BANK], emb_early[t][0][:], ADD)
+            nc.gpsimd.tensor_tensor(z[:], up[t][:, 0:BANK], emb_t[t][:, 0:BANK], ADD)
             for b in range(4):
                 nc.tensor.transpose(early[t][:, span(b, P)], z[:, span(b, P)], ident_bf[:])
+        w2_bf = sbuf([N, PACK], BF16, "w2_bf")
+        weave_gpsimd(w2_bf[:], w2_raw[:])
         spare = early[1][:, BANK:2 * BANK].bitcast(F32)
         for i in range(4):
             product(spare, w1_codes[:, span(i, P)], w1_scales[:, span(i, P)], x_codes[:, halves[0]], x_scales[0][:])

@@ -179,10 +179,11 @@ def tile_picked_devox_none_e_kernel(
         for b, t, c in ((6, 2, 0), (7, 3, 0), (1, 3, 1), (0, 2, 1)):
             acc = bank(b, "h_ps%d%d" % (t, c))[:, halves[0]]
             make_h(t, c * HALF, (c + 1) * HALF, acc)
+            if (t, c) == (2, 1):
+                scatter("scalar", 2, list_halves[0], h2[:, halves[0]])
             relu("scalar", (h2, h3)[t - 2][:, halves[c]], acc)
         scatter("vector", 3, slice(0, S // STRIPE), h3[:])
-        for c in range(2):
-            scatter("scalar", 2, list_halves[c], h2[:, halves[c]])
+        scatter("scalar", 2, list_halves[1], h2[:, halves[1]])
 
         zT = [sbuf([4, 2, HALF], BF16, "zT%d" % c) for c in range(2)]
         late = [bank(2 + q, "late%d" % q) for q in range(4)]
@@ -207,16 +208,13 @@ def tile_picked_devox_none_e_kernel(
         turn_late(emb_t[2:], True, ident)
         early = []
         for t in range(2):
-            early.append(psum.tile([P, 2 * BANK], BF16, name="early%d" % t, tag="bank%d" % (0, 6)[t]))
+            early.append(psum.tile([P, 2 * BANK], BF16, name="early%d" % t, tag="bank%d" % (6, 0)[t]))
             z = sbuf([BANK], BF16, "z%d" % t)
             nc.gpsimd.tensor_tensor(z[:], up[t][:, 0:BANK], emb_t[t][:, 0:BANK], ADD)
             for b in range(4):
                 nc.tensor.transpose(early[t][:, span(b, P)], z[:, span(b, P)], ident_bf[:])
         w2_bf = sbuf([N, PACK], BF16, "w2_bf")
         weave_gpsimd(w2_bf[:], w2_raw[:])
-        spare = early[1][:, BANK:2 * BANK].bitcast(F32)
-        for i in range(4):
-            product(spare, w1_codes[:, span(i, P)], w1_scales[:, span(i, P)], x_codes[:, halves[0]], x_scales[0][:])
         turn_late(up[2:], False, ident_late)
         w2_codes = sbuf([N], U32, "w2_codes", tag="h3")
         w2_scales = sbuf([N], U8, "w2_scales")
@@ -232,8 +230,8 @@ def tile_picked_devox_none_e_kernel(
             round_late(q, ("scalar", "vector")[q % 2])
 
         y = [sbuf([U], F32, "y%d" % n) for n in range(2)]
-        pieces = ((0, 2, 0, (2, 2), "scalar"), (2, 2, 6, (3, 3), "vector"), (4, 2, 7, (0, 0), "scalar"),
-                  (6, 1, 4, (6, 1), "scalar"), (7, 1, 5, (7, 2), "scalar"))
+        pieces = ((0, 2, 6, (2, 2), "scalar"), (2, 2, 0, (3, 3), "vector"), (4, 2, 7, (6, 6), "scalar"),
+                  (6, 2, 4, (0, 1), "scalar"))
         for i, (first, count, back_bank, y_banks, engine) in enumerate(pieces):
             width = count * P
             z_bf = sbuf([width, PACK], BF16, "z_bf%d" % i)
@@ -260,12 +258,12 @@ def tile_picked_devox_none_e_kernel(
             nc.vector.tensor_tensor(term[:], y[n][:].indirect(offsets), gate_t[:, d, cols], MULT)
             return term
 
-        total = [bank((7, 0)[c], "total%d" % c) for c in range(2)]
+        total = [bank((7, 6)[c], "total%d" % c) for c in range(2)]
         for d in range(D):
             blocks = 4 if d < D - 1 else 2
             got = sbuf([blocks * P], F32, "got%d" % d)
             nc.scalar.activation(got[:], y[0][:].indirect(pos_t[d][:, 0:blocks * P // STRIPE]), COPY)
-            turned = bank((6, 1, 2, 3)[d], "turned%d" % d)
+            turned = bank((0, 1, 2, 3)[d], "turned%d" % d)
             for b in range(blocks):
                 turn(turned[:, span(b, P)], got[:, span(b, P)], True, True, ident)
             gated = sbuf([blocks * P], F32, "gated%d" % d)

@@ -215,6 +215,9 @@ def tile_picked_devox_none_e_kernel(
                 nc.tensor.transpose(early[t][:, span(b, P)], z[:, span(b, P)], ident_bf[:])
         w2_bf = sbuf([N, PACK], BF16, "w2_bf")
         weave_gpsimd(w2_bf[:], w2_raw[:])
+        spare = early[1][:, BANK:2 * BANK].bitcast(F32)
+        for i in range(4):
+            product(spare, w1_codes[:, span(i, P)], w1_scales[:, span(i, P)], x_codes[:, halves[0]], x_scales[0][:])
         turn_late(up[2:], False, ident_late)
         w2_codes = sbuf([N], U32, "w2_codes", tag="h3")
         w2_scales = sbuf([N], U8, "w2_scales")

from contextlib import ExitStack

import concourse.mybir as mybir
from concourse.masks import make_identity

K, T, S, D, V, H, N, U = 512, 2048, 512, 4, 512, 512, 256, 1024
FLOPS = 2 * K * H * S + 2 * H * N * U

P = 128
PACK = 4
HALF = 256
BANK = 512
STRIPE = 16

F32 = mybir.dt.float32
BF16 = mybir.dt.bfloat16
U32 = mybir.dt.uint32
U16 = mybir.dt.uint16
U8 = mybir.dt.uint8
FP8X4 = mybir.dt.float8_e4m3fn_x4
COPY = mybir.ActivationFunctionType.Copy
RELU = mybir.ActivationFunctionType.Relu
MULT = mybir.AluOpType.mult
ADD = mybir.AluOpType.add


def span(index, width):
    return slice(index * width, (index + 1) * width)


def tile_picked_devox_none_e_kernel(
    tc, xT, w1, w2, gate, emb, offs, cell, pos1, pos2, pos3, pos4, out
):
    nc = tc.nc
    with ExitStack() as ctx:
        lists = ctx.enter_context(tc.tile_pool(name="lists", bufs=1))
        keep = ctx.enter_context(tc.tile_pool(name="keep", bufs=1))
        psum = ctx.enter_context(tc.psum_pool(name="psum", bufs=1))

        def bank(b, name):
            return psum.tile([P, BANK], F32, name=name, tag="bank%d" % b)

        def sbuf(shape, dtype, name, tag=None):
            return keep.tile([P] + shape, dtype, name=name, tag=tag or name, align_bytes=64)

        def load_list(src, name):
            offsets = lists.tile([P, S // STRIPE], U16, name=name)
            nc.sync.dma_start(offsets[:], src)
            return offsets

        def quantize(codes, scales, values):
            nc.vector.quantize_mx(out=codes.bitcast(FP8X4), scales=scales, in_=values.rearrange("p c j -> p (c j)"))

        def product(dst, w_codes, w_scales, moving_codes, moving_scales):
            nc.tensor.matmul_mx(
                out=dst, lhsT=w_codes.bitcast(FP8X4), lhsT_scale=w_scales,
                rhs=moving_codes.bitcast(FP8X4), rhs_scale=moving_scales, start=True, stop=True,
            )

        def turn(dst, src, start, stop, identity):
            nc.tensor.matmul(dst, src, identity[:], start=start, stop=stop, is_transpose=True)

        def copy_on(engine, dst, src):
            if engine == "vector":
                nc.vector.tensor_copy(dst, src)
            else:
                nc.scalar.copy(dst, src)

        def weave(engine, dst, src):
            copy_on(engine, dst.rearrange("p (c i) j -> p c j i", i=4), src.rearrange("p j (c i) -> p c j i", i=4))

        def weave_gpsimd(dst, src):
            nc.gpsimd.tensor_scalar(dst, src.rearrange("p j c -> p c j"), 1.0, 0.0, MULT, ADD)

        ident = sbuf([P], F32, "ident")
        make_identity(nc, ident[:])
        ident_bf = sbuf([P], BF16, "ident_bf")
        make_identity(nc, ident_bf[:])
        up = [sbuf([U], F32, "up%d" % t) for t in range(4)]
        for t in range(4):
            nc.vector.memset(up[t][:], 0.0)

        x_rows = xT.rearrange("(p j) c -> j p c", j=PACK)
        w1_rows = w1.rearrange("(p j) c -> p j c", j=PACK)
        w1_parts = [slice(0, P), slice(P, HALF), slice(HALF, H)]
        w1_raw = [sbuf([PACK, part.stop - part.start], F32, "w1_raw%d" % i) for i, part in enumerate(w1_parts)]
        x_plane = [sbuf([T], F32, "x_plane%d" % j) for j in range(PACK)]
        emb_t = [sbuf([U], F32, "emb%d" % t) for t in range(4)]
        w2_raw = sbuf([PACK, N], F32, "w2_raw")
        gate_t = sbuf([D, V], F32, "gate_t")
        nc.sync.dma_start(x_plane[0][:], x_rows[0])
        offs_t = load_list(offs, "offs_t")
        for j in range(1, PACK):
            nc.sync.dma_start(x_plane[j][:], x_rows[j])
        for i in range(2):
            nc.sync.dma_start(w1_raw[i][:], w1_rows[:, :, w1_parts[i]])
        cell_t = load_list(cell, "cell_t")
        nc.sync.dma_start(w1_raw[2][:], w1_rows[:, :, w1_parts[2]])
        for t in (2, 0, 3, 1):
            nc.sync.dma_start(emb_t[t][:], emb[span(t, P), :])
        nc.sync.dma_start(w2_raw[:], w2.rearrange("(p j) c -> p j c", j=PACK))
        pos_t = [load_list(src, "pos_t%d" % d) for d, src in enumerate((pos1, pos2, pos3, pos4))]
        ident_late = sbuf([P], F32, "ident_late")
        nc.sync.dma_start(ident_late[:], ident[:])
        nc.sync.dma_start(gate_t[:], gate.rearrange("d p v -> p d v"))
        gate_cols = sbuf([D, 8], F32, "gate_cols")
        with nc.allow_non_contiguous_dma(reason="one gate value a partition"):
            for d in range(D):
                nc.sync.dma_start(gate_cols[:, d, 0:4], gate[d, 0, :].rearrange("(b p) -> p b", p=P))

        halves = [span(c, HALF) for c in range(2)]
        list_halves = [span(c, HALF // STRIPE) for c in range(2)]
        x_bf = [sbuf([HALF, PACK], BF16, "x_bf%d" % c) for c in range(2)]
        x_planes = sbuf([PACK, HALF], BF16, "x_planes")
        for j in range(PACK):
            nc.vector.tensor_copy(x_bf[0][:, :, j], x_plane[j][:].indirect(offs_t[:, list_halves[0]]))
            nc.scalar.activation(x_planes[:, j, :], x_plane[j][:].indirect(offs_t[:, list_halves[1]]), COPY)
            if j == 1:
                weave("scalar", x_bf[1][:, :, 0:2], x_planes[:, 0:2, :])
        x_codes = sbuf([S], U32, "x_codes")
        x_scales = [sbuf([HALF], U8, "x_scales0")]
        w1_codes = sbuf([H], U32, "w1_codes")
        w1_scales = sbuf([H], U8, "w1_scales")
        w1_bf = [sbuf([P, PACK], BF16, "w1_bf%d" % i) for i in range(2)]
        for i in range(2):
            weave("scalar", w1_bf[i][:], w1_raw[i][:])
        weave("vector", x_bf[1][:, :, 2:PACK], x_planes[:, 2:PACK, :])
        quantize(x_codes[:, halves[0]], x_scales[0][:], x_bf[0][:])
        quantize(w1_codes[:, w1_parts[0]], w1_scales[:, w1_parts[0]], w1_bf[0][:])
        x_scales.append(sbuf([HALF], U8, "x_scales1", tag="w1_raw0"))
        quantize(x_codes[:, halves[1]], x_scales[1][:], x_bf[1][:])
        quantize(w1_codes[:, w1_parts[1]], w1_scales[:, w1_parts[1]], w1_bf[1][:])
        w1_bf.append(sbuf([HALF, PACK], BF16, "w1_bf2", tag="w1_bf1"))
        weave_gpsimd(w1_bf[2][:], w1_raw[2][:])

        def make_h(t, start, stop, acc):
            c, first = divmod(start, HALF)
            product(acc, w1_codes[:, span(t, P)], w1_scales[:, span(t, P)], x_codes[:, start:stop],
                    x_scales[c][:, first:first + stop - start])

        def relu(engine, dst, acc):
            if engine == "scalar":
                nc.scalar.activation(dst, acc, RELU)
            else:
                nc.vector.tensor_scalar_max(dst, acc, 0.0)

        def scatter(engine, t, columns, values):
            if engine == "scalar":
                nc.scalar.activation(up[t][:].indirect(cell_t[:, columns]), values, COPY)
            else:
                nc.vector.tensor_copy(up[t][:].indirect(cell_t[:, columns]), values)

        def entries(start, stop):
            return slice(start // STRIPE, stop // STRIPE)

        h0 = sbuf([S], F32, "h0")
        acc0 = [bank(0, "h_ps0_head"), bank(7, "h_ps0_rest")]
        acc1 = bank(1, "h_ps1")
        h1_head = sbuf([P], F32, "h1_head")
        make_h(0, 0, P, acc0[0][:, 0:P])
        relu("scalar", h0[:, 0:P], acc0[0][:, 0:P])
        make_h(0, P, HALF, acc0[1][:, P:HALF])
        make_h(1, 0, P, acc1[:, 0:P])
        relu("vector", h1_head[:], acc1[:, 0:P])
        make_h(0, HALF, S, acc0[1][:, halves[1]])
        relu("vector", h0[:, P:S], acc0[1][:, P:S])
        make_h(1, P, HALF, acc1[:, P:HALF])
        make_h(1, HALF, S, acc1[:, halves[1]])
        scatter("scalar", 0, entries(0, P), h0[:, 0:P])
        scatter("scalar", 0, entries(P, S), h0[:, P:S])
        scatter("vector", 1, entries(0, P), h1_head[:])
        h1_rest = sbuf([S - P], F32, "h1_rest", tag="w1_raw2")
        relu("vector", h1_rest[:], acc1[:, P:S])
        quantize(w1_codes[:, w1_parts[2]], w1_scales[:, w1_parts[2]], w1_bf[2][:])
        scatter("vector", 1, entries(P, S), h1_rest[:])

        h2 = sbuf([S], F32, "h2")
        h3 = sbuf([S], F32, "h3")
        for b, t, c in ((6, 2, 0), (7, 3, 0), (1, 3, 1), (0, 2, 1)):
            acc = bank(b, "h_ps%d%d" % (t, c))[:, halves[0]]
            make_h(t, c * HALF, (c + 1) * HALF, acc)
            if (t, c) == (2, 1):
                scatter("scalar", 2, list_halves[0], h2[:, halves[0]])
            relu("scalar", (h2, h3)[t - 2][:, halves[c]], acc)
        scatter("vector", 3, slice(0, S // STRIPE), h3[:])
        scatter("scalar", 2, list_halves[1], h2[:, halves[1]])

        zT = [sbuf([4, 2, HALF], BF16, "zT%d" % c) for c in range(2)]
        late = [bank(2 + q, "late%d" % q) for q in range(4)]

        def turn_late(source, first, identity):
            for q in range(4):
                for i in range(4):
                    t, b = divmod(i, 2)
                    turn(late[q][:, span(2 * b + t, P)], source[t][:, span(2 * q + b, P)],
                         first and i == 0, not first and i == 3, identity)

        def round_late(q, engine):
            c, pair = divmod(q, 2)
            copy_on(engine, zT[c][:, span(pair, 2), :, P:HALF].rearrange("p b u (s e) -> p b u s e", e=2),
                    late[q][:].rearrange("p (b s u e) -> p b u s e", b=2, u=2, e=2))

        sums = [bank((7, 1)[t], "sum%d" % t) for t in range(2)]
        for t in range(2):
            for first, src in ((True, emb_t[t][:, span(1, BANK)]), (False, up[t][:, span(1, BANK)])):
                for b in range(4):
                    turn(sums[t][:, span(b, P)], src[:, span(b, P)], first and b == 0, not first and b == 3, ident)
        turn_late(emb_t[2:], True, ident)
        early = []
        for t in range(2):
            early.append(psum.tile([P, 2 * BANK], BF16, name="early%d" % t, tag="bank%d" % (6, 0)[t]))
            z = sbuf([BANK], BF16, "z%d" % t)
            nc.gpsimd.tensor_tensor(z[:], up[t][:, 0:BANK], emb_t[t][:, 0:BANK], ADD)
            for b in range(4):
                nc.tensor.transpose(early[t][:, span(b, P)], z[:, span(b, P)], ident_bf[:])
        w2_bf = sbuf([N, PACK], BF16, "w2_bf")
        weave_gpsimd(w2_bf[:], w2_raw[:])
        spare = early[1][:, BANK:2 * BANK].bitcast(F32)
        for i in range(4):
            product(spare, w1_codes[:, span(i, P)], w1_scales[:, span(i, P)], x_codes[:, halves[0]], x_scales[0][:])
        turn_late(up[2:], False, ident_late)
        w2_codes = sbuf([N], U32, "w2_codes", tag="h3")
        w2_scales = sbuf([N], U8, "w2_scales")
        quantize(w2_codes[:], w2_scales[:], w2_bf[:])
        for t in range(2):
            nc.vector.tensor_copy(
                zT[0][:].rearrange("p b u r -> p (b u r)").bitcast(F32).rearrange("p (b u s) -> p b u s", b=4, u=2)[:, :, :, span(t, 32)],
                early[t][:, 0:BANK].bitcast(F32).rearrange("p (b s u) -> p b u s", b=4, u=2))
        for t in range(2):
            copy_on("scalar", zT[1][:, :, :, span(t, 64)].rearrange("p b u (s e) -> p b u s e", e=2),
                    sums[t][:].rearrange("p (b s u e) -> p b u s e", b=4, u=2, e=2))
        for q in range(4):
            round_late(q, ("scalar", "vector")[q % 2])

        y = [sbuf([U], F32, "y%d" % n) for n in range(2)]
        pieces = ((0, 2, 6, (2, 2), "scalar"), (2, 2, 0, (3, 3), "vector"), (4, 2, 7, (6, 6), "scalar"),
                  (6, 2, 4, (0, 1), "scalar"))
        for i, (first, count, back_bank, y_banks, engine) in enumerate(pieces):
            width = count * P
            z_bf = sbuf([width, PACK], BF16, "z_bf%d" % i)
            z_codes = sbuf([width], U32, "z_codes%d" % i)
            z_scales = sbuf([width], U8, "z_scales%d" % i)
            back = bank(back_bank, "back%d" % i)
            for u in range(2):
                words = zT[first // 4][:].rearrange("p b u r -> p (b u r)").bitcast(F32)
                for b in range(count):
                    turn(back[:, span(count * u + b, P)], words[:, span(2 * (first % 4 + b) + u, P)], True, True, ident)
            copy_on(engine, z_bf[:].rearrange("p c j -> p (c j)").bitcast(F32).rearrange("p (c u) -> p c u", u=2),
                    back[:, 0:2 * width].rearrange("p (u c) -> p c u", u=2))
            quantize(z_codes[:], z_scales[:], z_bf[:])
            acc = [bank(y_banks[0], "y_ps%d" % i)]
            acc.append(acc[0] if y_banks[1] == y_banks[0] else bank(y_banks[1], "y1_ps%d" % i))
            for n in range(2):
                product(acc[n][:, span(n, width)], w2_codes[:, span(n, P)], w2_scales[:, span(n, P)], z_codes[:], z_scales[:])
            for n in range(2):
                copy_on("scalar" if n == 0 else "vector", y[n][:, first * P:first * P + width], acc[n][:, span(n, width)])

        def fetch_gated(n, d, cols, name, tag=None):
            term = sbuf([cols.stop - cols.start], F32, name, tag)
            offsets = pos_t[d][:, cols.start // STRIPE:cols.stop // STRIPE]
            nc.vector.tensor_tensor(term[:], y[n][:].indirect(offsets), gate_t[:, d, cols], MULT)
            return term

        total = [bank((7, 6)[c], "total%d" % c) for c in range(2)]
        for d in range(D):
            blocks = 4 if d < D - 1 else 2
            got = sbuf([blocks * P], F32, "got%d" % d)
            nc.scalar.activation(got[:], y[0][:].indirect(pos_t[d][:, 0:blocks * P // STRIPE]), COPY)
            turned = bank((0, 1, 2, 3)[d], "turned%d" % d)
            for b in range(blocks):
                turn(turned[:, span(b, P)], got[:, span(b, P)], True, True, ident)
            gated = sbuf([blocks * P], F32, "gated%d" % d)
            for b in range(blocks):
                nc.scalar.activation(gated[:, span(b, P)], turned[:, span(b, P)], COPY, scale=gate_cols[:, d, b:b + 1])
            for b in range(blocks):
                turn(total[b // 2][:, span(b % 2, P)], gated[:, span(b, P)], d == 0 and b % 2 == 0,
                     d == D - 1 - b // 2 and b % 2 == 1, ident)

        terms = [fetch_gated(1, d, slice(0, V), "term%d" % d) for d in range(D - 1)]
        part = terms[0]
        for d in range(1, D - 1):
            more = sbuf([V], F32, "part%d" % d)
            nc.vector.tensor_tensor(more[:], part[:], terms[d][:], ADD)
            part = more
        last = [fetch_gated(1, D - 1, halves[c], "last1_%d" % c) for c in range(2)]
        for c in range(2):
            res1 = sbuf([HALF], F32, "res1_%d" % c)
            nc.vector.tensor_tensor(res1[:], part[:, halves[c]], last[c][:], ADD)
            nc.sync.dma_start(out[P:N, halves[c]], res1[:])
        last0 = [fetch_gated(0, D - 1, span(2 + b, P), "last0_%d" % b, (None, "last1_0")[b]) for b in range(2)]
        for b in range(2):
            res0 = sbuf([P], F32, "res0_%d" % b)
            nc.vector.tensor_tensor(res0[:], total[1][:, span(b, P)], last0[b][:], ADD)
            nc.sync.dma_start(out[0:P, span(2 + b, P)], res0[:])
        first0 = sbuf([HALF], F32, "first0")
        nc.scalar.copy(first0[:], total[0][:, 0:HALF])
        nc.scalar.dma_start(out[0:P, halves[0]], first0[:])
